import numpy as np, ml_dtypes
CORES = [40,42,43,45,46]
N = 5
BF = ml_dtypes.bfloat16
def gentries(a):
    return np.ascontiguousarray(a.reshape(8, 16, -1).transpose(0, 2, 1)).reshape(8, -1)
def gtable(e):
    e = np.asarray(e); return np.ascontiguousarray(e.reshape(8, -1, 16).transpose(0, 2, 1)).reshape(128, -1).astype(np.int32)
C, D, S, CAP, TH, HOP = 2560, 256, 3, 32, 11, 2
R = C // 16
def inverse(A):
    O = np.zeros_like(A); np.put_along_axis(O, A, np.broadcast_to(np.arange(C), A.shape), -1)
    return O
def estates(A, Y):
    V = np.zeros_like(Y)
    for k in range(16): V += np.take_along_axis(Y, A[:, :, k:k + 1, :], 3)
    return V
def judge(A, O, V, Y, h, z):
    n = h.shape[1]
    ca = np.take_along_axis(A, h[:, None, :], 2)
    yv = np.take_along_axis(Y, ca.reshape(8, 1, 16 * n), 2).reshape(8, 16, 16, n)
    k = np.argmax(np.add.reduce(np.minimum(yv, z[:, :, None, :]), axis=1), axis=1)
    a = np.take_along_axis(ca, k[:, None, :], 1)[:, 0]
    co = np.take_along_axis(O, a[:, None, :], 2)
    vv = np.take_along_axis(V, co.reshape(8, 1, 16 * n), 2).reshape(8, 16, 16, n)
    vc = np.take_along_axis(V, h[:, None, :], 2)
    over = np.add.reduce((vv > vc[:, :, None, :]).astype(np.int64), axis=1)
    j = np.argmax(over, axis=1)[:, None, :]
    return k, a, np.take_along_axis(co, j, 1)[:, 0], np.take_along_axis(over, j, 1)[:, 0]
def meets(x):
    eq = np.any(x[:, None, :, None] == x[None, :, None, :], axis=(2, 3))
    return np.any(np.tril(eq, -1), axis=1)
def exchange(A, O, V, Y, c, f, k, a):
    b = A[k, f]
    ok = ~(meets(np.stack([c, f], 1)) | meets(np.stack([a, b], 1)))
    c, f, k, a, b = c[ok], f[ok], k[ok], a[ok], b[ok]
    A[k, c] = b; A[k, f] = a; O[k, a] = f; O[k, b] = c
    dv = Y[:, b] - Y[:, a]
    V[:, c] += dv; V[:, f] -= dv
def cities(rng):
    rc = np.argsort(rng.random((N, 8, C)), axis=-1); ra = np.argsort(rng.random((N, 8, C)), axis=-1)
    key = rng.random((N, 8, 16, C)); key[:, :, 1:, :R] -= 1.0
    A = np.take_along_axis(ra[:, :, None, :], np.argsort(key, axis=-1), 3)
    A = np.take_along_axis(A, np.argsort(rc, axis=-1)[:, :, None, :], 3)
    m = np.zeros((N, 8, C), bool); np.put_along_axis(m, ra[:, :, :R], True, -1)
    Y = rng.integers(0, 16, (N, 8, 16, C)); Y = np.where(m[:, :, None, :], (Y >> 1) + 8, Y)
    return A, Y, np.ascontiguousarray(rc[:, :, :R])
def duties(rng, rc, n):
    h = np.where(rng.random((N, 8, n)) < 0.125, np.take_along_axis(rc, rng.integers(0, R, (N, 8, n)), 2), rng.integers(0, C, (N, 8, n)))
    top = rng.choice(np.array([0, 1, 3, 7, 7, 11, 15, 15, 15, 15]), (N, 8, 1, n))
    return h, rng.integers(0, top + 1, (N, 8, 16, n))
def ring(rng, A, Y, g, T):
    pc = np.argsort(rng.random((N, C)), axis=-1); pa = np.argsort(rng.random((N, C)), axis=-1)
    for q in range(N):
        A[q, g][:, pc[q]] = pa[q][(np.arange(C)[None, :] + np.arange(16)[:, None]) % C]
        Y[q, g][:, pa[q]] = T[q][:, np.arange(C) % 16]
    return pc
def pack(A, Y, h, z):
    O = inverse(A); V = estates(A, Y)
    w = lambda x: np.ascontiguousarray(x.reshape(N, 128, -1)).astype(np.float32).astype(BF)
    return {"ao": np.ascontiguousarray((A + 4096 * O).reshape(N, 128, C)).astype(np.int32), "yd": w(Y), "ve": w(V), "hd": np.stack([gtable(x) for x in h]), "zc": w(z)}
def setup_inputs(rng):
    A, Y, rc = cities(rng); h, z = duties(rng, rc, D)
    return pack(A, Y, h, z)
def setup_inputs_room(rng):
    A, Y, rc = cities(rng); h4, z4 = duties(rng, rc, 4 * D); O = inverse(A); V = estates(A, Y)
    h = np.zeros((N, 8, D), np.int64); z = np.zeros((N, 8, 16, D), np.int64)
    for q in range(N):
        k, a, f, m = judge(A[q], O[q], V[q], Y[q], h4[q], z4[q]); prop = (m < TH) & (f != h4[q])
        for g in range(8):
            yes = np.nonzero(prop[g])[0]; no = np.nonzero(~prop[g])[0]; ver = np.nonzero(m[g] >= TH)[0]
            if len(yes) == 0: yes = no
            if len(no) == 0: no = yes
            n = int(rng.choice(np.array([0, 1, CAP - 1, CAP, CAP + 1, D])))
            if q == 0: n = (CAP, CAP + 1, D, CAP - 1, 1, 0, CAP, CAP + 1)[g]
            if n == 0 and q % 2 == 0 and len(ver) > 0: no = ver
            ix = rng.permutation(np.concatenate([np.resize(rng.permutation(yes), n), np.resize(rng.permutation(no), D - n)]))
            h[q, g] = h4[q, g, ix]; z[q, g] = z4[q, g][:, ix]
    return pack(A, Y, h, z)
def setup_inputs_clash(rng):
    A, Y, rc = cities(rng); h, z = duties(rng, rc, D); iq = np.arange(N)
    T = rng.integers(0, 11, (N, 16, 16)); w = rng.integers(0, 16, N); T[iq, :, w] = 15
    p2 = ring(rng, A, Y, 2, T)
    T = rng.integers(0, 11, (N, 16, 16)); c4 = rng.integers(0, C, N); ks = np.argsort(rng.random((N, 15)), axis=-1)[:, :2] + 1
    T[iq, :8, (c4 + ks[:, 0]) % 16] = 15; T[iq, 8:, (c4 + ks[:, 1]) % 16] = 15
    p4 = ring(rng, A, Y, 4, T)
    e = int(rng.integers(0, C)); s = int(rng.integers(0, C)); r16 = np.arange(16)
    for q in range(N):
        at = np.argmax(A[q, 6] == s, axis=1); A[q, 6][r16, at] = A[q, 6][r16, e]; A[q, 6][r16, e] = s
    O = inverse(A)
    few = rng.integers(0, C, (N, 8, 24)); hf = np.take_along_axis(few, rng.integers(0, 24, (N, 8, D)), 2)
    st = np.argsort(rng.random((N, 8, C)), axis=-1)[:, :, None, :12]
    own = np.take_along_axis(O, st, 3).reshape(N, 8, 192); ho = np.take_along_axis(own, rng.integers(0, 192, (N, 8, D)), 2)
    Y2 = Y.copy(); np.put_along_axis(Y2, np.broadcast_to(st, (N, 8, 16, 12)), 15, 3)
    Y[:, 1::2] = Y2[:, 1::2]; h[:, ::2] = hf[:, ::2]; h[:, 1::2] = ho[:, 1::2]
    z[:, 1::2] = rng.integers(8, 16, (N, 4, 16, D))
    gap = C // CAP // 16 * 16
    for q in range(N):
        d = rng.permutation(D)[:CAP]; k = rng.integers(1, 16, CAP)
        z[q, 2] = 0; z[q, 2][:, d] = 15; h[q, 2, d] = p2[q, gap * np.arange(CAP) + (w[q] - k) % 16]
    kind = (np.arange(D)[None, :] + rng.integers(0, 2, (N, 1))) % 2
    h[:, 4] = p4[iq, c4][:, None]; z[:, 4] = np.where((np.arange(16) < 8)[None, :, None] == (kind == 0)[:, None, :], 15, 0)
    h[int(rng.integers(0, N)), 6] = e
    return pack(A, Y, h, z)
def setup_inputs_ties(rng):
    A, Y, rc = cities(rng); h, z = duties(rng, rc, D)
    lo = rng.integers(0, 4, (N, 8, 1, 1)); hi = lo + rng.integers(1, 12, (N, 8, 1, 1))
    Y = np.where(rng.random((N, 8, 16, C)) < 0.5, lo, hi)
    z = np.where(rng.random((N, 8, 1, D)) < 0.5, rng.integers(0, 16, (N, 8, 1, D)), z)
    g = rng.permutation(8); Y[:, g[0]] = rng.integers(1, 16, (N, 1, 1)); z[:, g[1]] = 0
    Y[:, g[2]] = rng.integers(14, 16, (N, 16, C)); z[:, g[2]] = np.where(rng.random((N, 1, D)) < 0.5, 15, rng.integers(14, 16, (N, 16, D)))
    return pack(A, Y, h, z)
def setup_inputs_ends(rng):
    A, Y, rc = cities(rng); h, z = duties(rng, rc, D)
    A[:, 1] = np.arange(C); A[:, 2] = (np.arange(C)[None, :] + np.arange(16)[:, None]) % C; A[:, 3] = A[:, 2]
    Y[..., 0] = 15; Y[..., C - 1] = 15; O = inverse(A)
    T = rng.integers(0, 16, (N, 16, 16)); Y[:, 3] = T[:, :, np.arange(C) % 16]
    own = np.ascontiguousarray(O[..., [0, C - 1]]).reshape(N, 8, 32)
    u = rng.random((N, 8, D)); e = rng.choice(np.array([0, C - 1]), (N, 8, D))
    h = np.where(u < 0.4, np.take_along_axis(own, rng.integers(0, 32, (N, 8, D)), 2), np.where(u < 0.5, e, h))
    h[..., 0] = 0; h[..., D - 1] = C - 1
    return pack(A, Y, h, z)
def setup_inputs_spread(rng):
    A, Y, rc = cities(rng); h, z = duties(rng, rc, D)
    s = np.exp2(4 * rng.random((N, 8, 1, C))) * np.exp2(-2 * rng.random((N, 8, 16, 1)))
    Y = np.minimum((s * rng.random((N, 8, 16, C))).astype(np.int64), 15)
    Y[rng.random(Y.shape) < 0.05] = 15
    z = np.minimum((np.exp2(5 * rng.random((N, 8, 1, D))) * rng.random((N, 8, 16, D))).astype(np.int64), 15)
    return pack(A, Y, h, z)
def check_inputs(d):
    bad = []
    for k, hi in (("yd", 15), ("zc", 15), ("ve", 240)):
        x = np.asarray(d[k]).astype(np.float32)
        if not np.all((x >= 0) & (x <= hi) & (x == np.floor(x))): bad.append("range of " + k)
    if np.min(d["hd"]) < 0 or np.max(d["hd"]) > C - 1: bad.append("range of hd")
    ao = np.asarray(d["ao"]).astype(np.int64).reshape(N, 8, 16, C); A = ao & 4095; O = ao >> 12
    if np.min(ao) < 0 or np.max(A) > C - 1 or np.max(O) > C - 1: return bad + ["range of ao"]
    m = np.zeros(A.shape, bool); np.put_along_axis(m, A, True, -1)
    if not np.all(m): bad.append("a row of A is no permutation")
    if not np.all(np.take_along_axis(O, A, 3) == np.arange(C)): bad.append("O is not the inverse of A")
    if not bad:
        Y = np.asarray(d["yd"]).astype(np.float32).astype(np.int64).reshape(N, 8, 16, C)
        if not np.all(estates(A, Y) == np.asarray(d["ve"]).astype(np.float32).astype(np.int64).reshape(N, 8, 16, C)): bad.append("ve is not the sum of the yields")
    return bad
def reference(ao, yd, ve, hd, zc):
    w = ao.astype(np.int64).reshape(N, 8, 16, C); A = w & 4095; O = w >> 12
    Y = yd.astype(np.float32).astype(np.int64).reshape(N, 8, 16, C); V = ve.astype(np.float32).astype(np.int64).reshape(N, 8, 16, C)
    z = zc.astype(np.float32).astype(np.int64).reshape(N, 8, 16, D); h = np.stack([gentries(x) for x in hd]).astype(np.int64)
    log = []
    for t in range(S):
        new = []
        for q in range(N):
            k, a, f, m = judge(A[q], O[q], V[q], Y[q], h[q], z[q])
            for g in range(8):
                ix = np.nonzero((m[g] < TH) & (f[g] != h[q, g]))[0][:CAP]
                exchange(A[q, g], O[q, g], V[q, g], Y[q, g], h[q, g, ix], f[g, ix], k[g, ix], a[g, ix])
            new.append(np.where(m >= TH, f, h[q]))
        h = np.stack(new); log.append(h)
        if t < S - 1:
            h = np.roll(h, HOP, axis=0); z = np.roll(z, HOP, axis=0)
    return {"vo": V.reshape(N, 128, C).astype(np.float32).astype(BF), "ho": np.stack(log, axis=2).reshape(N, 8, S * D).astype(np.float32)}

@@ -1,0 +1,621 @@
+from concourse.mybir import AluOpType as Op, ActivationFunctionType as Fn
+
+C, D, S, HOP = 2560, 256, 3, 2
+WD = 2640
+NONE = 2624
+MID = 1280
+OFF = 5376
+MAG = 1.5 * 2.0 ** 35
+BIG = 1.0e9
+NS = (64, 32)
+NV = (128 - NS[0], 128 - NS[1])
+SPW = 16 * max(NV)
+CH = 32
+
+f32, bf, i32, u16, h16 = "float32", "bfloat16", "int32", "uint16", "float16"
+SB = {
+    "WA": (WD, i32), "WO": (WD, i32), "Y": (WD, bf), "V": (WD, bf), "HD": (16, i32), "HDF": (16, f32), "Z": (256, bf),
+    "ZR0": (4096, bf), "ZR1": (4096, bf), "ZR2": (4096, bf), "M1": (4096, bf), "M2": (4096, bf), "GS": (2048, bf),
+    "SP0": (1024, bf), "SP1": (1024, bf), "KR": (1024, bf), "VR0": (16 * NV[0], bf), "VR1": (16 * NV[1], bf),
+    "HL0": (16, u16), "HL1": (16, u16), "HL2": (16, u16), "HC0": (16, f32), "HC1": (16, f32), "HC2": (16, f32),
+    "HS0": (16, u16), "HS1": (16, u16), "HN0": (16, f32), "HN1": (16, f32), "HN2": (16, f32), "HO": (768, f32),
+    "CA": (256, u16), "CO": (256, u16), "PL1": (256, h16), "PL2": (256, h16), "EE": (256, f32), "E2": (256, f32), "FT": (256, f32),
+    "HI": (16, f32), "HI2": (16, f32), "KI": (16, i32), "KJ": (16, i32), "XP": (256, h16), "XH": (256, h16), "AL": (16, u16),
+    "VCS": (128, bf), "VCT": (128, bf), "CE": (256, f32), "EQB": (256, bf), "SGB": (256, bf), "JK": (256, bf), "ACC": (4, f32), "PRE": (2, f32),
+    "DL": (4, u16), "FL": (264, f32), "FC": (64, f32), "FH": (32, h16), "TR": (64, f32), "LU": (16, u16), "LF": (16, f32), "LO": (16, u16),
+    "MK": (64, f32), "NK": (64, f32), "AM": (64, f32), "AN": (64, f32), "NA": (64, i32), "OM": (64, f32), "ON": (64, f32), "NO": (64, i32),
+    "HB": (32, f32), "EQ": (384, bf), "CF": (384, f32), "YA": (64, bf), "YB": (64, bf), "U": (64, bf),
+    "DF": (16, f32), "VER": (16, f32), "VD": (16, f32),
+    "IO": (256, f32), "IOC": (384, f32), "PI": (8, i32), "CC": (32, f32), "CI": (160, i32), "CL": (176, u16),
+    "ONF": (128, f32), "ONB": (512, bf), "IDF": (128, f32), "IDB": (128, bf), "NIB": (128, bf), "GB": (8, bf), "G0": (8, bf), "GI": (8, bf), "NGI": (8, bf),
+    "RM": (256, f32), "K16": (128, f32), "TRI": (256, bf), "N2T": (256, bf), "EXP": (16 * (NS[0] + NS[1]), bf), "CK": (128, bf),
+    "B0": (128, f32), "BO": (128, f32), "SEL": (512, bf), "CAB": (128, bf), "KH": (32, f32), "KT": (32, f32), "KC": (384, bf),
+}
+PS = ["D0", "D1", "D2", "D3", "E0", "E1", "PP", "PF"]
+SCRATCH = {k: ("sbuf", [128, w], d) for k, (w, d) in SB.items()}
+SCRATCH.update({k: ("psum", [128, 512], f32) for k in PS})
+NAO = 4
+SEMAPHORES = ["qg", "qv", "qs", "qp", "lh", "lz", "ly", "lv", "so", "sh", "z1", "z2", "hl1", "hl2", "hc1", "hc2", "sent"] + ["la%d" % j for j in range(NAO)]
+COSTS = [dict(pe=1.0, el=1.0, ga=1.56, sc=3.8, by=0.004, lat=2200, wake=60),
+         dict(pe=0.5, el=1.0, ga=1.56, sc=3.8, by=0.004, lat=2500, wake=100),
+         dict(pe=0.45, el=0.9, ga=1.0, sc=1.5, by=0.003, lat=2200, wake=60)]
+ROUNDS, SEED, DRIFT = 30000, 1, 0.002
+PLAN = {}
+
+
+def A(name, lo=0, hi=None, step=1, rows=128):
+    if hi is None:
+        hi = SB[name][0] if name in SB else 512
+    return ("ap", name, lo, hi, step, rows)
+
+
+def IND(win, off):
+    return ("ind", win, off)
+
+
+def col(j):
+    return A("CC", j, j + 1)
+
+
+def meet(a, b, same):
+    if a[1] in PS and not same:
+        return True
+    if a[3] <= b[2] or b[3] <= a[2]:
+        return False
+    return not (same and a[4] == b[4] and (a[2] - b[2]) % a[4] != 0)
+
+
+def width(x):
+    return 16 * (x[2][3] - x[2][2]) if x[0] == "ind" else (x[3] - x[2] + x[4] - 1) // x[4]
+
+
+def size(x):
+    return 4 if x[1] in PS or SB[x[1]][1] in (f32, i32) else 2
+
+
+def schedule(ops):
+    if "order" in PLAN:
+        return PLAN["order"]
+    m = len(ops)
+    before, seen, anc = [], {}, []
+    for i, (q, wr, rd, cost, lat, emit) in enumerate(ops):
+        d = set()
+        for aps, w_ in ((wr, True), (rd, False)):
+            for x in aps:
+                for y, yw, yq, j in seen.get(x[1], []):
+                    if x[1] in PS or ((w_ or yw) and meet(x, y, yq == q)):
+                        d.add(j)
+        for aps, w_ in ((wr, True), (rd, False)):
+            for x in aps:
+                seen.setdefault(x[1], []).append((x, w_, q, i))
+        mask, keep = 0, []
+        for j in sorted(d, reverse=True):
+            if not mask >> j & 1:
+                keep.append(j)
+                mask |= anc[j] | 1 << j
+        anc.append(mask)
+        before.append(keep)
+    qs = ["gvspy".index(o[0]) for o in ops]
+    sets = []
+    for c in COSTS:
+        busy = [o[3][1] + o[3][2] * c[o[3][0]] for o in ops]
+        lat = [o[4] and c["lat"] + o[4] * c["by"] for o in ops]
+        edge = [[(j, lat[j] + (0 if qs[i] == 3 and qs[j] == 3 else c["wake"])) for j in before[i]] for i in range(m)]
+        sets.append((busy, lat, edge))
+
+    def finish(seq, k, trace=False):
+        busy, lat, edge = sets[k]
+        free, end, who, why = [0.0] * 5, [0.0] * m, [-1] * 5, [-1] * m
+        for i in seq:
+            q = qs[i]
+            t, y = free[q], who[q]
+            for j, e in edge[i]:
+                if end[j] + e > t:
+                    t, y = end[j] + e, j
+            end[i] = free[q] = t + busy[i]
+            who[q], why[i] = i, y
+        i = max(range(m), key=lambda j: end[j] + lat[j])
+        if not trace:
+            return end[i] + lat[i]
+        path = []
+        while i >= 0:
+            path.append(i)
+            i = why[i]
+        return path
+
+    seed = [SEED]
+
+    def rnd(k):
+        seed[0] = (seed[0] * 1103515245 + 12345) % 2147483648
+        return (seed[0] >> 8) % k
+
+    seq = list(range(m))
+    norm = [finish(seq, k) for k in range(len(sets))]
+    score = lambda s_: sum(finish(s_, k) / norm[k] for k in range(len(sets)))
+    cur = score(seq)
+    paths = [finish(seq, k, True) for k in range(len(sets))]
+    for it in range(ROUNDS):
+        path = paths[rnd(len(paths))]
+        z = rnd(len(path) - 1)
+        i, j = path[z], path[z + 1]
+        if qs[i] == 4 or qs[j] == 4 or anc[i] >> j & 1:
+            continue
+        pi_, pj = seq.index(i), seq.index(j)
+        if rnd(2):
+            lo = max(0, pj - (rnd(12) if rnd(2) else 0))
+            part = seq[lo:pi_]
+            new = seq[:lo] + [x for x in part if anc[i] >> x & 1] + [i] + [x for x in part if not anc[i] >> x & 1] + seq[pi_ + 1:]
+        else:
+            hi = min(m, pi_ + 1 + (rnd(12) if rnd(2) else 0))
+            part = seq[pj + 1:hi]
+            new = seq[:pj] + [x for x in part if not anc[x] >> j & 1] + [j] + [x for x in part if anc[x] >> j & 1] + seq[hi:]
+        sc_ = score(new)
+        if sc_ <= cur + DRIFT * (1 - it / ROUNDS):
+            seq, cur = new, sc_
+            paths = [finish(seq, k, True) for k in range(len(sets))]
+    PLAN["order"], PLAN["est"] = seq, [finish(seq, k) for k in range(len(sets))] + norm
+    return seq
+
+
+def rank_program(g, core, T, topo):
+    rank = T.rank_of(core)
+    if rank is None:
+        return
+    n = len(T.cores)
+    Q = {"g": g, "v": g.vector, "s": g.scalar, "p": g.tensor, "y": g.sync}
+    count = {}
+    known = {q: {} for q in Q}
+    acc = {}
+    ops = []
+
+    def mk(x):
+        if isinstance(x, tuple) and x[0] == "ap":
+            return T[x[1]][0:x[5], x[2]:x[3]:x[4]] if x[4] > 1 else T[x[1]][0:x[5], x[2]:x[3]]
+        if isinstance(x, tuple) and x[0] == "ind":
+            return mk(x[1]).indirect(mk(x[2]))
+        return x
+
+    def need(q, tok):
+        sem, val, clock = tok
+        if known[q].get(sem, 0) < val:
+            Q[q].wait_ge(T.sem[sem], val)
+            known[q][sem] = val
+            for k, v in clock.items():
+                known[q][k] = max(known[q].get(k, 0), v)
+
+    def order(q, wr, rd):
+        toks = {}
+        for aps, w in ((wr, True), (rd, False)):
+            for a in aps:
+                for b, bw, bq, tok in acc.get(a[1], []):
+                    if q == "p" and bq == "p":
+                        continue
+                    if (w or bw or (a[1] in PS and bq != q)) and meet(a, b, bq == q):
+                        if tok[1] > toks.get(tok[0], (0, 0))[1]:
+                            toks[tok[0]] = tok
+        for tok in sorted(toks.values(), key=lambda t: -len(t[2])):
+            need(q, tok)
+
+    def note(q, wr, rd, tok):
+        for aps, w in ((wr, True), (rd, False)):
+            for a in aps:
+                acc.setdefault(a[1], []).append((a, w, q, tok))
+
+    def token(q, sem, inc):
+        count[sem] = count.get(sem, 0) + inc
+        return (sem, count[sem], dict(known[q]))
+
+    def parts(xs):
+        out = []
+        for x in xs:
+            if isinstance(x, tuple):
+                out += [x] if x[0] == "ap" else [x[1], x[2]]
+        return out
+
+    def op(q, rate, call, *a, **kw):
+        o = a[0]
+        wr = [o] if o[0] == "ap" else [o[1]]
+        ins = [x for x in a[1:] if isinstance(x, tuple)]
+        rd = ([] if o[0] == "ap" else [o[2]]) + parts(a[1:]) + parts([v for k, v in kw.items() if k != "accum_out"])
+        if "accum_out" in kw:
+            wr.append(kw["accum_out"])
+        if q == "p":
+            cost = ("pe", 0, max(min(64, width(a[1])), width(a[2])) * (4 if size(a[1]) == 4 else 1))
+        elif o[0] == "ind":
+            cost = ("sc", 50, width(o))
+        elif any(x[0] == "ind" for x in ins):
+            cost = ("ga", 60, width(o))
+        else:
+            if rate == 0.5 and any(size(x) == 4 for x in [o] + ins if width(x) > 1):
+                rate = 1
+            if rate == 2 and any(x[1] in PS for x in ins):
+                rate = 1
+            cost = ("el", {"v": 0, "s": 30, "g": 150}[q], max(64, rate * width(o)))
+
+        def emit():
+            order(q, wr, rd)
+            call(*[mk(x) for x in a], **{k: mk(v) for k, v in kw.items()}).then_inc(T.sem["q" + q], 1)
+            note(q, wr, rd, token(q, "q" + q, 1))
+        ops.append((q, wr, rd, cost, 0, emit))
+
+    ve, sc, pe = g.vector, g.scalar, g.tensor
+    cp = lambda o, i: op("v", 0.5, ve.tensor_copy, o, i)
+    tt = lambda o, a, b, x: op("v", 2, ve.tensor_tensor, o, a, b, x)
+    ts1 = lambda o, a, s1, x: op("v", 0.5, ve.tensor_scalar, o, a, s1, None, x)
+    ts2 = lambda o, a, s1, s2, x, y: op("v", 0.5, ve.tensor_scalar, o, a, s1, s2, x, y)
+    ms = lambda o, c: op("v", 0.5, ve.memset, o, c)
+    scan = lambda o, a, b, i, x, y: op("v", 0.5, ve.tensor_tensor_scan, o, a, b, i, x, y)
+    act = lambda o, i, f, **kw: op("s", 1, sc.activation, o, i, f, **kw)
+    mm = lambda o, l, r, st=True, sp=True: op("p", 1, pe.matmul, o, l, r, st, sp)
+    iota = lambda o, p, b, c: op("g", 2, g.iota, o, p, b, c, **({} if SB[o[1]][1] == i32 else {"allow_small_or_imprecise_dtypes": True}))
+    asel = lambda o, i, p, x, f, b, c: op("g", 2, g.affine_select, o, i, p, x, f, b, c)
+
+    def load(q, o, src, sem):
+        def emit():
+            order(q, [o], [])
+            Q[q].dma_start(mk(o), src).then_inc(T.sem[sem], 16)
+            note(q, [o], [], token(q, sem, 16))
+        ops.append((q, [o], [], ("by", 300, width(o) * size(o) * 128), 1, emit))
+
+    def store(q, dst, i, sem):
+        def emit():
+            order(q, [], [i])
+            Q[q].dma_start(dst, mk(i)).then_inc(T.sem[sem], 16)
+            note(q, [], [i], token(q, sem, 16))
+        ops.append((q, [], [i], ("el", 100, 0), width(i) * size(i) * i[5], emit))
+
+    def send(hops, o, i, sem, after=(), behind=()):
+        dst = T.cores[(rank + hops * HOP) % n]
+        src = T.cores[(rank - hops * HOP) % n]
+        rid, pid, _ = topo.addr(dst)
+
+        def emit():
+            order("g", [], [i] + list(after))
+            g.remote_dma(out_ap=mk(o), in_ap=mk(i), remote_sem=T.sem[sem], local_sem=T.sem.sent, pid=pid, routing_id=rid,
+                         dma_engine_mask=topo.mask(core, dst))
+            token("g", "sent", len(topo.engines(core, dst)))
+            count[sem] = len(topo.engines(src, core))
+            note("x", [o], [], (sem, count[sem], {}))
+        ops.append(("g", [o] + list(behind), [i] + list(after), ("el", 600, 0), width(i) * size(i) * 128, emit))
+
+    WA, WO, Y, V = A("WA"), A("WO"), A("Y"), A("V")
+    BC15, BCA, BC0, PAR = A("CL", 0, 8), A("CL", 16, 24), (lambda a, b: A("CL", 32 + a, 32 + b)), A("CL", 160, 161)
+    tl = lambda name, t: A(name, 128 * t, 128 * t + 128)
+    ONE = A("ONB", 0, 128)
+
+    load("y", A("Z"), T.zc[:, :], "lz")
+    load("y", A("HD"), T.hd[:, :], "lh")
+    w = C // NAO
+    for j in range(NAO):
+        load("y", A("WO", j * w, (j + 1) * w), T.ao[:, j * w:(j + 1) * w], "la%d" % j)
+    load("y", A("Y", 0, C), T.yd[:, :], "ly")
+    load("y", A("V", 0, C), T.ve[:, :], "lv")
+
+    iota(A("CI", 32, 160), [[1, 128]], 0, 0)
+    iota(A("CI", 0, 32), [[-13, 2], [16, 16]], 15, 0)
+    iota(A("PI", 0, 1), [[0, 1]], 0, 1)
+    iota(A("IO"), [[0, 16], [1, 16]], 0, 0)
+    ms(A("ONB"), 1.0)
+    ms(A("ONF"), 1.0)
+    ms(A("KR"), 1.0)
+    ms(A("SP0"), 0.0)
+    ms(A("KR", 0, 1024, 16), 0.0)
+    cp(A("CL", 0, 160), A("CI"))
+    ts1(A("PI", 1, 2), A("PI", 0, 1), 15, Op.bitwise_and)
+    ts2(A("PI", 2, 3), A("PI", 0, 1), 4, 1, Op.arith_shift_right, Op.bitwise_and)
+    ts1(A("PI", 3, 4), A("PI", 0, 1), 1, Op.bitwise_and)
+    ms(A("WA", C, WD), NONE)
+    ms(A("WO", C, WD), 0)
+    ms(A("Y", C, WD), 0.0)
+    ms(A("V", C, WD), 0.0)
+    cp(A("CC", 0, 3), A("PI", 1, 4))
+    asel(A("IDB"), ONE, [[-1, 128]], Op.is_equal, 0.0, 0, 1)
+    asel(A("G0"), A("ONB", 0, 8), [[-16, 8]], Op.is_ge, 0.0, 0, 1)
+    asel(A("GB"), A("G0"), [[16, 8]], Op.is_ge, 0.0, 15, -1)
+    iota(A("CK"), [[0, 8], [-32, 16]], 480, 0)
+    ms(A("SP1"), 0.0)
+    act(A("ZR0", 2048, 4096), IND(A("Z", 128, 256), BC0(0, 128)), Fn.Copy)
+    for j in range(2):
+        sp = "SP%d" % j
+        cp(A(sp, 0, 1024, 16), A("Z", 64 * j, 64 * j + 64))
+        scan(A("ZR0", 1024 * j, 1024 * j + 1024), A("KR"), A(sp), 0.0, Op.mult, Op.add)
+    cp(A("HL0"), A("HD"))
+    ts1(A("HDF"), A("HD"), -float(MID), Op.add)
+    act(A("GI"), A("GB"), Fn.Copy, scale=65536.0)
+    act(A("NGI"), A("GB"), Fn.Copy, scale=-65536.0)
+    act(A("NIB"), A("IDB"), Fn.Copy, scale=-1.0)
+    unpack = lambda j: ts1(A("WA", j * w, (j + 1) * w), A("WO", j * w, (j + 1) * w), 4095, Op.bitwise_and)
+    unpack(0)
+    ts1(A("RM"), A("IO"), col(0), Op.is_equal)
+    ts2(A("K16"), A("IO", 0, 128), 0.0, -BIG, Op.is_equal, Op.mult)
+    ms(A("FT"), 0.0)
+    unpack(1)
+    tt(A("XH"), IND(A("HDF"), BC0(0, 16)), A("RM"), Op.mult)
+    for t in (0, 1):
+        mm(A("PF", 256 + 8 * t, 264 + 8 * t), tl("XH", t), A("GB"))
+    act(A("HC0"), A("PF", 256, 272), Fn.Copy)
+    unpack(2)
+    for j, (a_, b_) in {3: (-1, 15), 5: (-2, -1), 6: (-2, -33), 7: (1, C), 8: (1, C + 16), 9: (1, C + 32),
+                        10: (1, C + 48), 15: (1, 1), 16: (8, 0), 17: (8, 256), 19: (1, -2.5)}.items():
+        act(col(j), col(0), Fn.Identity, scale=float(a_), bias=float(b_))
+    act(col(19), col(19), Fn.Abs)
+    act(A("VCS"), ONE, Fn.Copy, scale=0.0)
+    act(A("CC", 20, 22), A("ONB", 0, 2), Fn.Copy, scale=-0.5)
+    act(A("CAB"), ONE, Fn.Copy, scale=-32.0)
+    act(A("CAB", 65, 128, 2), A("ONB", 0, 32), Fn.Copy, scale=-OFF / 128.0)
+    asel(A("IDF"), A("ONF"), [[-1, 128]], Op.is_equal, 0.0, 0, 1)
+    asel(A("B0"), A("ONF"), [[-16, 8], [0, 16]], Op.is_ge, 0.0, 0, 1)
+    asel(A("BO"), A("B0"), [[16, 8], [0, 16]], Op.is_ge, 0.0, 15, -1)
+    iota(A("IOC"), [[1, 384]], 0, 0)
+    for t in (0, 1):
+        for j, v, d in ((11 + t, 11 * 65536 - 2048, -5 * 65536), (13 + t, 61440, -16 * 65536)):
+            iota(col(j + 12), [[0, 1]], v, 0)
+            asel(col(j), col(j + 12), [[0, 1]], Op.is_gt, float(v + d), NV[t], -1)
+    asel(A("TRI", 0, 128), ONE, [[1, 128]], Op.is_ge, 0.0, 0, -1)
+    asel(A("TRI", 128, 256), ONE, [[0, 128]], Op.is_ge, 0.0, 0, 0)
+    for j in range((NS[0] + NS[1]) // 32):
+        asel(A("EXP", 512 * j, 512 * j + 512), A("ONB"), [[-1, 32], [0, 16]], Op.is_equal, 0.0, -32 * j, 1)
+    ts2(col(4), col(0), 15.0, 32768.0, Op.is_lt, Op.mult)
+    for j in range(4):
+        ts1(col(27 + j), col(0), float(j), Op.is_equal)
+    ts2(col(18), col(0), 6.0, 2.0, Op.is_ge, Op.mult)
+    ts2(A("FL", 256, 264), A("RM", 3, 131, 16), -float(NONE - MID), float(NONE - MID), Op.mult, Op.add)
+    ts2(col(18), col(2), 32.0, col(18), Op.mult, Op.add)
+    unpack(3)
+    act(A("N2T"), A("TRI"), Fn.Copy, scale=-2.0)
+    for j in range(4):
+        act(A("SEL", 128 * j, 128 * j + 128), A("BO"), Fn.Copy, scale=col(27 + j))
+
+    def late_constants():
+        ts2(col(19), col(19), 1.0, col(18), Op.is_lt, Op.add)
+        ts2(A("KH"), A("IO", 0, 32), col(0), -BIG, Op.is_equal, Op.mult)
+        ts2(A("KT"), A("IO", 0, 32), col(15), 32768.0, Op.is_equal, Op.mult)
+        ts2(A("KC", 0, 128), A("IOC", 0, 128), col(16), float(OFF), Op.is_equal, Op.mult)
+        ts2(A("KC", 128, 384), A("IOC", 128, 384), col(17), float(OFF), Op.is_equal, Op.mult)
+        ts2(PAR, col(1), 16.0, col(19), Op.mult, Op.add)
+        tt(A("KH"), A("KH"), A("KT"), Op.add)
+        ms(A("KC", 128, 129), -16384.0)
+
+    send(1, A("ZR1"), A("ZR0"), "z1", after=[V])
+    send(2, A("ZR2"), A("ZR0"), "z2", after=[V])
+
+    cf, fc, la, ab, ba, lb = A("LU", 0, 4), A("LU", 2, 6), A("LU", 6, 8), A("LU", 6, 10), A("LU", 8, 12), A("LU", 8, 10)
+
+    def update_v():
+        tt(A("U"), IND(V, cf), A("YA"), Op.add)
+        tt(IND(V, A("LO", 0, 4)), A("U"), A("YB"), Op.add)
+
+    def update_o():
+        tt(A("OM"), IND(WO, ba), A("MK"), Op.mult)
+        tt(A("ON"), IND(WO, ab), A("NK"), Op.mult)
+        tt(A("NO"), A("OM"), A("ON"), Op.add)
+        cp(IND(WO, A("LO", 6, 10)), A("NO"))
+
+    def costs_in(st):
+        for j in range(4):
+            mm(A("D%d" % j), A("IDB"), A("ZR%d" % st, 2048 + 512 * j, 2560 + 512 * j), True, False)
+
+    def s_gather(j, table, lst, d0, sign):
+        gs = A("GS", 512 * j, 512 * j + 512)
+        act(gs, IND(table, A(lst, d0, d0 + 32)), Fn.Copy)
+        mm(A("D%d" % j), A(sign), gs, False, True)
+
+    def reduce_head(t, pl):
+        mm(A("E%d" % t, 0, 128), ONE, A("CK"), True, False)
+        mm(A("E%d" % t, 0, 128), tl(pl, t), A("IDB"), False, False)
+
+    def reduce(t, m, gi):
+        for k in range(16):
+            mm(A("E%d" % t, k, 128, 16), A(m, 2048 * t + k, 2048 * t + 2048, 16), A(gi), False, k == 15)
+
+    def top(t, e):
+        scan(tl(e, t), A("K16"), A("E%d" % t, 0, 128), 0.0, Op.add, Op.max)
+
+    def split(t, e, hi, fld):
+        last = A(e, 128 * t + 15, 128 * t + 128, 16)
+        ts2(A(hi, 8 * t, 8 * t + 8), last, MAG, MAG, Op.add, Op.subtract)
+        tt(A("FT", 128 * t + fld, 128 * t + 128, 16), last, A(hi, 8 * t, 8 * t + 8), Op.subtract)
+
+    def expand(t):
+        top(t, "EE")
+        split(t, "EE", "HI", 2)
+        tt(tl("XP", t), IND(tl("FT", t), BCA), A("RM", 0, 128), Op.mult)
+        mm(A("PP", 256 + 8 * t, 264 + 8 * t), tl("XP", t), A("GB"))
+
+    def owners(t):
+        ts1(A("AL", 8 * t, 8 * t + 8), A("PP", 256 + 8 * t, 264 + 8 * t), float(MID), Op.add)
+        ts2(tl("CO", t), IND(WO, A("AL", 8 * t, 8 * t + 8)), 1.0 / 4096, -0.3125, Op.mult, Op.add)
+
+    def repeat_0(hl):
+        wv = 16 * NV[0]
+        cp(A("SP0", 0, wv, 16), IND(V, A(hl, 0, NV[0] // 16)))
+        scan(A("VR0"), A("KR", 0, wv), A("SP0", 0, wv), 0.0, Op.mult, Op.add)
+
+    def repeat_1(hl):
+        cp(A("SP1", 0, NV[1]), IND(V, A(hl, 8, 8 + NV[1] // 16)))
+        for j in range(16):
+            asel(A("VR1", j, 16 * NV[1], 16), A("SP1", 0, NV[1]), [[0, NV[1]]], Op.is_ge, 0.0, 0, 0)
+
+    def least(zr, a, b):
+        for x in range(a, b, CH):
+            tt(A("M1", 16 * x, 16 * (x + CH)), IND(Y, A("CA", x, x + CH)), A(zr, 16 * x, 16 * (x + CH)), Op.min)
+
+    def compare(t, a, b):
+        for x in range(a, b, CH):
+            y = min(b, x + CH)
+            tt(A("M2", 2048 * t + 16 * x, 2048 * t + 16 * y), IND(V, A("CO", 128 * t + x, 128 * t + y)), A("VR%d" % t, 16 * x, 16 * y), Op.is_gt)
+
+    def flags(t):
+        tt(tl("EQB", t), IND(tl("E2", t), BC15), tl("CE", t), Op.is_equal)
+        act(tl("SGB", t), IND(tl("E2", t), BC15), Fn.Sign, scale=-1.0, bias=col(11 + t))
+
+    def prefix(t):
+        o = tl("PP", t)
+        mm(o, tl("EQB", t), A("N2T", 0, 128), False, False)
+        mm(o, tl("SGB", t), A("TRI", 0, 128), False, True)
+        for hs in (0, 1):
+            act(A("JK", 128 * hs, 128 * hs + 128), o, Fn.Sign, bias=col(5 + hs), accum_out=A("ACC", 2 * t + hs, 2 * t + hs + 1))
+
+    def same(bank, ty):
+        for hs in (0, 1):
+            for own in (0, 1):
+                j, x = 2 * ty + own, 6 * ty + 2 * own + hs
+                ts2(A("EQ", 128 * hs + j, 128 + 256 * hs, 4), A(bank, 0, 32 + 32 * hs), A("LF", x, x + 1), float(OFF), Op.is_equal, Op.mult)
+
+    costs_in(0)
+    for st in range(S):
+        hl, hc, hn, zr, last = "HL%d" % st, "HC%d" % st, "HN%d" % st, "ZR%d" % st, st == S - 1
+        relu = lambda j: act(A("M1", 2048 + 512 * j, 2560 + 512 * j), A("D%d" % j), Fn.Relu)
+        y_job = lambda j: s_gather(j, Y, "CA", 128 + 32 * j, "NIB")
+        cp(A("CA"), IND(WA, A(hl)))
+        y_job(0)
+        if st == 0:
+            ts1(A("PL1"), A("CA"), -float(MID), Op.add)
+            late_constants()
+            least(zr, 0, 128)
+            repeat_1(hl)
+        else:
+            update_v()
+            repeat_1(hl)
+            least(zr, 0, 64)
+            ts1(A("PL1"), A("CA"), -float(MID), Op.add)
+            least(zr, 64, 128)
+        y_job(1)
+        reduce_head(0, "PL1")
+        reduce_head(1, "PL1")
+        relu(0)
+        y_job(2)
+        relu(1)
+        reduce(0, "M1", "GI")
+        y_job(3)
+        u = 0
+        for t in (0, 1):
+            act(A("VCS", u, u + NS[t]), IND(V, A(hl, 8 * t + NV[t] // 16, 8 * t + 8)), Fn.Copy)
+            u += NS[t]
+        relu(2)
+        mm(A("PF", 0, 128), A("VCS"), A("NIB"))
+        relu(3)
+        act(A("VCT"), A("PF", 0, 128), Fn.Copy)
+        repeat_0(hl)
+        if st > 0:
+            update_o()
+        expand(0)
+        owners(0)
+        reduce(1, "M1", "NGI")
+        where = [128 * t + NV[t] + 32 * j for t in (0, 1) for j in range(NS[t] // 32)]
+        n0 = NS[0] // 32
+        sign = lambda k: act(A("M2", 16 * where[k], 16 * where[k] + 512), A("D%d" % k), Fn.Sign, bias=-0.5)
+        held = lambda k: mm(A("D%d" % k), A("VCT"), A("EXP", 512 * k, 512 * k + 512), True, False)
+        compare(0, 0, NV[0] // 2)
+        for k in range(n0):
+            held(k)
+            s_gather(k, V, "CO", where[k], "IDB")
+            if k == 0:
+                expand(1)
+        ts1(tl("PL2", 0), tl("CO", 0), -float(MID), Op.add)
+        compare(0, NV[0] // 2, NV[0])
+        owners(1)
+        for k in range(n0):
+            sign(k)
+        reduce_head(0, "PL2")
+        for k in range(n0, len(where)):
+            held(k)
+        act(A("FT", 0, 256, 16), A(hc), Fn.Copy)
+        reduce(0, "M2", "GI")
+        for k in range(n0, len(where)):
+            s_gather(k, V, "CO", where[k], "IDB")
+        for t in (0, 1):
+            act(tl("CE", t), IND(A(hc), BC0(8 * t, 8 * t + 8)), Fn.Identity, bias=col(13 + t))
+        for k in range(n0, len(where)):
+            sign(k)
+        compare(1, 0, CH)
+        ts1(tl("PL2", 1), tl("CO", 1), -float(MID), Op.add)
+        ts1(A("KI"), A("HI"), 1.0 / 4096, Op.mult)
+        reduce_head(1, "PL2")
+        mm(A("PP", 0, 128), ONE, A("TRI", 0, 128), True, False)
+        top(0, "E2")
+        ts1(A("KJ"), A("KI"), 15, Op.bitwise_and)
+        flags(0)
+        split(0, "E2", "HI2", 1)
+        cp(A("FT", 3, 256, 16), A("KJ"))
+        prefix(0)
+        mm(A("PF", 0, 128), tl("FT", 0), A("IDF"))
+        act(A("FL", 0, 128), A("PF", 0, 128), Fn.Copy)
+        mm(tl("PP", 1), ONE, A("TRI", 0, 128), True, False)
+        mm(tl("PP", 1), ONE, A("TRI", 128, 256), False, False)
+        mm(tl("PP", 1), tl("EQB", 0), A("N2T", 128, 256), False, False)
+        mm(tl("PP", 1), tl("SGB", 0), A("TRI", 128, 256), False, False)
+        act(A("PRE"), A("ACC", 0, 2), Fn.Identity, scale=-0.5, bias=128.0)
+        compare(1, CH, NV[1])
+        reduce(1, "M2", "GI")
+        mm(A("D0", 0, 64), ONE, A("CAB", 0, 64), True, False)
+        mm(A("D1", 0, 64), ONE, A("CAB", 64, 128), True, False)
+        top(1, "E2")
+        flags(1)
+        split(1, "E2", "HI2", 1)
+        act(A("VER"), A("SGB", 0, 256, 16), Fn.Identity, scale=-0.5, bias=0.5)
+        prefix(1)
+        mm(A("PF", 128, 256), tl("FT", 1), A("IDF"))
+        tt(A("DF"), A("FT", 1, 256, 16), A("FT", 0, 256, 16), Op.subtract)
+        tt(A("VD"), A("DF"), A("VER"), Op.mult)
+        tt(A(hn), A("VD"), A(hc), Op.add)
+        if not last:
+            tt(A("XH"), IND(A(hn), BC0(0, 16)), A("RM"), Op.mult)
+            for t in (0, 1):
+                mm(A("E0", 8 * t, 8 * t + 8), tl("XH", t), A("GB"))
+        act(A("FL", 128, 256), A("PF", 128, 256), Fn.Copy)
+        for hs in (0, 1):
+            ts2(A("DL", 2 * hs, 2 * hs + 2), A("CC", 20, 22), A("ACC", 2 + hs, 3 + hs), A("PRE", hs, hs + 1), Op.mult, Op.add)
+        if not last:
+            hs_, nl, nc = A("HS%d" % st), "%d" % (st + 1), A("HC%d" % (st + 1))
+            ts1(hs_, A("E0", 0, 16), float(MID), Op.add)
+            send(1, A("HL" + nl), hs_, "hl" + nl)
+            send(1, nc, A(hn), "hc" + nl, behind=[hs_])
+        cp(A("FC"), IND(A("FL"), A("DL")))
+        cp(A("FH"), A("FC", 16, 48))
+        op("v", 1, ve.transpose, A("TR"), A("FC"))
+        for j in (0, 1):
+            mm(A("E1", 32 * j, 32 * j + 32), A("SEL", 384, 512), A("FH"))
+        mm(A("D0", 0, 64, 2), A("SEL", 0, 128), A("FH"), False, False)
+        mm(A("D0", 1, 64, 2), A("SEL", 128, 256), A("FH"), False, True)
+        mm(A("D1", 0, 64, 2), A("SEL", 256, 384), A("FH"), False, False)
+        ts1(A("LU"), IND(A("TR"), PAR), float(MID), Op.add)
+        ts1(A("MK"), A("E1", 0, 64), col(3), Op.is_equal)
+        tt(A("AM"), IND(WA, fc), A("MK"), Op.mult)
+        mm(A("D1", 1, 64, 2), A("BO"), A("AM", 0, 32), False, True)
+        act(A("LF"), IND(A("TR"), PAR), Fn.Identity, bias=float(MID - OFF))
+        act(A("YA", 0, 32), IND(Y, la), Fn.Copy, scale=-1.0)
+        act(A("YA", 32, 64), IND(Y, la), Fn.Copy)
+        same("D0", 0)
+        scan(A("HB"), A("KH"), A("D1", 1, 64, 2), 0.0, Op.add, Op.max)
+        if not last:
+            act(A("NK"), A("MK"), Fn.Identity, scale=-1.0, bias=1.0)
+        ts1(A("LF", 8, 10), A("HB", 15, 32, 16), col(4), Op.subtract)
+        ts2(lb, A("HB", 15, 32, 16), col(4), float(OFF), Op.subtract, Op.add)
+        same("D1", 1)
+        act(A("YB", 0, 32), IND(Y, lb), Fn.Copy)
+        act(A("YB", 32, 64), IND(Y, lb), Fn.Copy, scale=-1.0)
+        for t in (0, 1):
+            mm(A("PF", 256 + 128 * t, 384 + 128 * t, 1, 8), A(hn, 8 * t, 8 * t + 8), A("IDF"))
+        act(A("HO", 256 * st, 256 * st + 256, 1, 8), A("PF", 256, 512, 1, 8), Fn.Identity, bias=float(MID))
+        if not last:
+            costs_in(st + 1)
+            tt(A("AN"), IND(WA, cf), A("NK"), Op.mult)
+        scan(A("CF"), A("KC"), A("EQ"), 0.0, Op.add, Op.max)
+        if not last:
+            tt(A("NA"), A("AN"), A("AM"), Op.add)
+        for ty in (0, 1):
+            for hs in (0, 1):
+                x, y = 2 * ty + hs, 127 + 256 * hs
+                ts2(A("LO", x, x + 7, 6), A("LF", x, x + 7, 6), A("CF", y, y + 1), col(7 + x), Op.add, Op.min)
+        if not last:
+            cp(IND(WA, A("LO", 0, 4)), A("NA"))
+        else:
+            store("s", T.ho[:, :], A("HO", 0, 768, 1, 8), "sh")
+            update_v()
+            store("y", T.vo[:, :], A("V", 0, C), "so")
+    for i in schedule(ops):
+        ops[i][5]()
+    for sem, val in count.items():
+        if known["g"].get(sem, 0) < val or sem == "qg":
+            g.wait_ge(T.sem[sem], val)

@@ -7,46 +7,47 @@ MID = 1280
 OFF = 5376
 MAG = 1.5 * 2.0 ** 35
 BIG = 1.0e9
-NS = (64, 32)
-NV = (128 - NS[0], 128 - NS[1])
-SPW = 16 * max(NV)
-CH = 32
+W1, W2 = 65536, 131072
+J2V = (96, 208)
+REP_V = 32
+NB = 3
 
 f32, bf, i32, u16, h16 = "float32", "bfloat16", "int32", "uint16", "float16"
 SB = {
     "WA": (WD, i32), "WO": (WD, i32), "Y": (WD, bf), "V": (WD, bf), "HD": (16, i32), "HDF": (16, f32), "Z": (256, bf),
-    "ZR0": (4096, bf), "ZR1": (4096, bf), "ZR2": (4096, bf), "M1": (4096, bf), "M2": (4096, bf), "GS": (2048, bf),
-    "SP0": (1024, bf), "SP1": (1024, bf), "KR": (1024, bf), "VR0": (16 * NV[0], bf), "VR1": (16 * NV[1], bf),
-    "HL0": (16, u16), "HL1": (16, u16), "HL2": (16, u16), "HC0": (16, f32), "HC1": (16, f32), "HC2": (16, f32),
-    "HS0": (16, u16), "HS1": (16, u16), "HN0": (16, f32), "HN1": (16, f32), "HN2": (16, f32), "HO": (768, f32),
-    "CA": (256, u16), "CO": (256, u16), "PL1": (256, h16), "PL2": (256, h16), "EE": (256, f32), "E2": (256, f32), "FT": (256, f32),
-    "HI": (16, f32), "HI2": (16, f32), "KI": (16, i32), "KJ": (16, i32), "XP": (256, h16), "XH": (256, h16), "AL": (16, u16),
-    "VCS": (128, bf), "VCT": (128, bf), "CE": (256, f32), "EQB": (256, bf), "SGB": (256, bf), "JK": (256, bf), "ACC": (4, f32), "PRE": (2, f32),
-    "DL": (4, u16), "FL": (264, f32), "FC": (64, f32), "FH": (32, h16), "TR": (64, f32), "LU": (16, u16), "LF": (16, f32), "LO": (16, u16),
-    "MK": (64, f32), "NK": (64, f32), "AM": (64, f32), "AN": (64, f32), "NA": (64, i32), "OM": (64, f32), "ON": (64, f32), "NO": (64, i32),
-    "HB": (32, f32), "EQ": (384, bf), "CF": (384, f32), "YA": (64, bf), "YB": (64, bf), "U": (64, bf),
-    "DF": (16, f32), "VER": (16, f32), "VD": (16, f32),
-    "IO": (256, f32), "IOC": (384, f32), "PI": (8, i32), "CC": (32, f32), "CI": (160, i32), "CL": (176, u16),
-    "ONF": (128, f32), "ONB": (512, bf), "IDF": (128, f32), "IDB": (128, bf), "NIB": (128, bf), "GB": (8, bf), "G0": (8, bf), "GI": (8, bf), "NGI": (8, bf),
-    "RM": (256, f32), "K16": (128, f32), "TRI": (256, bf), "N2T": (256, bf), "EXP": (16 * (NS[0] + NS[1]), bf), "CK": (128, bf),
-    "B0": (128, f32), "BO": (128, f32), "SEL": (512, bf), "CAB": (128, bf), "KH": (32, f32), "KT": (32, f32), "KC": (384, bf),
+    "ZR0": (2560, bf), "ZR1": (2560, bf), "ZR2": (2560, bf), "M1": (4096, bf), "M2": (4096, bf), "GS": (512 * NB, bf),
+    "ZT0": (128, bf), "ZT1": (128, bf), "ZT2": (128, bf), "SP0": (1024, bf), "SP1": (512, bf), "KR": (1024, bf), "VR": (16 * (J2V[1] - J2V[0]), bf),
+    "HL0": (16, u16), "HL1": (16, u16), "HL2": (16, u16), "FT0": (256, h16), "FT1": (256, h16), "FT2": (256, h16),
+    "HS0": (16, u16), "HS1": (16, u16), "HX0": (256, h16), "HX1": (256, h16), "HX2": (256, h16), "HO": (768, f32),
+    "CA": (256, u16), "CO": (256, u16), "PL1": (256, h16), "PL2": (256, h16), "EE": (512, f32), "E2": (272, f32),
+    "HI2": (32, f32), "HK": (16, f32), "KI": (16, i32), "XH": (256, h16), "AL": (16, u16), "LS": (256, f32),
+    "VCS": (256, bf), "VCT": (256, bf), "SPF": (512, bf), "FB": (512, bf), "JK": (256, bf), "ACC": (4, f32), "PRE": (2, f32),
+    "DL": (4, u16), "FL": (264, f32), "FC": (64, f32), "KB": (64, bf), "TR": (64, f32), "LU": (16, u16), "LF": (64, f32), "LN": (16, f32), "LO": (16, u16),
+    "MK": (96, f32), "AM": (64, f32), "DA": (64, f32), "NA": (64, i32), "DO": (64, f32), "NO": (64, i32),
+    "EQ": (384, bf), "CF": (384, f32), "YA": (64, bf), "YB": (64, bf), "VG": (64, bf), "U": (64, bf),
+    "IO": (256, bf), "IO8": (64, bf), "IOG": (128, bf), "IOC": (192, bf), "IO17": (136, bf), "PI": (8, i32), "CC": (48, f32), "CI": (128, i32), "CL": (144, u16),
+    "ONB": (1024, bf), "IDB": (128, bf), "NIB": (128, bf), "GB": (8, bf), "GI": (16, bf), "NGI": (16, bf), "GJ": (8, bf),
+    "RM": (256, bf), "RN": (1024, bf), "K16": (256, bf), "K17": (136, bf), "KL": (64, f32), "TRI": (256, bf), "NTR": (256, bf), "EXP": (512, bf),
+    "CK": (256, bf), "CK17": (136, bf), "I17": (136, bf), "I0": (136, bf), "CND": (48, bf),
+    "BO": (128, f32), "SEL": (640, f32), "SELK": (128, bf), "CAB": (320, bf), "KH": (32, f32), "KC": (384, bf),
 }
-PS = ["D0", "D1", "D2", "D3", "E0", "E1", "PP", "PF"]
+PS = ["D0", "D1", "D2", "E0", "E1", "LL", "PP", "PF"]
 SCRATCH = {k: ("sbuf", [128, w], d) for k, (w, d) in SB.items()}
 SCRATCH.update({k: ("psum", [128, 512], f32) for k in PS})
-NAO = 4
-SEMAPHORES = ["qg", "qv", "qs", "qp", "lh", "lz", "ly", "lv", "so", "sh", "z1", "z2", "hl1", "hl2", "hc1", "hc2", "sent"] + ["la%d" % j for j in range(NAO)]
-COSTS = [dict(pe=1.0, el=1.0, ga=1.56, sc=3.8, by=0.004, lat=2200, wake=60),
-         dict(pe=0.5, el=1.0, ga=1.56, sc=3.8, by=0.004, lat=2500, wake=100),
-         dict(pe=0.45, el=0.9, ga=1.0, sc=1.5, by=0.003, lat=2200, wake=60)]
-ROUNDS, SEED, DRIFT = 30000, 1, 0.002
+AO = [0, 1024, 1920, 2560]
+NAO = len(AO) - 1
+SEMAPHORES = ["qg", "qv", "qs", "qp", "lh", "lz", "ly", "lv", "so", "sh", "z1", "z2", "t1", "t2", "hl10", "hl11", "hl20", "hl21", "hc1", "hc2", "sent", "la0", "la1", "la2"]
+COSTS = [dict(pe=0.48, el=0.95, ga=1.5, sc=3.6, by=0.004, lat=1700, far=1200, wake=120),
+         dict(pe=0.6, el=1.15, ga=2.1, sc=5.0, by=0.005, lat=2200, far=2000, wake=120),
+         dict(pe=0.45, el=0.9, ga=1.1, sc=2.5, by=0.003, lat=2000, far=2800, wake=160)]
+ROUNDS, SEED, DRIFT, FREE = 40000, 1, 0.0005, 20
 PLAN = {}
 
 
-def A(name, lo=0, hi=None, step=1, rows=128):
+def A(name, lo=0, hi=None, step=1, rows=128, r0=0):
     if hi is None:
         hi = SB[name][0] if name in SB else 512
-    return ("ap", name, lo, hi, step, rows)
+    return ("ap", name, lo, hi, step, rows, r0)
 
 
 def IND(win, off):
@@ -62,7 +63,7 @@ def meet(a, b, same):
         return True
     if a[3] <= b[2] or b[3] <= a[2]:
         return False
-    return not (same and a[4] == b[4] and (a[2] - b[2]) % a[4] != 0)
+    return not (a[4] == b[4] and (a[2] - b[2]) % a[4] != 0)
 
 
 def width(x):
@@ -77,13 +78,13 @@ def schedule(ops):
     if "order" in PLAN:
         return PLAN["order"]
     m = len(ops)
-    before, seen, anc = [], {}, []
+    before, seen, anc, soft = [], {}, [], set()
     for i, (q, wr, rd, cost, lat, emit) in enumerate(ops):
         d = set()
         for aps, w_ in ((wr, True), (rd, False)):
             for x in aps:
                 for y, yw, yq, j in seen.get(x[1], []):
-                    if x[1] in PS or ((w_ or yw) and meet(x, y, yq == q)):
+                    if (x[1] in PS and (yq != q or q == "p")) or ((w_ or yw) and meet(x, y, yq == q)):
                         d.add(j)
         for aps, w_ in ((wr, True), (rd, False)):
             for x in aps:
@@ -93,14 +94,20 @@ def schedule(ops):
             if not mask >> j & 1:
                 keep.append(j)
                 mask |= anc[j] | 1 << j
+        if lat:
+            for j in [j for j in range(i) if ops[j][0] == q and ops[j][4]][-1:]:
+                if j not in keep:
+                    keep.append(j)
+                    soft.add((j, i))
+                    mask |= anc[j] | 1 << j
         anc.append(mask)
         before.append(keep)
     qs = ["gvspy".index(o[0]) for o in ops]
     sets = []
     for c in COSTS:
         busy = [o[3][1] + o[3][2] * c[o[3][0]] for o in ops]
-        lat = [o[4] and c["lat"] + o[4] * c["by"] for o in ops]
-        edge = [[(j, lat[j] + (0 if qs[i] == 3 and qs[j] == 3 else c["wake"])) for j in before[i]] for i in range(m)]
+        lat = [o[4] and c["far" if o[0] == "g" else "lat"] + o[4] * c["by"] for o in ops]
+        edge = [[(j, 0 if qs[i] == qs[j] == 3 or (j, i) in soft else lat[j] + c["wake"]) for j in before[i]] for i in range(m)]
         sets.append((busy, lat, edge))
 
     def finish(seq, k, trace=False):
@@ -114,7 +121,7 @@ def schedule(ops):
                     t, y = end[j] + e, j
             end[i] = free[q] = t + busy[i]
             who[q], why[i] = i, y
-        i = max(range(m), key=lambda j: end[j] + lat[j])
+        i = m - 1
         if not trace:
             return end[i] + lat[i]
         path = []
@@ -129,7 +136,35 @@ def schedule(ops):
         seed[0] = (seed[0] * 1103515245 + 12345) % 2147483648
         return (seed[0] >> 8) % k
 
-    seq = list(range(m))
+    def first_order(k):
+        busy, lat, edge = sets[k]
+        ahead = [list(e) for e in edge]
+        last = {}
+        for i in range(m):
+            if qs[i] != 3 and qs[i] in last:
+                ahead[i].append((last[qs[i]], 0))
+            last[qs[i]] = i
+        way, after = [busy[i] + lat[i] for i in range(m)], [[] for _ in range(m)]
+        for i in reversed(range(m)):
+            for j, e in ahead[i]:
+                way[j] = max(way[j], busy[j] + e + way[i])
+                after[j].append(i)
+        free, end, left, out = [0.0] * 5, [0.0] * m, [len(x) for x in ahead], []
+        ready = {i: 0.0 for i in range(m) if not left[i]}
+        while ready:
+            i = min(ready, key=lambda i: max(ready[i], free[qs[i]]) + busy[i] * (qs[i] == 3))
+            if qs[i] == 3:
+                t0 = max(ready[i], free[3]) + busy[i]
+                i = max((x for x in ready if qs[x] == 3 and ready[x] < t0), key=lambda x: way[x])
+            end[i] = free[qs[i]] = max(ready.pop(i), free[qs[i]]) + busy[i]
+            out.append(i)
+            for j in after[i]:
+                left[j] -= 1
+                if not left[j]:
+                    ready[j] = max(end[x] + e for x, e in ahead[j])
+        return out
+
+    seq = first_order(0)
     norm = [finish(seq, k) for k in range(len(sets))]
     score = lambda s_: sum(finish(s_, k) / norm[k] for k in range(len(sets)))
     cur = score(seq)
@@ -138,6 +173,12 @@ def schedule(ops):
         path = paths[rnd(len(paths))]
         z = rnd(len(path) - 1)
         i, j = path[z], path[z + 1]
+        if rnd(100) < FREE:
+            a_ = rnd(m - 1)
+            near = [x for x in seq[a_ + 1:a_ + 40] if qs[x] == qs[seq[a_]]][:4]
+            if not near:
+                continue
+            j, i = seq[a_], near[rnd(len(near))]
         if qs[i] == 4 or qs[j] == 4 or anc[i] >> j & 1:
             continue
         pi_, pj = seq.index(i), seq.index(j)
@@ -170,7 +211,8 @@ def rank_program(g, core, T, topo):
 
     def mk(x):
         if isinstance(x, tuple) and x[0] == "ap":
-            return T[x[1]][0:x[5], x[2]:x[3]:x[4]] if x[4] > 1 else T[x[1]][0:x[5], x[2]:x[3]]
+            r = slice(x[6], x[6] + x[5])
+            return T[x[1]][r, x[2]:x[3]:x[4]] if x[4] > 1 else T[x[1]][r, x[2]:x[3]]
         if isinstance(x, tuple) and x[0] == "ind":
             return mk(x[1]).indirect(mk(x[2]))
         return x
@@ -222,21 +264,26 @@ def rank_program(g, core, T, topo):
         if q == "p":
             cost = ("pe", 0, max(min(64, width(a[1])), width(a[2])) * (4 if size(a[1]) == 4 else 1))
         elif o[0] == "ind":
-            cost = ("sc", 50, width(o))
+            cost = ("sc", 60, width(o))
         elif any(x[0] == "ind" for x in ins):
-            cost = ("ga", 60, width(o))
+            cost = ("ga", 60 if q == "v" else 75, width(o))
         else:
             if rate == 0.5 and any(size(x) == 4 for x in [o] + ins if width(x) > 1):
                 rate = 1
             if rate == 2 and any(x[1] in PS for x in ins):
                 rate = 1
-            cost = ("el", {"v": 0, "s": 30, "g": 150}[q], max(64, rate * width(o)))
+            cost = ("el", {"v": 0, "s": 30, "g": 180}[q], max(64 * (q != "g"), rate * width(o)))
 
         def emit():
             order(q, wr, rd)
             call(*[mk(x) for x in a], **{k: mk(v) for k, v in kw.items()}).then_inc(T.sem["q" + q], 1)
             note(q, wr, rd, token(q, "q" + q, 1))
         ops.append((q, wr, rd, cost, 0, emit))
+
+    def together(k):
+        run = [ops.pop() for _ in range(k)][::-1]
+        cost = (run[0][3][0], sum(o[3][1] for o in run), sum(o[3][2] for o in run))
+        ops.append((run[0][0], [x for o in run for x in o[1]], [x for o in run for x in o[2]], cost, 0, lambda: [o[5]() for o in run]))
 
     ve, sc, pe = g.vector, g.scalar, g.tensor
     cp = lambda o, i: op("v", 0.5, ve.tensor_copy, o, i)
@@ -250,12 +297,12 @@ def rank_program(g, core, T, topo):
     iota = lambda o, p, b, c: op("g", 2, g.iota, o, p, b, c, **({} if SB[o[1]][1] == i32 else {"allow_small_or_imprecise_dtypes": True}))
     asel = lambda o, i, p, x, f, b, c: op("g", 2, g.affine_select, o, i, p, x, f, b, c)
 
-    def load(q, o, src, sem):
+    def load(q, o, src, sem, after=()):
         def emit():
-            order(q, [o], [])
+            order(q, [o], list(after))
             Q[q].dma_start(mk(o), src).then_inc(T.sem[sem], 16)
             note(q, [o], [], token(q, sem, 16))
-        ops.append((q, [o], [], ("by", 300, width(o) * size(o) * 128), 1, emit))
+        ops.append((q, [o], [], ("by", 100, width(o) * size(o) * 128), 1, emit))
 
     def store(q, dst, i, sem):
         def emit():
@@ -264,7 +311,7 @@ def rank_program(g, core, T, topo):
             note(q, [], [i], token(q, sem, 16))
         ops.append((q, [], [i], ("el", 100, 0), width(i) * size(i) * i[5], emit))
 
-    def send(hops, o, i, sem, after=(), behind=()):
+    def send(hops, o, i, sem, after=()):
         dst = T.cores[(rank + hops * HOP) % n]
         src = T.cores[(rank - hops * HOP) % n]
         rid, pid, _ = topo.addr(dst)
@@ -276,343 +323,433 @@ def rank_program(g, core, T, topo):
             token("g", "sent", len(topo.engines(core, dst)))
             count[sem] = len(topo.engines(src, core))
             note("x", [o], [], (sem, count[sem], {}))
-        ops.append(("g", [o] + list(behind), [i] + list(after), ("el", 600, 0), width(i) * size(i) * 128, emit))
+        ops.append(("g", [o], [i] + list(after), ("el", 3000 if sem == "t1" else 700, 0), width(i) * size(i) * 128, emit))
 
     WA, WO, Y, V = A("WA"), A("WO"), A("Y"), A("V")
-    BC15, BCA, BC0, PAR = A("CL", 0, 8), A("CL", 16, 24), (lambda a, b: A("CL", 32 + a, 32 + b)), A("CL", 160, 161)
+    BC0, PAR = (lambda a, b: A("CL", a, b)), A("CL", 128, 129)
     tl = lambda name, t: A(name, 128 * t, 128 * t + 128)
+    fld = lambda name, t, j: A(name, 128 * t + j, 128 * t + 128, 16)
     ONE = A("ONB", 0, 128)
+    SEL = lambda j: A("SEL", 128 * j, 128 * j + 128)
 
     load("y", A("Z"), T.zc[:, :], "lz")
     load("y", A("HD"), T.hd[:, :], "lh")
-    w = C // NAO
     for j in range(NAO):
-        load("y", A("WO", j * w, (j + 1) * w), T.ao[:, j * w:(j + 1) * w], "la%d" % j)
+        load("y", A("WO", AO[j], AO[j + 1]), T.ao[:, AO[j]:AO[j + 1]], "la%d" % j)
     load("y", A("Y", 0, C), T.yd[:, :], "ly")
-    load("y", A("V", 0, C), T.ve[:, :], "lv")
+    load("y", A("V", 0, C), T.ve[:, :], "lv", [A("WO", AO[NAO - 2], AO[NAO - 1])])
 
-    iota(A("CI", 32, 160), [[1, 128]], 0, 0)
-    iota(A("CI", 0, 32), [[-13, 2], [16, 16]], 15, 0)
+    iota(A("CI"), [[1, 128]], 0, 0)
     iota(A("PI", 0, 1), [[0, 1]], 0, 1)
-    iota(A("IO"), [[0, 16], [1, 16]], 0, 0)
     ms(A("ONB"), 1.0)
-    ms(A("ONF"), 1.0)
     ms(A("KR"), 1.0)
     ms(A("SP0"), 0.0)
     ms(A("KR", 0, 1024, 16), 0.0)
-    cp(A("CL", 0, 160), A("CI"))
+    cp(A("CL", 0, 128), A("CI"))
     ts1(A("PI", 1, 2), A("PI", 0, 1), 15, Op.bitwise_and)
     ts2(A("PI", 2, 3), A("PI", 0, 1), 4, 1, Op.arith_shift_right, Op.bitwise_and)
     ts1(A("PI", 3, 4), A("PI", 0, 1), 1, Op.bitwise_and)
+    ts1(A("PI", 4, 5), A("PI", 0, 1), 4, Op.arith_shift_right)
+    ts1(A("PI", 5, 6), A("PI", 0, 1), 31, Op.bitwise_and)
+    ms(A("SP1"), 0.0)
+    cp(A("CC", 0, 5), A("PI", 1, 6))
+    asel(A("IDB"), ONE, [[-1, 128]], Op.is_equal, 0.0, 0, 1)
+    iota(A("IO8"), [[0, 8], [1, 8]], 0, 0)
+    iota(A("IO"), [[0, 16], [1, 16]], 0, 0)
+    iota(A("IOC"), [[1, 192]], 0, 0)
+    ts1(A("GB"), A("IO8", 0, 8), col(3), Op.is_equal)
+    act(A("CK"), A("IO"), Fn.Identity, scale=-32.0, bias=480.0)
+    act(A("K16"), A("KR", 0, 256), Fn.Identity, scale=BIG, bias=-BIG)
+    act(A("ZR0", 1536, 2560), IND(A("Z", 192, 256), BC0(0, 64)), Fn.Copy)
+    for j, w_ in ((0, 64), (1, 32)):
+        sp = "SP%d" % j
+        cp(A(sp, 0, 16 * w_, 16), A("Z", 64 * j, 64 * j + w_))
+        scan(A("ZR0", 1024 * j, 1024 * j + 16 * w_), A("KR", 0, 16 * w_), A(sp, 0, 16 * w_), 0.0, Op.mult, Op.add)
+    mm(A("PP", 0, 128, 1, 64, 0), A("Z", 128, 192), A("IDB"))
+    mm(A("PP", 0, 128, 1, 64, 64), A("Z", 64, 128), A("IDB"))
+    act(A("ZT0"), A("PP", 0, 128), Fn.Copy)
+    send(1, A("ZT1"), A("ZT0"), "t1")
+    send(2, A("ZT2"), A("ZT0"), "t2")
+    cp(A("HL0"), A("HD"))
+    ts1(A("HDF"), A("HD"), -float(MID), Op.add)
     ms(A("WA", C, WD), NONE)
     ms(A("WO", C, WD), 0)
     ms(A("Y", C, WD), 0.0)
     ms(A("V", C, WD), 0.0)
-    cp(A("CC", 0, 3), A("PI", 1, 4))
-    asel(A("IDB"), ONE, [[-1, 128]], Op.is_equal, 0.0, 0, 1)
-    asel(A("G0"), A("ONB", 0, 8), [[-16, 8]], Op.is_ge, 0.0, 0, 1)
-    asel(A("GB"), A("G0"), [[16, 8]], Op.is_ge, 0.0, 15, -1)
-    iota(A("CK"), [[0, 8], [-32, 16]], 480, 0)
-    ms(A("SP1"), 0.0)
-    act(A("ZR0", 2048, 4096), IND(A("Z", 128, 256), BC0(0, 128)), Fn.Copy)
-    for j in range(2):
-        sp = "SP%d" % j
-        cp(A(sp, 0, 1024, 16), A("Z", 64 * j, 64 * j + 64))
-        scan(A("ZR0", 1024 * j, 1024 * j + 1024), A("KR"), A(sp), 0.0, Op.mult, Op.add)
-    cp(A("HL0"), A("HD"))
-    ts1(A("HDF"), A("HD"), -float(MID), Op.add)
-    act(A("GI"), A("GB"), Fn.Copy, scale=65536.0)
-    act(A("NGI"), A("GB"), Fn.Copy, scale=-65536.0)
+    for j in (0, 8):
+        act(A("GI", j, j + 8), A("GB"), Fn.Copy, scale=float(W1))
+    act(A("NGI"), A("GI"), Fn.Copy, scale=-1.0)
+    act(A("GJ"), A("GB"), Fn.Copy, scale=float(W2))
     act(A("NIB"), A("IDB"), Fn.Copy, scale=-1.0)
-    unpack = lambda j: ts1(A("WA", j * w, (j + 1) * w), A("WO", j * w, (j + 1) * w), 4095, Op.bitwise_and)
-    unpack(0)
+    unpack = lambda j: ts1(A("WA", AO[j], AO[j + 1]), A("WO", AO[j], AO[j + 1]), 4095, Op.bitwise_and)
     ts1(A("RM"), A("IO"), col(0), Op.is_equal)
-    ts2(A("K16"), A("IO", 0, 128), 0.0, -BIG, Op.is_equal, Op.mult)
-    ms(A("FT"), 0.0)
-    unpack(1)
+    ts1(A("SP1", 0, 512, 16), A("IOC", 0, 32), col(4), Op.is_equal)
+    scan(A("EXP"), A("KR", 0, 512), A("SP1"), 0.0, Op.mult, Op.add)
+    for b_ in ("FT0", "HX0", "HX1"):
+        ts1(A(b_), A("ONB", 0, 256), 0.0, Op.mult)
+    unpack(0)
     tt(A("XH"), IND(A("HDF"), BC0(0, 16)), A("RM"), Op.mult)
     for t in (0, 1):
         mm(A("PF", 256 + 8 * t, 264 + 8 * t), tl("XH", t), A("GB"))
-    act(A("HC0"), A("PF", 256, 272), Fn.Copy)
-    unpack(2)
-    for j, (a_, b_) in {3: (-1, 15), 5: (-2, -1), 6: (-2, -33), 7: (1, C), 8: (1, C + 16), 9: (1, C + 32),
-                        10: (1, C + 48), 15: (1, 1), 16: (8, 0), 17: (8, 256), 19: (1, -2.5)}.items():
-        act(col(j), col(0), Fn.Identity, scale=float(a_), bias=float(b_))
-    act(col(19), col(19), Fn.Abs)
-    act(A("VCS"), ONE, Fn.Copy, scale=0.0)
+    cp(A("FT0", 0, 256, 16), A("PF", 256, 272))
+    ms(A("SPF"), 0.0)
+    if NAO > 2:
+        unpack(1)
+    for j, (x_, a_, b_) in {5: (0, -1, -0.5), 6: (0, -1, -16.5), 7: (0, 1, C), 8: (0, 1, C + 16), 9: (0, 1, C + 32), 10: (0, 1, C + 48),
+                            15: (0, -1 / 16, 15 / 16), 16: (0, 4, 0), 17: (0, 4, 128), 19: (3, -4096, 7 * 4096 - MID),
+                            22: (0, 3072, -OFF - 15 * 3072)}.items():
+        act(col(j), col(x_), Fn.Identity, scale=float(a_), bias=float(b_))
     act(A("CC", 20, 22), A("ONB", 0, 2), Fn.Copy, scale=-0.5)
-    act(A("CAB"), ONE, Fn.Copy, scale=-32.0)
-    act(A("CAB", 65, 128, 2), A("ONB", 0, 32), Fn.Copy, scale=-OFF / 128.0)
-    asel(A("IDF"), A("ONF"), [[-1, 128]], Op.is_equal, 0.0, 0, 1)
-    asel(A("B0"), A("ONF"), [[-16, 8], [0, 16]], Op.is_ge, 0.0, 0, 1)
-    asel(A("BO"), A("B0"), [[16, 8], [0, 16]], Op.is_ge, 0.0, 15, -1)
-    iota(A("IOC"), [[1, 384]], 0, 0)
-    for t in (0, 1):
-        for j, v, d in ((11 + t, 11 * 65536 - 2048, -5 * 65536), (13 + t, 61440, -16 * 65536)):
-            iota(col(j + 12), [[0, 1]], v, 0)
-            asel(col(j), col(j + 12), [[0, 1]], Op.is_gt, float(v + d), NV[t], -1)
+    act(A("CAB", 0, 64), A("ONB", 0, 64), Fn.Copy, scale=(MID - OFF) / 128.0)
+    act(A("CAB", 64, 192, 2), A("ONB", 0, 64), Fn.Copy, scale=float(MID - OFF))
+    act(A("CAB", 65, 128, 2), A("ONB", 0, 32), Fn.Copy, scale=-float(OFF))
+    act(A("CAB", 129, 192, 2), A("ONB", 0, 32), Fn.Copy, scale=col(22))
+    act(A("CAB", 192, 256), A("ONB", 0, 64), Fn.Copy, scale=-MID / 128.0)
+    act(A("CAB", 256, 320), A("ONB", 0, 64), Fn.Copy, scale=0.0)
+    asel(A("RN"), A("ONB"), [[-16, 8], [0, 8], [-1, 16]], Op.is_equal, 0.0, 0, 1)
+    iota(A("IOG"), [[1, 8], [0, 16]], 0, 0)
+    iota(A("IO17"), [[0, 8], [1, 17]], 0, 0)
+    ts1(A("BO"), A("IOG"), col(3), Op.is_equal)
+    ts1(A("I0"), A("IO17"), 16.0, Op.is_lt)
+    act(A("CK17"), A("IO17"), Fn.Identity, scale=-32.0, bias=480.0)
+    asel(A("I17"), A("I0"), [[-16, 8], [-1, 17]], Op.is_equal, 0.0, 0, 1)
+    ts1(col(36), A("PI", 0, 1), float(J2V[0]), Op.is_lt)
+    ts1(col(37), A("PI", 0, 1), float(J2V[1] - 128), Op.is_ge)
     asel(A("TRI", 0, 128), ONE, [[1, 128]], Op.is_ge, 0.0, 0, -1)
-    asel(A("TRI", 128, 256), ONE, [[0, 128]], Op.is_ge, 0.0, 0, 0)
-    for j in range((NS[0] + NS[1]) // 32):
-        asel(A("EXP", 512 * j, 512 * j + 512), A("ONB"), [[-1, 32], [0, 16]], Op.is_equal, 0.0, -32 * j, 1)
-    ts2(col(4), col(0), 15.0, 32768.0, Op.is_lt, Op.mult)
+    act(A("TRI", 128, 256), ONE, Fn.Copy)
+    ts2(A("KL"), A("IO8"), col(3), -BIG, Op.is_equal, Op.mult)
     for j in range(4):
         ts1(col(27 + j), col(0), float(j), Op.is_equal)
-    ts2(col(18), col(0), 6.0, 2.0, Op.is_ge, Op.mult)
-    ts2(A("FL", 256, 264), A("RM", 3, 131, 16), -float(NONE - MID), float(NONE - MID), Op.mult, Op.add)
-    ts2(col(18), col(2), 32.0, col(18), Op.mult, Op.add)
-    unpack(3)
-    act(A("N2T"), A("TRI"), Fn.Copy, scale=-2.0)
-    for j in range(4):
-        act(A("SEL", 128 * j, 128 * j + 128), A("BO"), Fn.Copy, scale=col(27 + j))
+    unpack(NAO - 1)
+    act(A("KL"), A("KL"), Fn.Identity, bias=4096.0)
+    act(A("NTR"), A("TRI"), Fn.Copy, scale=-1.0)
+    act(col(31), col(29), Fn.Copy, scale=-1.0)
+    act(col(33), col(27), Fn.Copy, scale=-4096.0)
+    act(col(32), col(28), Fn.Identity, scale=4096.0, bias=col(33))
+    act(A("CC", 11, 13), A("CC", 36, 38), Fn.Identity, scale=-5.75 * W2, bias=10.75 * W2)
+    act(A("CC", 13, 15), A("CC", 36, 38), Fn.Copy, scale=-16.0 * W2)
+    for t in (0, 1):
+        act(A("CND", 8 * t, 8 * t + 8), A("ONB", 0, 8), Fn.Copy, scale=col(11 + t))
+        act(A("CND", 16 + 8 * t, 24 + 8 * t), A("ONB", 0, 8), Fn.Copy, scale=col(13 + t))
+    act(A("CND", 32, 48), A("ONB", 0, 16), Fn.Copy, scale=15 * 4096.0)
+    for j, x_ in enumerate((27, 28, 29, 31, 32)):
+        act(SEL(j), A("BO"), Fn.Copy, scale=col(x_))
+    act(A("SELK"), A("BO"), Fn.Copy, scale=col(30))
 
     def late_constants():
-        ts2(col(19), col(19), 1.0, col(18), Op.is_lt, Op.add)
-        ts2(A("KH"), A("IO", 0, 32), col(0), -BIG, Op.is_equal, Op.mult)
-        ts2(A("KT"), A("IO", 0, 32), col(15), 32768.0, Op.is_equal, Op.mult)
-        ts2(A("KC", 0, 128), A("IOC", 0, 128), col(16), float(OFF), Op.is_equal, Op.mult)
-        ts2(A("KC", 128, 384), A("IOC", 128, 384), col(17), float(OFF), Op.is_equal, Op.mult)
-        ts2(PAR, col(1), 16.0, col(19), Op.mult, Op.add)
-        tt(A("KH"), A("KH"), A("KT"), Op.add)
-        ms(A("KC", 128, 129), -16384.0)
+        ts2(A("K17"), A("IO17"), 0.0, -BIG, Op.is_equal, Op.mult)
+        ts2(col(18), col(0), 6.0, col(2), Op.is_ge, Op.add)
+        ts2(col(34), col(0), 2.0, col(18), Op.is_ge, Op.add)
+        ts2(col(35), col(2), 31.0, col(34), Op.mult, Op.add)
+        ts2(PAR, col(1), 16.0, col(35), Op.mult, Op.add)
+        ts2(A("FL", 256, 264), A("RM", 3, 131, 16), -float(NONE - MID), float(NONE - MID), Op.mult, Op.add)
+        ts2(A("KH"), A("IOC", 0, 32), col(0), -BIG, Op.is_equal, Op.mult)
+        ts2(A("KC", 0, 64), A("IOC", 0, 64), col(16), float(OFF), Op.is_equal, Op.mult)
+        ts2(A("KC", 64, 192), A("IOC", 64, 192), col(17), float(OFF), Op.is_equal, Op.mult)
+        cp(A("KH", 16, 32), A("KH", 0, 16))
+        cp(A("KC", 192, 384), A("KC", 0, 192))
+        ts1(A("KC", 192, 257, 64), A("KC", 0, 65, 64), -float(OFF), Op.add)
+        ms(A("KC", 64, 65), -16384.0)
+        act(A("KH"), A("KH"), Fn.Identity, bias=3072.0)
 
+    late_constants()
     send(1, A("ZR1"), A("ZR0"), "z1", after=[V])
-    send(2, A("ZR2"), A("ZR0"), "z2", after=[V])
 
-    cf, fc, la, ab, ba, lb = A("LU", 0, 4), A("LU", 2, 6), A("LU", 6, 8), A("LU", 6, 10), A("LU", 8, 12), A("LU", 8, 10)
+    cf, ff, ab, ba, lb = A("LU", 0, 4), A("LU", 2, 6), A("LU", 6, 10), A("LU", 8, 12), A("LU", 8, 10)
+    MKS = A("MK", 32, 96)
+    write_v = lambda: cp(IND(V, A("LO", 0, 4)), A("U"))
+    go = lambda line, k=1: [next(line, None) for _ in range(k)]
+    bank = [0]
 
-    def update_v():
-        tt(A("U"), IND(V, cf), A("YA"), Op.add)
-        tt(IND(V, A("LO", 0, 4)), A("U"), A("YB"), Op.add)
+    def s_job(first, table, lst, d0, d1, sign, out, fn, **kw):
+        j, w_ = bank[0] % NB, 16 * (d1 - d0)
+        bank[0] += 1
+        gs, b_ = A("GS", 512 * j, 512 * j + w_), A("D%d" % j, 0, w_)
+        act(gs, IND(table, A(lst, d0, d1)), Fn.Copy)
+        yield
+        mm(b_, *first, True, False)
+        mm(b_, A(sign), gs, False, True)
+        yield
+        act(A(out, 16 * d0, 16 * d1), b_, fn, **kw)
 
-    def update_o():
-        tt(A("OM"), IND(WO, ba), A("MK"), Op.mult)
-        tt(A("ON"), IND(WO, ab), A("NK"), Op.mult)
-        tt(A("NO"), A("OM"), A("ON"), Op.add)
-        cp(IND(WO, A("LO", 6, 10)), A("NO"))
+    def head_1(t):
+        mm(A("E%d" % t, 0, 256), ONE, A("CK"), True, False)
+        mm(A("E%d" % t, 128 * t, 128 * t + 128), tl("PL1", t), A("IDB"), False, False)
+        together(2)
 
-    def costs_in(st):
-        for j in range(4):
-            mm(A("D%d" % j), A("IDB"), A("ZR%d" % st, 2048 + 512 * j, 2560 + 512 * j), True, False)
+    def head_2(t, ft):
+        e = "E%d" % t
+        mm(A(e, 0, 136), ONE, A("CK17"), True, False)
+        mm(A(e, 16, 136, 17), A("IDB"), A("CND", 8 * t, 8 * t + 8), False, False)
+        mm(A(e, 16, 136, 17), A("IDB"), fld(ft, t, 0), False, False)
+        mm(A(e, 0, 136), tl("PL2", t), A("I17"), False, False)
+        together(4)
 
-    def s_gather(j, table, lst, d0, sign):
-        gs = A("GS", 512 * j, 512 * j + 512)
-        act(gs, IND(table, A(lst, d0, d0 + 32)), Fn.Copy)
-        mm(A("D%d" % j), A(sign), gs, False, True)
-
-    def reduce_head(t, pl):
-        mm(A("E%d" % t, 0, 128), ONE, A("CK"), True, False)
-        mm(A("E%d" % t, 0, 128), tl(pl, t), A("IDB"), False, False)
-
-    def reduce(t, m, gi):
+    def reduce(a, b, m, gi):
+        t, (step, end) = a // 128, (16, 256) if m == "M1" else (17, 136)
         for k in range(16):
-            mm(A("E%d" % t, k, 128, 16), A(m, 2048 * t + k, 2048 * t + 2048, 16), A(gi), False, k == 15)
+            mm(A("E%d" % t, k, end, step, b - a, a - 128 * t), A(m, 16 * a + k, 16 * b, 16), A(gi), False, k == 15)
+            if k % 4 == 3:
+                together(4)
 
-    def top(t, e):
-        scan(tl(e, t), A("K16"), A("E%d" % t, 0, 128), 0.0, Op.add, Op.max)
+    def to_list(src, j, t, base, out):
+        for x in range(8):
+            mm(A("LL", base + 8 * x, base + 8 * x + 8), A("RN", 128 * x, 128 * x + 128), fld(src, t, j))
+        together(8)
+        yield
+        scan(A("LS", base, base + 64), A("KL"), A("LL", base, base + 64), 0.0, Op.add, Op.max)
+        yield
+        ts1(out, A("LS", base + 7, base + 64, 8), col(19), Op.subtract)
 
-    def split(t, e, hi, fld):
-        last = A(e, 128 * t + 15, 128 * t + 128, 16)
-        ts2(A(hi, 8 * t, 8 * t + 8), last, MAG, MAG, Op.add, Op.subtract)
-        tt(A("FT", 128 * t + fld, 128 * t + 128, 16), last, A(hi, 8 * t, 8 * t + 8), Op.subtract)
+    def owners(t, ft):
+        scan(A("EE", 256 * t, 256 * t + 256), A("K16"), A("E%d" % t, 0, 256), 0.0, Op.add, Op.max)
+        yield
+        tt(fld(ft, t, 2), A("EE", 384 * t + 15, 384 * t + 128, 16), A("EE", 128 * t + 143, 128 * t + 256, 16), Op.subtract)
+        al = A("AL", 8 * t, 8 * t + 8)
+        yield from to_list(ft, 2, t, 64 * t, al)
+        yield
+        ts2(tl("CO", t), IND(WO, al), 1.0 / 4096, -0.3125, Op.mult, Op.add)
+        yield
+        ts1(tl("PL2", t), tl("CO", t), -float(MID), Op.add)
 
-    def expand(t):
-        top(t, "EE")
-        split(t, "EE", "HI", 2)
-        tt(tl("XP", t), IND(tl("FT", t), BCA), A("RM", 0, 128), Op.mult)
-        mm(A("PP", 256 + 8 * t, 264 + 8 * t), tl("XP", t), A("GB"))
+    LT, EQL = (lambda b_, t, s_=1: A(b_, 128 + 128 * t, 256 + 128 * t, s_)), (lambda b_, t, s_=1: A(b_, 384 * t, 384 * t + 128, s_))
 
-    def owners(t):
-        ts1(A("AL", 8 * t, 8 * t + 8), A("PP", 256 + 8 * t, 264 + 8 * t), float(MID), Op.add)
-        ts2(tl("CO", t), IND(WO, A("AL", 8 * t, 8 * t + 8)), 1.0 / 4096, -0.3125, Op.mult, Op.add)
+    def verdict(t, st):
+        ft, hx, x = "FT%d" % st, "HX%d" % st, 136 * t
+        best, new = A("E2", x + 15, x + 136, 17), A("E2", x + 16, x + 136, 17)
+        h0, h1 = A("HI2", 16 * t, 16 * t + 8), A("HI2", 16 * t + 8, 16 * t + 16)
+        scan(A("E2", x, x + 136), A("K17"), A("E%d" % t, 0, 136), 0.0, Op.add, Op.max)
+        yield
+        ts1(LT("SPF", t, 16), best, col(11 + t), Op.is_lt)
+        tt(EQL("SPF", t, 16), best, A("LL", 256 + 8 * t, 264 + 8 * t), Op.is_equal)
+        ts2(h0, best, MAG, MAG, Op.add, Op.subtract)
+        yield
+        scan(A("FB", 256 * t, 256 * t + 256), A("KR", 0, 256), A("SPF", 256 * t, 256 * t + 256), 0.0, Op.mult, Op.add)
+        tt(fld(ft, t, 1), best, h0, Op.subtract)
+        yield
+        ts2(h1, new, MAG, MAG, Op.add, Op.subtract)
+        yield
+        tt(fld(hx, t, 0), new, h1, Op.subtract)
+        if st < S - 1:
+            hs_ = A("HS%d" % st, 8 * t, 8 * t + 8)
+            yield from to_list(hx, 0, t, 128 + 64 * t, hs_)
+            send(1, A("HL%d" % (st + 1), 8 * t, 8 * t + 8), hs_, "hl%d%d" % (st + 1, t))
 
-    def repeat_0(hl):
-        wv = 16 * NV[0]
-        cp(A("SP0", 0, wv, 16), IND(V, A(hl, 0, NV[0] // 16)))
-        scan(A("VR0"), A("KR", 0, wv), A("SP0", 0, wv), 0.0, Op.mult, Op.add)
-
-    def repeat_1(hl):
-        cp(A("SP1", 0, NV[1]), IND(V, A(hl, 8, 8 + NV[1] // 16)))
+    def repeat_g():
+        x, y = J2V[0] + REP_V, J2V[1]
         for j in range(16):
-            asel(A("VR1", j, 16 * NV[1], 16), A("SP1", 0, NV[1]), [[0, NV[1]]], Op.is_ge, 0.0, 0, 0)
+            asel(A("VR", 16 * REP_V + j, 16 * (y - J2V[0]), 16), A("VCS", x, y), [[0, y - x]], Op.is_ge, 0.0, 0, 0)
+        together(16)
 
     def least(zr, a, b):
-        for x in range(a, b, CH):
-            tt(A("M1", 16 * x, 16 * (x + CH)), IND(Y, A("CA", x, x + CH)), A(zr, 16 * x, 16 * (x + CH)), Op.min)
+        x = 16 * (a - 96 * (a >= 192))
+        tt(A("M1", 16 * a, 16 * b), IND(Y, A("CA", a, b)), A(zr, x, x + 16 * (b - a)), Op.min)
 
-    def compare(t, a, b):
-        for x in range(a, b, CH):
-            y = min(b, x + CH)
-            tt(A("M2", 2048 * t + 16 * x, 2048 * t + 16 * y), IND(V, A("CO", 128 * t + x, 128 * t + y)), A("VR%d" % t, 16 * x, 16 * y), Op.is_gt)
-
-    def flags(t):
-        tt(tl("EQB", t), IND(tl("E2", t), BC15), tl("CE", t), Op.is_equal)
-        act(tl("SGB", t), IND(tl("E2", t), BC15), Fn.Sign, scale=-1.0, bias=col(11 + t))
+    def compare(a, b):
+        tt(A("M2", 16 * a, 16 * b), IND(V, A("CO", a, b)), A("VR", 16 * (a - J2V[0]), 16 * (b - J2V[0])), Op.is_gt)
 
     def prefix(t):
         o = tl("PP", t)
-        mm(o, tl("EQB", t), A("N2T", 0, 128), False, False)
-        mm(o, tl("SGB", t), A("TRI", 0, 128), False, True)
+        mm(o, LT("FB", t), A("TRI", 0, 128), t == 0, False)
+        mm(o, EQL("FB", t), A("NTR", 0, 128), False, True)
+        together(2)
+        yield
         for hs in (0, 1):
             act(A("JK", 128 * hs, 128 * hs + 128), o, Fn.Sign, bias=col(5 + hs), accum_out=A("ACC", 2 * t + hs, 2 * t + hs + 1))
 
-    def same(bank, ty):
+    def same_citizen():
         for hs in (0, 1):
             for own in (0, 1):
-                j, x = 2 * ty + own, 6 * ty + 2 * own + hs
-                ts2(A("EQ", 128 * hs + j, 128 + 256 * hs, 4), A(bank, 0, 32 + 32 * hs), A("LF", x, x + 1), float(OFF), Op.is_equal, Op.mult)
+                x = 2 * own + hs
+                act(A("EQ", 64 * hs + own, 64 + 128 * hs, 2), A("D0", 0, 32 + 32 * hs), Fn.Abs, bias=A("LN", x, x + 1))
+        act(A("EQ", 0, 192), A("EQ", 0, 192), Fn.Relu, scale=-float(OFF), bias=float(OFF))
 
-    costs_in(0)
+    def same_asset(own):
+        for hs in (0, 1):
+            j, x = 192 + 64 * hs, 47 + 16 * hs if own else 6 + hs
+            ts2(A("EQ", j + own, j + 64 + 64 * hs, 2), A("D1", 0, 32 + 32 * hs), A("LF", x, x + 1), float(OFF), Op.is_equal, Op.mult)
+
     for st in range(S):
-        hl, hc, hn, zr, last = "HL%d" % st, "HC%d" % st, "HN%d" % st, "ZR%d" % st, st == S - 1
-        relu = lambda j: act(A("M1", 2048 + 512 * j, 2560 + 512 * j), A("D%d" % j), Fn.Relu)
-        y_job = lambda j: s_gather(j, Y, "CA", 128 + 32 * j, "NIB")
-        cp(A("CA"), IND(WA, A(hl)))
-        y_job(0)
-        if st == 0:
-            ts1(A("PL1"), A("CA"), -float(MID), Op.add)
-            late_constants()
-            least(zr, 0, 128)
-            repeat_1(hl)
-        else:
-            update_v()
-            repeat_1(hl)
-            least(zr, 0, 64)
-            ts1(A("PL1"), A("CA"), -float(MID), Op.add)
-            least(zr, 64, 128)
-        y_job(1)
-        reduce_head(0, "PL1")
-        reduce_head(1, "PL1")
-        relu(0)
-        y_job(2)
-        relu(1)
-        reduce(0, "M1", "GI")
-        y_job(3)
-        u = 0
+        hl, ft, hx, zr, later, last = "HL%d" % st, "FT%d" % st, "HX%d" % st, "ZR%d" % st, st > 0, st == S - 1
+        ya, yb, yc = [s_job((A("ZT%d" % st, 0, 128, 1, 32, x % 128), A("EXP", 0, 512, 1, 32, x % 128)), Y, "CA", x, x + 32, "NIB", "M1", Fn.Relu)
+                      for x in (96, 128, 160)]
+        held = lambda x, y: (A("VCT", x // 128 * 128, x // 128 * 128 + 128, 1, 32, x % 128 // 32 * 32),
+                             A("EXP", 16 * (x % 32), 16 * (x % 32 + y - x), 1, 32, x % 128 // 32 * 32))
+        va, vb, vc, vd, vf = [s_job(held(x, y), V, "CO", x, y, "IDB", "M2", Fn.Sign, bias=-0.5)
+                              for x, y in ((0, 32), (32, 64), (64, 96), (224, 256), (J2V[1], 224))]
+        own0, own1, ver0, ver1, pre0, pre1 = owners(0, ft), owners(1, ft), verdict(0, st), verdict(1, st), prefix(0), prefix(1)
+        cp(tl("CA", 0), IND(WA, A(hl, 0, 8)))
+        go(ya, 2)
+        if later:
+            write_v()
+        cp(tl("CA", 1), IND(WA, A(hl, 8, 16)))
+        least(zr, 0, 32)
+        act(tl("VCS", 1), IND(V, A(hl, 8, 16)), Fn.Copy)
+        repeat_g()
+        go(yb, 2)
+        ts1(A("PL1"), A("CA"), -float(MID), Op.add)
+        head_1(0)
+        least(zr, 32, 64)
+        go(ya)
+        reduce(96, 128, "M1", "NGI")
+        reduce(0, 64, "M1", "GI")
+        act(tl("VCS", 0), IND(V, A(hl, 0, 8)), Fn.Copy)
+        least(zr, 64, 96)
+        reduce(64, 96, "M1", "GI")
+        go(yc, 2)
         for t in (0, 1):
-            act(A("VCS", u, u + NS[t]), IND(V, A(hl, 8 * t + NV[t] // 16, 8 * t + 8)), Fn.Copy)
-            u += NS[t]
-        relu(2)
-        mm(A("PF", 0, 128), A("VCS"), A("NIB"))
-        relu(3)
-        act(A("VCT"), A("PF", 0, 128), Fn.Copy)
-        repeat_0(hl)
-        if st > 0:
-            update_o()
-        expand(0)
-        owners(0)
-        reduce(1, "M1", "NGI")
-        where = [128 * t + NV[t] + 32 * j for t in (0, 1) for j in range(NS[t] // 32)]
-        n0 = NS[0] // 32
-        sign = lambda k: act(A("M2", 16 * where[k], 16 * where[k] + 512), A("D%d" % k), Fn.Sign, bias=-0.5)
-        held = lambda k: mm(A("D%d" % k), A("VCT"), A("EXP", 512 * k, 512 * k + 512), True, False)
-        compare(0, 0, NV[0] // 2)
-        for k in range(n0):
-            held(k)
-            s_gather(k, V, "CO", where[k], "IDB")
-            if k == 0:
-                expand(1)
-        ts1(tl("PL2", 0), tl("CO", 0), -float(MID), Op.add)
-        compare(0, NV[0] // 2, NV[0])
-        owners(1)
-        for k in range(n0):
-            sign(k)
-        reduce_head(0, "PL2")
-        for k in range(n0, len(where)):
-            held(k)
-        act(A("FT", 0, 256, 16), A(hc), Fn.Copy)
-        reduce(0, "M2", "GI")
-        for k in range(n0, len(where)):
-            s_gather(k, V, "CO", where[k], "IDB")
-        for t in (0, 1):
-            act(tl("CE", t), IND(A(hc), BC0(8 * t, 8 * t + 8)), Fn.Identity, bias=col(13 + t))
-        for k in range(n0, len(where)):
-            sign(k)
-        compare(1, 0, CH)
-        ts1(tl("PL2", 1), tl("CO", 1), -float(MID), Op.add)
-        ts1(A("KI"), A("HI"), 1.0 / 4096, Op.mult)
-        reduce_head(1, "PL2")
-        mm(A("PP", 0, 128), ONE, A("TRI", 0, 128), True, False)
-        top(0, "E2")
-        ts1(A("KJ"), A("KI"), 15, Op.bitwise_and)
-        flags(0)
-        split(0, "E2", "HI2", 1)
-        cp(A("FT", 3, 256, 16), A("KJ"))
-        prefix(0)
-        mm(A("PF", 0, 128), tl("FT", 0), A("IDF"))
-        act(A("FL", 0, 128), A("PF", 0, 128), Fn.Copy)
-        mm(tl("PP", 1), ONE, A("TRI", 0, 128), True, False)
-        mm(tl("PP", 1), ONE, A("TRI", 128, 256), False, False)
-        mm(tl("PP", 1), tl("EQB", 0), A("N2T", 128, 256), False, False)
-        mm(tl("PP", 1), tl("SGB", 0), A("TRI", 128, 256), False, False)
+            mm(tl("PF", t), tl("VCS", t), A("NIB"))
+        together(2)
+        head_1(1)
+        least(zr, 192, 208)
+        go(yb)
+        go(own0)
+        if later:
+            tt(A("NO"), IND(WO, ab), A("DO"), Op.add)
+        act(A("VCT"), A("PF", 0, 256), Fn.Copy)
+        go(own0)
+        if later:
+            cp(IND(WO, A("LO", 6, 10)), A("NO"))
+        go(yc)
+        act(A("SP0", 0, 16 * REP_V, 16), IND(V, A(hl, J2V[0] // 16, (J2V[0] + REP_V) // 16)), Fn.Copy)
+        go(own0, 3)
+        reduce(128, 192, "M1", "NGI")
+        go(va)
+        least(zr, 208, 224)
+        go(own0)
+        reduce(192, 224, "M1", "GI")
+        go(va)
+        least(zr, 224, 256)
+        go(vb)
+        reduce(224, 256, "M1", "GI")
+        go(vb)
+        head_2(0, ft)
+        scan(A("VR", 0, 16 * REP_V), A("KR", 0, 16 * REP_V), A("SP0", 0, 16 * REP_V), 0.0, Op.mult, Op.add)
+        go(va)
+        go(own1, 2)
+        go(vc, 2)
+        compare(96, 112)
+        go(own1, 2)
+        mm(A("LL", 256, 272), A("IDB"), A(ft, 0, 256, 16), True, False)
+        mm(A("LL", 256, 272), A("IDB"), A("CND", 16, 32), False, False)
+        mm(A("LL", 256, 272), A("IDB"), A("CND", 32, 48), False, True)
+        together(3)
+        go(vb)
+        reduce(0, 64, "M2", "GJ")
+        go(own1)
+        compare(112, 128)
+        reduce(96, 128, "M2", "GJ")
+        go(vc)
+        act(A("HK"), A("EE", 143, 384, 16), Fn.Copy, scale=1.0 / W1)
+        go(own1)
+        reduce(64, 96, "M2", "GJ")
+        go(vd, 2)
+        head_2(1, ft)
+        compare(128, 160)
+        ts1(A("KI"), A("HK"), -0.47, Op.add)
+        go(vf, 2)
+        go(ver0)
+        tt(A(ft, 3, 256, 16), A("HK"), A("KI"), Op.subtract)
+        go(ver0)
+        go(vd)
+        compare(160, 192)
+        reduce(224, 256, "M2", "GJ")
+        go(ver0)
+        go(pre0)
+        reduce(128, 192, "M2", "GJ")
+        go(vf)
+        go(ver0)
+        compare(192, J2V[1])
+        reduce(192, 224, "M2", "GJ")
+        mm(tl("PF", 0), tl(ft, 0), A("IDB"))
+        go(pre0)
+        act(A("FL", 0, 128), tl("PF", 0), Fn.Copy)
         act(A("PRE"), A("ACC", 0, 2), Fn.Identity, scale=-0.5, bias=128.0)
-        compare(1, CH, NV[1])
-        reduce(1, "M2", "GI")
+        go(ver0)
+        mm(tl("PP", 1), LT("FB", 0), A("TRI", 128, 256), True, False)
+        mm(tl("PP", 1), EQL("FB", 0), A("NTR", 128, 256), False, False)
+        together(2)
+        go(ver1)
+        go(ver0)
+        go(ver1)
+        go(ver0)
+        go(ver1)
+        go(pre1)
+        mm(tl("PF", 1), tl(ft, 1), A("IDB"))
+        go(pre1)
+        act(A("FL", 128, 256), tl("PF", 1), Fn.Copy)
+        go(ver1, 2)
         mm(A("D0", 0, 64), ONE, A("CAB", 0, 64), True, False)
-        mm(A("D1", 0, 64), ONE, A("CAB", 64, 128), True, False)
-        top(1, "E2")
-        flags(1)
-        split(1, "E2", "HI2", 1)
-        act(A("VER"), A("SGB", 0, 256, 16), Fn.Identity, scale=-0.5, bias=0.5)
-        prefix(1)
-        mm(A("PF", 128, 256), tl("FT", 1), A("IDF"))
-        tt(A("DF"), A("FT", 1, 256, 16), A("FT", 0, 256, 16), Op.subtract)
-        tt(A("VD"), A("DF"), A("VER"), Op.mult)
-        tt(A(hn), A("VD"), A(hc), Op.add)
+        mm(A("D1", 0, 128), A("IDB"), A("CAB", 64, 192), True, False)
         if not last:
-            tt(A("XH"), IND(A(hn), BC0(0, 16)), A("RM"), Op.mult)
-            for t in (0, 1):
-                mm(A("E0", 8 * t, 8 * t + 8), tl("XH", t), A("GB"))
-        act(A("FL", 128, 256), A("PF", 128, 256), Fn.Copy)
+            mm(A("E1", 0, 128), ONE, A("CAB", 192, 320), True, False)
+        go(ver1)
         for hs in (0, 1):
             ts2(A("DL", 2 * hs, 2 * hs + 2), A("CC", 20, 22), A("ACC", 2 + hs, 3 + hs), A("PRE", hs, hs + 1), Op.mult, Op.add)
-        if not last:
-            hs_, nl, nc = A("HS%d" % st), "%d" % (st + 1), A("HC%d" % (st + 1))
-            ts1(hs_, A("E0", 0, 16), float(MID), Op.add)
-            send(1, A("HL" + nl), hs_, "hl" + nl)
-            send(1, nc, A(hn), "hc" + nl, behind=[hs_])
+        go(ver1)
         cp(A("FC"), IND(A("FL"), A("DL")))
-        cp(A("FH"), A("FC", 16, 48))
-        op("v", 1, ve.transpose, A("TR"), A("FC"))
-        for j in (0, 1):
-            mm(A("E1", 32 * j, 32 * j + 32), A("SEL", 384, 512), A("FH"))
-        mm(A("D0", 0, 64, 2), A("SEL", 0, 128), A("FH"), False, False)
-        mm(A("D0", 1, 64, 2), A("SEL", 128, 256), A("FH"), False, True)
-        mm(A("D1", 0, 64, 2), A("SEL", 256, 384), A("FH"), False, False)
-        ts1(A("LU"), IND(A("TR"), PAR), float(MID), Op.add)
-        ts1(A("MK"), A("E1", 0, 64), col(3), Op.is_equal)
-        tt(A("AM"), IND(WA, fc), A("MK"), Op.mult)
-        mm(A("D1", 1, 64, 2), A("BO"), A("AM", 0, 32), False, True)
-        act(A("LF"), IND(A("TR"), PAR), Fn.Identity, bias=float(MID - OFF))
-        act(A("YA", 0, 32), IND(Y, la), Fn.Copy, scale=-1.0)
-        act(A("YA", 32, 64), IND(Y, la), Fn.Copy)
-        same("D0", 0)
-        scan(A("HB"), A("KH"), A("D1", 1, 64, 2), 0.0, Op.add, Op.max)
+        act(A("KB"), IND(A("FL"), A("DL")), Fn.Copy)
         if not last:
-            act(A("NK"), A("MK"), Fn.Identity, scale=-1.0, bias=1.0)
-        ts1(A("LF", 8, 10), A("HB", 15, 32, 16), col(4), Op.subtract)
-        ts2(lb, A("HB", 15, 32, 16), col(4), float(OFF), Op.subtract, Op.add)
-        same("D1", 1)
-        act(A("YB", 0, 32), IND(Y, lb), Fn.Copy)
-        act(A("YB", 32, 64), IND(Y, lb), Fn.Copy, scale=-1.0)
+            send(1, A("FT%d" % (st + 1)), A(hx), "hc%d" % (st + 1))
+            if st == 0:
+                send(2, A("ZR2"), A("ZR0"), "z2")
+        FH = A("FC", 16, 48)
+        mm(A("D0", 0, 64, 2), SEL(0), FH, False, False)
+        for j in (0, 1):
+            mm(A("E0", 32 * j, 32 * j + 32), A("SELK"), A("KB", 16, 48))
+        together(2)
+        op("v", 1, ve.transpose, A("TR"), A("FC"))
+        mm(A("D0", 1, 64, 2), SEL(1), FH, False, True)
+        mm(A("D1", 0, 64, 2), SEL(2), FH, False, False)
+        together(2)
+        ts1(A("LU"), IND(A("TR"), PAR), float(MID), Op.add)
+        act(A("LN"), IND(A("TR"), PAR), Fn.Identity, scale=-1.0, bias=float(OFF - MID))
+        ts1(A("MK", 0, 64), A("E0", 0, 64), col(15), Op.is_equal)
+        act(A("LF", 0, 16), A("LN"), Fn.Copy, scale=-1.0)
+        tt(A("AM"), IND(WA, ff), A("MK", 0, 64), Op.mult)
+        mm(A("D1", 1, 128, 2), A("BO"), A("AM"), False, True)
+        same_citizen()
+        if not last:
+            act(A("MK", 64, 96), A("MK", 0, 32), Fn.Copy, scale=-1.0)
+            mm(A("E1", 0, 64), A("BO"), A("AM"), False, False)
+            for j in (0, 1):
+                mm(A("E1", 32 * j, 32 * j + 32), SEL(3), FH, False, False)
+                mm(A("E1", 64 + 32 * j, 96 + 32 * j), SEL(4), FH, False, j == 1)
+            together(5)
+        scan(A("LF", 32, 64), A("KH"), A("D1", 65, 128, 2), 0.0, Op.add, Op.max)
+        same_asset(0)
+        ts1(lb, A("LF", 47, 64, 16), float(OFF), Op.add)
+        same_asset(1)
+        act(A("VG"), IND(V, cf), Fn.Copy)
+        act(A("YA"), IND(Y, ab), Fn.Copy)
+        act(A("YB"), IND(Y, ba), Fn.Copy)
+        for j, (l_, r_) in enumerate((("IDB", "VG"), ("NIB", "YA"), ("IDB", "YB"))):
+            mm(A("PP", 0, 64), A(l_), A(r_), j == 0, j == 2)
+        together(3)
+        act(A("U"), A("PP", 0, 64), Fn.Copy)
+        scan(A("CF", 0, 192), A("KC", 0, 192), A("EQ", 0, 192), 0.0, Op.add, Op.max)
+        if not last:
+            tt(A("DA"), A("E1", 0, 64), MKS, Op.mult)
+        for hs in (1, 0):
+            a_, b_ = 192 + 64 * hs, 256 + 128 * hs
+            scan(A("CF", a_, b_), A("KC", a_, b_), A("EQ", a_, b_), A("CF", b_ - 193, b_ - 192), Op.add, Op.max)
+        if not last:
+            tt(A("NA"), IND(WA, cf), A("DA"), Op.add)
+        for hs in (1, 0):
+            for ty in (0, 1):
+                x, y = 2 * ty + hs, 255 + 128 * hs
+                z = 47 + 16 * hs if ty else x + 6
+                ts2(A("LO", x, x + 7, 6), A("LF", x, z + 1, z - x), A("CF", y, y + 1), col(7 + x), Op.add, Op.min)
         for t in (0, 1):
-            mm(A("PF", 256 + 128 * t, 384 + 128 * t, 1, 8), A(hn, 8 * t, 8 * t + 8), A("IDF"))
+            mm(A("PF", 256 + 128 * t, 384 + 128 * t, 1, 8), fld(hx, t, 0), A("IDB"))
+        together(2)
         act(A("HO", 256 * st, 256 * st + 256, 1, 8), A("PF", 256, 512, 1, 8), Fn.Identity, bias=float(MID))
         if not last:
-            costs_in(st + 1)
-            tt(A("AN"), IND(WA, cf), A("NK"), Op.mult)
-        scan(A("CF"), A("KC"), A("EQ"), 0.0, Op.add, Op.max)
-        if not last:
-            tt(A("NA"), A("AN"), A("AM"), Op.add)
-        for ty in (0, 1):
-            for hs in (0, 1):
-                x, y = 2 * ty + hs, 127 + 256 * hs
-                ts2(A("LO", x, x + 7, 6), A("LF", x, x + 7, 6), A("CF", y, y + 1), col(7 + x), Op.add, Op.min)
-        if not last:
+            tt(A("DO"), A("E1", 64, 128), MKS, Op.mult)
             cp(IND(WA, A("LO", 0, 4)), A("NA"))
         else:
             store("s", T.ho[:, :], A("HO", 0, 768, 1, 8), "sh")
-            update_v()
+            write_v()
             store("y", T.vo[:, :], A("V", 0, C), "so")
     for i in schedule(ops):
         ops[i][5]()

@@ -8,39 +8,41 @@ OFF = 5376
 MAG = 1.5 * 2.0 ** 35
 BIG = 1.0e9
 W1, W2 = 65536, 131072
-J2V = (96, 208)
-REP_V = 32
+J2V = (96, 212)
+REP_G = (160, 128, 128)
+HI_S = 2
 NB = 3
 
 f32, bf, i32, u16, h16 = "float32", "bfloat16", "int32", "uint16", "float16"
 SB = {
     "WA": (WD, i32), "WO": (WD, i32), "Y": (WD, bf), "V": (WD, bf), "HD": (16, i32), "HDF": (16, f32), "Z": (256, bf),
     "ZR0": (2560, bf), "ZR1": (2560, bf), "ZR2": (2560, bf), "M1": (4096, bf), "M2": (4096, bf), "GS": (512 * NB, bf),
-    "ZT0": (128, bf), "ZT1": (128, bf), "ZT2": (128, bf), "SP0": (1024, bf), "SP1": (512, bf), "KR": (1024, bf), "VR": (16 * (J2V[1] - J2V[0]), bf),
-    "HL0": (16, u16), "HL1": (16, u16), "HL2": (16, u16), "FT0": (256, h16), "FT1": (256, h16), "FT2": (256, h16),
-    "HS0": (16, u16), "HS1": (16, u16), "HX0": (256, h16), "HX1": (256, h16), "HX2": (256, h16), "HO": (768, f32),
-    "CA": (256, u16), "CO": (256, u16), "PL1": (256, h16), "PL2": (256, h16), "EE": (512, f32), "E2": (272, f32),
+    "ZT0": (128, bf), "ZT1": (128, bf), "ZT2": (128, bf), "SP0": (512, bf), "SP1": (512, bf), "KR": (512, bf), "VR": (16 * (J2V[1] - J2V[0]), bf),
+    "HL0": (16, u16), "HL1": (16, u16), "HL2": (16, u16), "FT0": (520, h16), "FT1": (520, h16), "FT2": (520, h16),
+    "HS0": (16, u16), "HS1": (16, u16), "HO": (768, f32),
+    "CA": (256, u16), "CO": (256, u16), "PL1": (256, h16), "PL2": (256, h16), "EE": (512, f32), "E2": (512, f32),
     "HI2": (32, f32), "HK": (16, f32), "KI": (16, i32), "XH": (256, h16), "AL": (16, u16), "LS": (256, f32),
-    "VCS": (256, bf), "VCT": (256, bf), "SPF": (512, bf), "FB": (512, bf), "JK": (256, bf), "ACC": (4, f32), "PRE": (2, f32),
-    "DL": (4, u16), "FL": (264, f32), "FC": (64, f32), "KB": (64, bf), "TR": (64, f32), "LU": (16, u16), "LF": (64, f32), "LN": (16, f32), "LO": (16, u16),
+    "VCS": (256, bf), "VCT": (256, bf), "FB": (512, bf), "JK": (256, bf), "ACC": (6, f32), "PRE": (2, f32),
+    "DL": (4, u16), "FL": (264, f32), "FC": (64, f32), "KB": (64, bf), "TR": (64, f32), "LU": (16, u16), "LF": (64, f32), "LO": (16, u16),
     "MK": (96, f32), "AM": (64, f32), "DA": (64, f32), "NA": (64, i32), "DO": (64, f32), "NO": (64, i32),
-    "EQ": (384, bf), "CF": (384, f32), "YA": (64, bf), "YB": (64, bf), "VG": (64, bf), "U": (64, bf),
-    "IO": (256, bf), "IO8": (64, bf), "IOG": (128, bf), "IOC": (192, bf), "IO17": (136, bf), "PI": (8, i32), "CC": (48, f32), "CI": (128, i32), "CL": (144, u16),
-    "ONB": (1024, bf), "IDB": (128, bf), "NIB": (128, bf), "GB": (8, bf), "GI": (16, bf), "NGI": (16, bf), "GJ": (8, bf),
-    "RM": (256, bf), "RN": (1024, bf), "K16": (256, bf), "K17": (136, bf), "KL": (64, f32), "TRI": (256, bf), "NTR": (256, bf), "EXP": (512, bf),
-    "CK": (256, bf), "CK17": (136, bf), "I17": (136, bf), "I0": (136, bf), "CND": (48, bf),
-    "BO": (128, f32), "SEL": (640, f32), "SELK": (128, bf), "CAB": (320, bf), "KH": (32, f32), "KC": (384, bf),
+    "EQ": (192, bf), "CF": (192, f32), "YA": (64, bf), "YB": (64, bf), "VG": (64, bf), "U": (64, bf),
+    "IO": (256, bf), "IO8": (64, bf), "IOC": (192, bf), "PI": (8, i32), "CC": (48, f32), "CI": (64, i32), "CL": (144, u16),
+    "ONB": (520, bf), "IDB": (128, bf), "NIB": (128, bf), "GB": (16, bf), "GI": (16, bf), "NGI": (16, bf), "GJ": (8, bf),
+    "RM": (256, bf), "RN": (1024, bf), "K16": (256, bf), "KL": (64, f32), "TRI": (128, bf), "NTR": (256, bf), "EXP": (512, bf),
+    "CK": (256, bf), "CK2": (144, bf), "CND": (32, bf),
+    "BO": (128, f32), "SEL": (640, f32), "SELK": (128, bf), "CAB": (320, bf), "KH": (32, f32), "KC": (192, bf), "CM": (96, bf),
 }
 PS = ["D0", "D1", "D2", "E0", "E1", "LL", "PP", "PF"]
 SCRATCH = {k: ("sbuf", [128, w], d) for k, (w, d) in SB.items()}
 SCRATCH.update({k: ("psum", [128, 512], f32) for k in PS})
-AO = [0, 1024, 1920, 2560]
+AO = [0, 1536, 2560]
 NAO = len(AO) - 1
-SEMAPHORES = ["qg", "qv", "qs", "qp", "lh", "lz", "ly", "lv", "so", "sh", "z1", "z2", "t1", "t2", "hl10", "hl11", "hl20", "hl21", "hc1", "hc2", "sent", "la0", "la1", "la2"]
-COSTS = [dict(pe=0.48, el=0.95, ga=1.5, sc=3.6, by=0.004, lat=1700, far=1200, wake=120),
-         dict(pe=0.6, el=1.15, ga=2.1, sc=5.0, by=0.005, lat=2200, far=2000, wake=120),
-         dict(pe=0.45, el=0.9, ga=1.1, sc=2.5, by=0.003, lat=2000, far=2800, wake=160)]
-ROUNDS, SEED, DRIFT, FREE = 40000, 1, 0.0005, 20
+SEMAPHORES = ["qg", "qv", "qs", "qp", "lh", "lz", "ly", "lv", "so", "sh", "z1", "z2", "t1", "t2", "hl10", "hl11", "hl20", "hl21", "hc10", "hc11", "hc20", "hc21", "sent", "la0", "la1"]
+COSTS = [dict(pe=0.44, el=0.85, ga=1.33, sc=3.2, by=0.003, lat=1600, far=2500, first=4000, wake=150),
+         dict(pe=0.6, el=1.2, ga=2.2, sc=5.0, by=0.004, lat=2000, far=3000, first=5000, wake=120),
+         dict(pe=0.5, el=0.95, ga=1.5, sc=3.6, by=0.0025, lat=1400, far=2500, first=4000, wake=100),
+         dict(pe=0.45, el=0.88, ga=1.0, sc=2.3, by=0.003, lat=1500, far=3000, first=3000, wake=140)]
+ROUNDS, SEED, DRIFT, FREE, EARLY = 200000, 1, 0.002, 30, 0.2
 PLAN = {}
 
 
@@ -84,6 +86,8 @@ def schedule(ops):
         for aps, w_ in ((wr, True), (rd, False)):
             for x in aps:
                 for y, yw, yq, j in seen.get(x[1], []):
+                    if q == yq == "p" and (x[6] + x[5] <= y[6] or y[6] + y[5] <= x[6]):
+                        continue
                     if (x[1] in PS and (yq != q or q == "p")) or ((w_ or yw) and meet(x, y, yq == q)):
                         d.add(j)
         for aps, w_ in ((wr, True), (rd, False)):
@@ -94,8 +98,8 @@ def schedule(ops):
             if not mask >> j & 1:
                 keep.append(j)
                 mask |= anc[j] | 1 << j
-        if lat:
-            for j in [j for j in range(i) if ops[j][0] == q and ops[j][4]][-1:]:
+        if lat or q == "g":
+            for j in [j for j in range(i) if ops[j][0] == q and (ops[j][4] or q == "g")][-1:]:
                 if j not in keep:
                     keep.append(j)
                     soft.add((j, i))
@@ -166,8 +170,30 @@ def schedule(ops):
 
     seq = first_order(0)
     norm = [finish(seq, k) for k in range(len(sets))]
-    score = lambda s_: sum(finish(s_, k) / norm[k] for k in range(len(sets)))
-    cur = score(seq)
+    ends = [[0.0] * m for _ in sets]
+
+    def score(s_, lo):
+        head, out, total = {}, [], 0.0
+        for i in reversed(s_[:lo]):
+            head.setdefault(qs[i], i)
+            if len(head) == 5:
+                break
+        for k, (busy, lat, edge) in enumerate(sets):
+            end = ends[k][:]
+            free = [end[head[q]] if q in head else 0.0 for q in range(5)]
+            for i in s_[lo:]:
+                q = qs[i]
+                t = free[q]
+                for j, e in edge[i]:
+                    e += end[j]
+                    if e > t:
+                        t = e
+                end[i] = free[q] = t + busy[i]
+            out.append(end)
+            total += (end[m - 1] + lat[m - 1] + EARLY * sum(end) / m) / norm[k]
+        return total, out
+
+    cur, ends[:] = score(seq, 0)
     paths = [finish(seq, k, True) for k in range(len(sets))]
     for it in range(ROUNDS):
         path = paths[rnd(len(paths))]
@@ -182,18 +208,23 @@ def schedule(ops):
         if qs[i] == 4 or qs[j] == 4 or anc[i] >> j & 1:
             continue
         pi_, pj = seq.index(i), seq.index(j)
+        if pi_ < pj:
+            continue
         if rnd(2):
             lo = max(0, pj - (rnd(12) if rnd(2) else 0))
             part = seq[lo:pi_]
             new = seq[:lo] + [x for x in part if anc[i] >> x & 1] + [i] + [x for x in part if not anc[i] >> x & 1] + seq[pi_ + 1:]
         else:
-            hi = min(m, pi_ + 1 + (rnd(12) if rnd(2) else 0))
+            lo, hi = pj, min(m, pi_ + 1 + (rnd(12) if rnd(2) else 0))
             part = seq[pj + 1:hi]
             new = seq[:pj] + [x for x in part if not anc[x] >> j & 1] + [j] + [x for x in part if anc[x] >> j & 1] + seq[hi:]
-        sc_ = score(new)
+        sc_, out = score(new, lo)
         if sc_ <= cur + DRIFT * (1 - it / ROUNDS):
+            if sc_ != cur:
+                k = rnd(len(sets))
+                paths[k] = finish(new, k, True)
             seq, cur = new, sc_
-            paths = [finish(seq, k, True) for k in range(len(sets))]
+            ends[:] = out
     PLAN["order"], PLAN["est"] = seq, [finish(seq, k) for k in range(len(sets))] + norm
     return seq
 
@@ -323,12 +354,14 @@ def rank_program(g, core, T, topo):
             token("g", "sent", len(topo.engines(core, dst)))
             count[sem] = len(topo.engines(src, core))
             note("x", [o], [], (sem, count[sem], {}))
-        ops.append(("g", [o], [i] + list(after), ("el", 3000 if sem == "t1" else 700, 0), width(i) * size(i) * 128, emit))
+        ops.append(("g", [o], [i] + list(after), ("first", 700, sem == "t1"), width(i) * size(i) * 128, emit))
 
     WA, WO, Y, V = A("WA"), A("WO"), A("Y"), A("V")
     BC0, PAR = (lambda a, b: A("CL", a, b)), A("CL", 128, 129)
     tl = lambda name, t: A(name, 128 * t, 128 * t + 128)
-    fld = lambda name, t, j: A(name, 128 * t + j, 128 * t + 128, 16)
+    LT = lambda b_, t, s_=1, j=0: A(b_, 128 + 128 * t + j, 256 + 128 * t, s_)
+    EQL = lambda b_, t, s_=1, j=0: A(b_, 384 * t + j, 384 * t + 128, s_)
+    fld = lambda name, t, j: LT(name, t, 16, j)
     ONE = A("ONB", 0, 128)
     SEL = lambda j: A("SEL", 128 * j, 128 * j + 128)
 
@@ -339,121 +372,114 @@ def rank_program(g, core, T, topo):
     load("y", A("Y", 0, C), T.yd[:, :], "ly")
     load("y", A("V", 0, C), T.ve[:, :], "lv", [A("WO", AO[NAO - 2], AO[NAO - 1])])
 
-    iota(A("CI"), [[1, 128]], 0, 0)
     iota(A("PI", 0, 1), [[0, 1]], 0, 1)
     ms(A("ONB"), 1.0)
+    asel(A("IDB"), ONE, [[-1, 128]], Op.is_equal, 0.0, 0, 1)
+    iota(A("CI"), [[1, 64]], 0, 0)
+    iota(A("IO8"), [[0, 8], [1, 8]], 0, 0)
+    iota(A("IOC"), [[1, 192]], 0, 0)
+    iota(A("IO"), [[0, 16], [1, 16]], 0, 0)
     ms(A("KR"), 1.0)
     ms(A("SP0"), 0.0)
-    ms(A("KR", 0, 1024, 16), 0.0)
-    cp(A("CL", 0, 128), A("CI"))
+    ms(A("SP1"), 0.0)
+    ms(A("KR", 0, 512, 16), 0.0)
     ts1(A("PI", 1, 2), A("PI", 0, 1), 15, Op.bitwise_and)
     ts2(A("PI", 2, 3), A("PI", 0, 1), 4, 1, Op.arith_shift_right, Op.bitwise_and)
     ts1(A("PI", 3, 4), A("PI", 0, 1), 1, Op.bitwise_and)
     ts1(A("PI", 4, 5), A("PI", 0, 1), 4, Op.arith_shift_right)
     ts1(A("PI", 5, 6), A("PI", 0, 1), 31, Op.bitwise_and)
-    ms(A("SP1"), 0.0)
+    ts1(col(36), A("PI", 0, 1), float(J2V[0]), Op.is_lt)
+    ts1(col(37), A("PI", 0, 1), float(J2V[1] - 128), Op.is_ge)
     cp(A("CC", 0, 5), A("PI", 1, 6))
-    asel(A("IDB"), ONE, [[-1, 128]], Op.is_equal, 0.0, 0, 1)
-    iota(A("IO8"), [[0, 8], [1, 8]], 0, 0)
-    iota(A("IO"), [[0, 16], [1, 16]], 0, 0)
-    iota(A("IOC"), [[1, 192]], 0, 0)
-    ts1(A("GB"), A("IO8", 0, 8), col(3), Op.is_equal)
-    act(A("CK"), A("IO"), Fn.Identity, scale=-32.0, bias=480.0)
-    act(A("K16"), A("KR", 0, 256), Fn.Identity, scale=BIG, bias=-BIG)
-    act(A("ZR0", 1536, 2560), IND(A("Z", 192, 256), BC0(0, 64)), Fn.Copy)
-    for j, w_ in ((0, 64), (1, 32)):
-        sp = "SP%d" % j
-        cp(A(sp, 0, 16 * w_, 16), A("Z", 64 * j, 64 * j + w_))
-        scan(A("ZR0", 1024 * j, 1024 * j + 16 * w_), A("KR", 0, 16 * w_), A(sp, 0, 16 * w_), 0.0, Op.mult, Op.add)
-    mm(A("PP", 0, 128, 1, 64, 0), A("Z", 128, 192), A("IDB"))
-    mm(A("PP", 0, 128, 1, 64, 64), A("Z", 64, 128), A("IDB"))
-    act(A("ZT0"), A("PP", 0, 128), Fn.Copy)
-    send(1, A("ZT1"), A("ZT0"), "t1")
-    send(2, A("ZT2"), A("ZT0"), "t2")
-    cp(A("HL0"), A("HD"))
-    ts1(A("HDF"), A("HD"), -float(MID), Op.add)
+    cp(A("CL", 0, 64), A("CI"))
     ms(A("WA", C, WD), NONE)
     ms(A("WO", C, WD), 0)
     ms(A("Y", C, WD), 0.0)
     ms(A("V", C, WD), 0.0)
-    for j in (0, 8):
-        act(A("GI", j, j + 8), A("GB"), Fn.Copy, scale=float(W1))
-    act(A("NGI"), A("GI"), Fn.Copy, scale=-1.0)
-    act(A("GJ"), A("GB"), Fn.Copy, scale=float(W2))
+    ts1(A("FT0"), A("ONB"), 0.0, Op.mult)
+    ts1(A("GB"), A("IO8", 0, 16), col(3), Op.is_equal)
     act(A("NIB"), A("IDB"), Fn.Copy, scale=-1.0)
-    unpack = lambda j: ts1(A("WA", AO[j], AO[j + 1]), A("WO", AO[j], AO[j + 1]), 4095, Op.bitwise_and)
-    ts1(A("RM"), A("IO"), col(0), Op.is_equal)
-    ts1(A("SP1", 0, 512, 16), A("IOC", 0, 32), col(4), Op.is_equal)
-    scan(A("EXP"), A("KR", 0, 512), A("SP1"), 0.0, Op.mult, Op.add)
-    for b_ in ("FT0", "HX0", "HX1"):
-        ts1(A(b_), A("ONB", 0, 256), 0.0, Op.mult)
-    unpack(0)
-    tt(A("XH"), IND(A("HDF"), BC0(0, 16)), A("RM"), Op.mult)
-    for t in (0, 1):
-        mm(A("PF", 256 + 8 * t, 264 + 8 * t), tl("XH", t), A("GB"))
-    cp(A("FT0", 0, 256, 16), A("PF", 256, 272))
-    ms(A("SPF"), 0.0)
-    if NAO > 2:
-        unpack(1)
-    for j, (x_, a_, b_) in {5: (0, -1, -0.5), 6: (0, -1, -16.5), 7: (0, 1, C), 8: (0, 1, C + 16), 9: (0, 1, C + 32), 10: (0, 1, C + 48),
-                            15: (0, -1 / 16, 15 / 16), 16: (0, 4, 0), 17: (0, 4, 128), 19: (3, -4096, 7 * 4096 - MID),
-                            22: (0, 3072, -OFF - 15 * 3072)}.items():
-        act(col(j), col(x_), Fn.Identity, scale=float(a_), bias=float(b_))
-    act(A("CC", 20, 22), A("ONB", 0, 2), Fn.Copy, scale=-0.5)
-    act(A("CAB", 0, 64), A("ONB", 0, 64), Fn.Copy, scale=(MID - OFF) / 128.0)
-    act(A("CAB", 64, 192, 2), A("ONB", 0, 64), Fn.Copy, scale=float(MID - OFF))
-    act(A("CAB", 65, 128, 2), A("ONB", 0, 32), Fn.Copy, scale=-float(OFF))
-    act(A("CAB", 129, 192, 2), A("ONB", 0, 32), Fn.Copy, scale=col(22))
-    act(A("CAB", 192, 256), A("ONB", 0, 64), Fn.Copy, scale=-MID / 128.0)
-    act(A("CAB", 256, 320), A("ONB", 0, 64), Fn.Copy, scale=0.0)
-    asel(A("RN"), A("ONB"), [[-16, 8], [0, 8], [-1, 16]], Op.is_equal, 0.0, 0, 1)
-    iota(A("IOG"), [[1, 8], [0, 16]], 0, 0)
-    iota(A("IO17"), [[0, 8], [1, 17]], 0, 0)
-    ts1(A("BO"), A("IOG"), col(3), Op.is_equal)
-    ts1(A("I0"), A("IO17"), 16.0, Op.is_lt)
-    act(A("CK17"), A("IO17"), Fn.Identity, scale=-32.0, bias=480.0)
-    asel(A("I17"), A("I0"), [[-16, 8], [-1, 17]], Op.is_equal, 0.0, 0, 1)
-    ts1(col(36), A("PI", 0, 1), float(J2V[0]), Op.is_lt)
-    ts1(col(37), A("PI", 0, 1), float(J2V[1] - 128), Op.is_ge)
-    asel(A("TRI", 0, 128), ONE, [[1, 128]], Op.is_ge, 0.0, 0, -1)
-    act(A("TRI", 128, 256), ONE, Fn.Copy)
-    ts2(A("KL"), A("IO8"), col(3), -BIG, Op.is_equal, Op.mult)
-    for j in range(4):
-        ts1(col(27 + j), col(0), float(j), Op.is_equal)
-    unpack(NAO - 1)
-    act(A("KL"), A("KL"), Fn.Identity, bias=4096.0)
-    act(A("NTR"), A("TRI"), Fn.Copy, scale=-1.0)
-    act(col(31), col(29), Fn.Copy, scale=-1.0)
-    act(col(33), col(27), Fn.Copy, scale=-4096.0)
-    act(col(32), col(28), Fn.Identity, scale=4096.0, bias=col(33))
+    act(A("K16"), A("KR", 0, 256), Fn.Identity, scale=BIG, bias=-BIG)
+    act(A("NTR", 128, 256), ONE, Fn.Copy, scale=-1.0)
     act(A("CC", 11, 13), A("CC", 36, 38), Fn.Identity, scale=-5.75 * W2, bias=10.75 * W2)
     act(A("CC", 13, 15), A("CC", 36, 38), Fn.Copy, scale=-16.0 * W2)
+    mm(A("PP", 0, 128, 1, 64, 0), A("Z", 128, 192), A("IDB"))
+    mm(A("PP", 0, 128, 1, 64, 64), A("Z", 64, 128), A("IDB"))
+    act(A("ZT0"), A("PP", 0, 128), Fn.Copy)
+    send(1, A("ZT1"), A("ZT0"), "t1")
+    act(A("ZR0", 1536, 2560), IND(A("Z", 192, 256), BC0(0, 64)), Fn.Copy)
+
+    def repeat_costs(j):
+        sp = "SP%d" % (j % 2)
+        cp(A(sp, 0, 512, 16), A("Z", 32 * j, 32 * j + 32))
+        scan(A("ZR0", 512 * j, 512 * j + 512), A("KR"), A(sp), 0.0, Op.mult, Op.add)
+
+    repeat_costs(0)
+    cp(A("HL0"), A("HD"))
+    ts1(A("HDF"), A("HD"), -float(MID), Op.add)
+    repeat_costs(1)
+    unpack = lambda j: ts1(A("WA", AO[j], AO[j + 1]), A("WO", AO[j], AO[j + 1]), 4095, Op.bitwise_and)
+    ts1(A("SP1", 0, 512, 16), A("IOC", 0, 32), col(4), Op.is_equal)
+    repeat_costs(2)
+    scan(A("EXP"), A("KR"), A("SP1"), 0.0, Op.mult, Op.add)
+    unpack(0)
+    ts1(A("RM"), A("IO"), col(0), Op.is_equal)
+    ts2(A("KL"), A("IO8"), col(3), -BIG, Op.is_equal, Op.mult)
+    for x in (0, 384):
+        ts1(A("FT1", x, x + 136 - 8 * (x == 0)), A("ONB", 0, 136 - 8 * (x == 0)), 0.0, Op.mult)
+    tt(A("XH"), IND(A("HDF"), BC0(0, 16)), A("RM"), Op.mult)
     for t in (0, 1):
-        act(A("CND", 8 * t, 8 * t + 8), A("ONB", 0, 8), Fn.Copy, scale=col(11 + t))
-        act(A("CND", 16 + 8 * t, 24 + 8 * t), A("ONB", 0, 8), Fn.Copy, scale=col(13 + t))
-    act(A("CND", 32, 48), A("ONB", 0, 16), Fn.Copy, scale=15 * 4096.0)
-    for j, x_ in enumerate((27, 28, 29, 31, 32)):
-        act(SEL(j), A("BO"), Fn.Copy, scale=col(x_))
-    act(A("SELK"), A("BO"), Fn.Copy, scale=col(30))
+        mm(A("PF", 256 + 8 * t, 264 + 8 * t), tl("XH", t), A("GB", 0, 8))
+    for j in range(8):
+        ts1(tl("RN", j), A("RM", 0, 128), A("GB", j, j + 1), Op.mult)
+    act(A("GI"), A("GB"), Fn.Copy, scale=float(W1))
+    act(A("NGI"), A("GB"), Fn.Copy, scale=-float(W1))
+    act(A("GJ"), A("GB", 0, 8), Fn.Copy, scale=float(W2))
+    act(A("CK"), A("IO"), Fn.Identity, scale=-32.0, bias=480.0)
+    act(A("CK2"), A("IO", 0, 144), Fn.Identity, scale=-32.0, bias=480.0)
+    act(A("CK2", 128, 136), A("ONB", 0, 8), Fn.Copy, scale=0.0)
+    act(A("CK2", 136, 144), A("ONB", 0, 8), Fn.Copy, scale=480.0)
+    act(A("KL"), A("KL"), Fn.Identity, bias=4096.0)
+    act(A("KH"), A("RM", 0, 32), Fn.Identity, scale=-BIG, bias=3072.0)
+    for t in (0, 1):
+        act(A("CND", 16 * t, 16 * t + 8), A("ONB", 0, 8), Fn.Copy, scale=col(11 + t))
+        act(A("CND", 16 * t + 8, 16 * t + 16), A("ONB", 0, 8), Fn.Copy, scale=col(13 + t))
+    for j, (x_, a_, b_) in {19: (3, -4096, 7 * 4096 - MID), 5: (0, -1, -0.5), 6: (0, -1, -16.5), 23: (0, 1, C), 15: (0, -1 / 16, 15 / 16),
+                            16: (0, 4, 0), 17: (0, 4, 128), 22: (0, 3072, -OFF - 15 * 3072),
+                            24: (0, -2, 0.5), 25: (0, -2, -31.5)}.items():
+        act(col(j), col(x_), Fn.Identity, scale=float(a_), bias=float(b_))
+    act(A("CC", 7, 11), A("IOC", 0, 64, 16), Fn.Identity, bias=col(23))
+    act(A("CAB", 129, 192, 2), A("ONB", 0, 32), Fn.Copy, scale=col(22))
+    act(A("CC", 20, 22), A("ONB", 0, 2), Fn.Copy, scale=-0.5)
+    if NAO > 2:
+        unpack(1)
+    cp(A("FT0", 128, 384, 16), A("PF", 256, 272))
+    ts2(col(18), col(0), 6.0, col(2), Op.is_ge, Op.add)
+    ts2(A("FL", 256, 264), A("RM", 3, 131, 16), -float(NONE - MID), float(NONE - MID), Op.mult, Op.add)
+    ts2(col(34), col(0), 2.0, col(18), Op.is_ge, Op.add)
+    ts2(A("KC", 0, 64), A("IOC", 0, 64), col(16), float(OFF), Op.is_equal, Op.mult)
+    ts2(col(35), col(2), 31.0, col(34), Op.mult, Op.add)
+    ts2(A("KC", 64, 192), A("IOC", 64, 192), col(17), float(OFF), Op.is_equal, Op.mult)
+    ts2(PAR, col(1), 16.0, col(35), Op.mult, Op.add)
+    for hs in (0, 1):
+        act(A("CM", 32 * hs, 32 + 64 * hs), A("IOC", 0, 32 + 32 * hs), Fn.Sign, bias=col(24 + hs))
+    act(A("CM"), A("CM"), Fn.Copy, scale=float(OFF - MID))
+    cp(A("SP1", 0, 128, 16), A("GB", 0, 8))
+    unpack(NAO - 1)
+    scan(A("BO"), A("KR", 0, 128), A("SP1", 0, 128), 0.0, Op.mult, Op.add)
+    for x, y, s_, v in ((64, 192, 2, MID - OFF), (65, 128, 2, -OFF), (192, 256, 1, -MID / 128), (256, 320, 1, 0)):
+        act(A("CAB", x, y, s_), A("ONB", 0, (y - x + s_ - 1) // s_), Fn.Copy, scale=float(v))
 
     def late_constants():
-        ts2(A("K17"), A("IO17"), 0.0, -BIG, Op.is_equal, Op.mult)
-        ts2(col(18), col(0), 6.0, col(2), Op.is_ge, Op.add)
-        ts2(col(34), col(0), 2.0, col(18), Op.is_ge, Op.add)
-        ts2(col(35), col(2), 31.0, col(34), Op.mult, Op.add)
-        ts2(PAR, col(1), 16.0, col(35), Op.mult, Op.add)
-        ts2(A("FL", 256, 264), A("RM", 3, 131, 16), -float(NONE - MID), float(NONE - MID), Op.mult, Op.add)
-        ts2(A("KH"), A("IOC", 0, 32), col(0), -BIG, Op.is_equal, Op.mult)
-        ts2(A("KC", 0, 64), A("IOC", 0, 64), col(16), float(OFF), Op.is_equal, Op.mult)
-        ts2(A("KC", 64, 192), A("IOC", 64, 192), col(17), float(OFF), Op.is_equal, Op.mult)
-        cp(A("KH", 16, 32), A("KH", 0, 16))
-        cp(A("KC", 192, 384), A("KC", 0, 192))
-        ts1(A("KC", 192, 257, 64), A("KC", 0, 65, 64), -float(OFF), Op.add)
-        ms(A("KC", 64, 65), -16384.0)
-        act(A("KH"), A("KH"), Fn.Identity, bias=3072.0)
-
-    late_constants()
-    send(1, A("ZR1"), A("ZR0"), "z1", after=[V])
+        pick = lambda o, i, j, x=Op.is_equal, f=0.0: asel(o, i, [[-16, 8], [0, 16]], x, f, -j, 1)
+        asel(A("TRI"), ONE, [[1, 128]], Op.is_ge, 0.0, 0, -1)
+        asel(A("NTR", 0, 128), A("NTR", 128, 256), [[1, 128]], Op.is_ge, 0.0, 0, -1)
+        iota(SEL(4), [[0, 128]], 4096, 0)
+        pick(A("SELK"), ONE, 3)
+        pick(SEL(4), SEL(4), 1)
+        asel(A("SEL", 0, 384), A("ONB", 0, 384), [[-1, 3], [-16, 8], [0, 16]], Op.is_equal, 0.0, 0, 1)
+        pick(SEL(4), SEL(4), 0, Op.not_equal, -4096.0)
+        pick(SEL(3), A("NTR", 128, 256), 2)
 
     cf, ff, ab, ba, lb = A("LU", 0, 4), A("LU", 2, 6), A("LU", 6, 10), A("LU", 8, 12), A("LU", 8, 10)
     MKS = A("MK", 32, 96)
@@ -479,22 +505,24 @@ def rank_program(g, core, T, topo):
 
     def head_2(t, ft):
         e = "E%d" % t
-        mm(A(e, 0, 136), ONE, A("CK17"), True, False)
-        mm(A(e, 16, 136, 17), A("IDB"), A("CND", 8 * t, 8 * t + 8), False, False)
-        mm(A(e, 16, 136, 17), A("IDB"), fld(ft, t, 0), False, False)
-        mm(A(e, 0, 136), tl("PL2", t), A("I17"), False, False)
+        mm(A(e, 0, 144), ONE, A("CK2"), True, False)
+        mm(A(e, 128, 144), A("IDB"), A("CND", 16 * t, 16 * t + 16), False, False)
+        for x in (128, 136):
+            mm(A(e, x, x + 8), A("IDB"), fld(ft, t, 0), False, False)
         together(4)
+        mm(A(e, 0, 128), tl("PL2", t), A("IDB"), False, False)
 
     def reduce(a, b, m, gi):
-        t, (step, end) = a // 128, (16, 256) if m == "M1" else (17, 136)
-        for k in range(16):
-            mm(A("E%d" % t, k, end, step, b - a, a - 128 * t), A(m, 16 * a + k, 16 * b, 16), A(gi), False, k == 15)
-            if k % 4 == 3:
-                together(4)
+        t, end = a // 128, 256 if m == "M1" else 128
+        for x in range(a, b, 32):
+            for k in range(16):
+                mm(A("E%d" % t, k, end, 16, 32, x - 128 * t), A(m, 16 * x + k, 16 * x + 512, 16), A(gi), False, k == 15)
+                if k % 8 == 7:
+                    together(8)
 
-    def to_list(src, j, t, base, out):
+    def to_list(src, base, out):
         for x in range(8):
-            mm(A("LL", base + 8 * x, base + 8 * x + 8), A("RN", 128 * x, 128 * x + 128), fld(src, t, j))
+            mm(A("LL", base + 8 * x, base + 8 * x + 8), A("RN", 128 * x, 128 * x + 128), src)
         together(8)
         yield
         scan(A("LS", base, base + 64), A("KL"), A("LL", base, base + 64), 0.0, Op.add, Op.max)
@@ -506,40 +534,50 @@ def rank_program(g, core, T, topo):
         yield
         tt(fld(ft, t, 2), A("EE", 384 * t + 15, 384 * t + 128, 16), A("EE", 128 * t + 143, 128 * t + 256, 16), Op.subtract)
         al = A("AL", 8 * t, 8 * t + 8)
-        yield from to_list(ft, 2, t, 64 * t, al)
+        yield from to_list(fld(ft, t, 2), 64 * t, al)
         yield
-        ts2(tl("CO", t), IND(WO, al), 1.0 / 4096, -0.3125, Op.mult, Op.add)
+        for a, b in ((0, 2), (2, 8)) if t == 0 else ((8, 16),):
+            ts2(A("CO", 16 * a, 16 * b), IND(WO, A("AL", a, b)), 1.0 / 4096, -0.3125, Op.mult, Op.add)
         yield
         ts1(tl("PL2", t), tl("CO", t), -float(MID), Op.add)
 
-    LT, EQL = (lambda b_, t, s_=1: A(b_, 128 + 128 * t, 256 + 128 * t, s_)), (lambda b_, t, s_=1: A(b_, 384 * t, 384 * t + 128, s_))
 
     def verdict(t, st):
-        ft, hx, x = "FT%d" % st, "HX%d" % st, 136 * t
-        best, new = A("E2", x + 15, x + 136, 17), A("E2", x + 16, x + 136, 17)
-        h0, h1 = A("HI2", 16 * t, 16 * t + 8), A("HI2", 16 * t + 8, 16 * t + 16)
-        scan(A("E2", x, x + 136), A("K17"), A("E%d" % t, 0, 136), 0.0, Op.add, Op.max)
+        ft, e, hi = "FT%d" % st, "E%d" % t, A("HI2", 16 * t, 16 * t + 16)
+        best, both = LT("E2", t, 16, 15), A("E2", 256 * t + 15, 256 * t + 256, 16)
+        scan(LT("E2", t), A("K16", 0, 128), A(e, 0, 128), 0.0, Op.add, Op.max)
         yield
-        ts1(LT("SPF", t, 16), best, col(11 + t), Op.is_lt)
-        tt(EQL("SPF", t, 16), best, A("LL", 256 + 8 * t, 264 + 8 * t), Op.is_equal)
-        ts2(h0, best, MAG, MAG, Op.add, Op.subtract)
+        ts1(LT("SP1", t, 16), best, col(11 + t), Op.is_lt)
+        tt(EQL("SP1", t, 16), best, A(e, 136, 144), Op.is_equal)
+        tt(EQL("E2", t, 16, 15), best, A(e, 128, 136), Op.max)
         yield
-        scan(A("FB", 256 * t, 256 * t + 256), A("KR", 0, 256), A("SPF", 256 * t, 256 * t + 256), 0.0, Op.mult, Op.add)
-        tt(fld(ft, t, 1), best, h0, Op.subtract)
+        scan(A("FB", 256 * t, 256 * t + 256), A("KR", 0, 256), A("SP1", 256 * t, 256 * t + 256), 0.0, Op.mult, Op.add)
+        if t < HI_S:
+            ts2(hi, both, MAG, MAG, Op.add, Op.subtract)
+        else:
+            act(hi, both, Fn.Identity, bias=MAG)
+            act(hi, hi, Fn.Identity, bias=-MAG)
         yield
-        ts2(h1, new, MAG, MAG, Op.add, Op.subtract)
+        tt(A(ft, 256 * t + 1, 256 * t + 256, 16), both, hi, Op.subtract)
+        mm(tl("PF", t), LT(ft, t), A("IDB"))
         yield
-        tt(fld(hx, t, 0), new, h1, Op.subtract)
         if st < S - 1:
             hs_ = A("HS%d" % st, 8 * t, 8 * t + 8)
-            yield from to_list(hx, 0, t, 128 + 64 * t, hs_)
+            yield from to_list(EQL(ft, t, 16, 1), 128 + 64 * t, hs_)
             send(1, A("HL%d" % (st + 1), 8 * t, 8 * t + 8), hs_, "hl%d%d" % (st + 1, t))
+            for x in range(2 * t):
+                send(1, LT("FT%d" % (st + 1), x), A(ft, 384 * x + 1, 384 * x + 129), "hc%d%d" % (st + 1, x))
 
-    def repeat_g():
-        x, y = J2V[0] + REP_V, J2V[1]
+    def repeat_g(x):
+        y = J2V[1]
         for j in range(16):
-            asel(A("VR", 16 * REP_V + j, 16 * (y - J2V[0]), 16), A("VCS", x, y), [[0, y - x]], Op.is_ge, 0.0, 0, 0)
+            asel(A("VR", 16 * (x - J2V[0]) + j, 16 * (y - J2V[0]), 16), A("VCS", x, y), [[0, y - x]], Op.is_ge, 0.0, 0, 0)
         together(16)
+
+    def repeat_v(x):
+        act(A("SP0", 0, 512, 16), A("VCS", x, x + 32), Fn.Copy)
+        yield
+        scan(A("VR", 16 * (x - J2V[0]), 16 * (x + 32 - J2V[0])), A("KR"), A("SP0"), 0.0, Op.mult, Op.add)
 
     def least(zr, a, b):
         x = 16 * (a - 96 * (a >= 192))
@@ -557,20 +595,20 @@ def rank_program(g, core, T, topo):
         for hs in (0, 1):
             act(A("JK", 128 * hs, 128 * hs + 128), o, Fn.Sign, bias=col(5 + hs), accum_out=A("ACC", 2 * t + hs, 2 * t + hs + 1))
 
-    def same_citizen():
-        for hs in (0, 1):
-            for own in (0, 1):
-                x = 2 * own + hs
-                act(A("EQ", 64 * hs + own, 64 + 128 * hs, 2), A("D0", 0, 32 + 32 * hs), Fn.Abs, bias=A("LN", x, x + 1))
-        act(A("EQ", 0, 192), A("EQ", 0, 192), Fn.Relu, scale=-float(OFF), bias=float(OFF))
+    def same_citizen(hs):
+        j, w_ = 64 * hs, 32 + 32 * hs
+        for own in (0, 1):
+            x = 2 * own + hs
+            ts2(A("JK", j + own * w_, j + own * w_ + w_), A("D0", 32 * hs, 32 * hs + w_), A("LF", x, x + 1), float(OFF), Op.is_equal, Op.mult)
+        act(A("JK", j, j + 2 * w_), A("JK", j, j + 2 * w_), Fn.Copy, accum_out=A("ACC", 4 + hs, 5 + hs))
 
     def same_asset(own):
-        for hs in (0, 1):
-            j, x = 192 + 64 * hs, 47 + 16 * hs if own else 6 + hs
+        for hs in (1, 0):
+            j, x = 64 * hs, 47 + 16 * hs if own else 6 + hs
             ts2(A("EQ", j + own, j + 64 + 64 * hs, 2), A("D1", 0, 32 + 32 * hs), A("LF", x, x + 1), float(OFF), Op.is_equal, Op.mult)
 
     for st in range(S):
-        hl, ft, hx, zr, later, last = "HL%d" % st, "FT%d" % st, "HX%d" % st, "ZR%d" % st, st > 0, st == S - 1
+        hl, ft, zr, later, last = "HL%d" % st, "FT%d" % st, "ZR%d" % st, st > 0, st == S - 1
         ya, yb, yc = [s_job((A("ZT%d" % st, 0, 128, 1, 32, x % 128), A("EXP", 0, 512, 1, 32, x % 128)), Y, "CA", x, x + 32, "NIB", "M1", Fn.Relu)
                       for x in (96, 128, 160)]
         held = lambda x, y: (A("VCT", x // 128 * 128, x // 128 * 128 + 128, 1, 32, x % 128 // 32 * 32),
@@ -584,10 +622,15 @@ def rank_program(g, core, T, topo):
             write_v()
         cp(tl("CA", 1), IND(WA, A(hl, 8, 16)))
         least(zr, 0, 32)
+        if not later:
+            send(1, A("ZR1"), A("ZR0"), "z1", after=[V])
         act(tl("VCS", 1), IND(V, A(hl, 8, 16)), Fn.Copy)
-        repeat_g()
+        repeat_g(REP_G[st])
+        if not later:
+            late_constants()
         go(yb, 2)
-        ts1(A("PL1"), A("CA"), -float(MID), Op.add)
+        for t in (0, 1):
+            ts1(tl("PL1", t), tl("CA", t), -float(MID), Op.add)
         head_1(0)
         least(zr, 32, 64)
         go(ya)
@@ -611,7 +654,8 @@ def rank_program(g, core, T, topo):
         if later:
             cp(IND(WO, A("LO", 6, 10)), A("NO"))
         go(yc)
-        act(A("SP0", 0, 16 * REP_V, 16), IND(V, A(hl, J2V[0] // 16, (J2V[0] + REP_V) // 16)), Fn.Copy)
+        rep = repeat_v(J2V[0])
+        go(rep)
         go(own0, 3)
         reduce(128, 192, "M1", "NGI")
         go(va)
@@ -624,16 +668,14 @@ def rank_program(g, core, T, topo):
         reduce(224, 256, "M1", "GI")
         go(vb)
         head_2(0, ft)
-        scan(A("VR", 0, 16 * REP_V), A("KR", 0, 16 * REP_V), A("SP0", 0, 16 * REP_V), 0.0, Op.mult, Op.add)
+        go(rep)
+        for x in range(128, REP_G[st], 32):
+            go(repeat_v(x), 2)
         go(va)
         go(own1, 2)
         go(vc, 2)
         compare(96, 112)
         go(own1, 2)
-        mm(A("LL", 256, 272), A("IDB"), A(ft, 0, 256, 16), True, False)
-        mm(A("LL", 256, 272), A("IDB"), A("CND", 16, 32), False, False)
-        mm(A("LL", 256, 272), A("IDB"), A("CND", 32, 48), False, True)
-        together(3)
         go(vb)
         reduce(0, 64, "M2", "GJ")
         go(own1)
@@ -649,7 +691,7 @@ def rank_program(g, core, T, topo):
         ts1(A("KI"), A("HK"), -0.47, Op.add)
         go(vf, 2)
         go(ver0)
-        tt(A(ft, 3, 256, 16), A("HK"), A("KI"), Op.subtract)
+        tt(A(ft, 131, 384, 16), A("HK"), A("KI"), Op.subtract)
         go(ver0)
         go(vd)
         compare(160, 192)
@@ -661,12 +703,11 @@ def rank_program(g, core, T, topo):
         go(ver0)
         compare(192, J2V[1])
         reduce(192, 224, "M2", "GJ")
-        mm(tl("PF", 0), tl(ft, 0), A("IDB"))
         go(pre0)
         act(A("FL", 0, 128), tl("PF", 0), Fn.Copy)
         act(A("PRE"), A("ACC", 0, 2), Fn.Identity, scale=-0.5, bias=128.0)
         go(ver0)
-        mm(tl("PP", 1), LT("FB", 0), A("TRI", 128, 256), True, False)
+        mm(tl("PP", 1), LT("FB", 0), ONE, True, False)
         mm(tl("PP", 1), EQL("FB", 0), A("NTR", 128, 256), False, False)
         together(2)
         go(ver1)
@@ -675,11 +716,11 @@ def rank_program(g, core, T, topo):
         go(ver0)
         go(ver1)
         go(pre1)
-        mm(tl("PF", 1), tl(ft, 1), A("IDB"))
+        go(ver1)
         go(pre1)
         act(A("FL", 128, 256), tl("PF", 1), Fn.Copy)
-        go(ver1, 2)
-        mm(A("D0", 0, 64), ONE, A("CAB", 0, 64), True, False)
+        go(ver1)
+        mm(A("D0", 0, 96), A("IDB"), A("CM"), True, False)
         mm(A("D1", 0, 128), A("IDB"), A("CAB", 64, 192), True, False)
         if not last:
             mm(A("E1", 0, 128), ONE, A("CAB", 192, 320), True, False)
@@ -689,66 +730,63 @@ def rank_program(g, core, T, topo):
         go(ver1)
         cp(A("FC"), IND(A("FL"), A("DL")))
         act(A("KB"), IND(A("FL"), A("DL")), Fn.Copy)
-        if not last:
-            send(1, A("FT%d" % (st + 1)), A(hx), "hc%d" % (st + 1))
-            if st == 0:
-                send(2, A("ZR2"), A("ZR0"), "z2")
+        if st == 0:
+            send(2, A("ZT2"), A("ZT0"), "t2")
+            send(2, A("ZR2"), A("ZR0"), "z2")
         FH = A("FC", 16, 48)
-        mm(A("D0", 0, 64, 2), SEL(0), FH, False, False)
+        mm(A("D0", 0, 96, 2), SEL(0), A("FC", 0, 48), False, False)
         for j in (0, 1):
             mm(A("E0", 32 * j, 32 * j + 32), A("SELK"), A("KB", 16, 48))
         together(2)
         op("v", 1, ve.transpose, A("TR"), A("FC"))
-        mm(A("D0", 1, 64, 2), SEL(1), FH, False, True)
+        mm(A("D0", 1, 96, 2), SEL(1), A("FC", 0, 48), False, True)
         mm(A("D1", 0, 64, 2), SEL(2), FH, False, False)
-        together(2)
         ts1(A("LU"), IND(A("TR"), PAR), float(MID), Op.add)
-        act(A("LN"), IND(A("TR"), PAR), Fn.Identity, scale=-1.0, bias=float(OFF - MID))
+        act(A("LF", 0, 16), IND(A("TR"), PAR), Fn.Identity, bias=float(MID - OFF))
         ts1(A("MK", 0, 64), A("E0", 0, 64), col(15), Op.is_equal)
-        act(A("LF", 0, 16), A("LN"), Fn.Copy, scale=-1.0)
         tt(A("AM"), IND(WA, ff), A("MK", 0, 64), Op.mult)
         mm(A("D1", 1, 128, 2), A("BO"), A("AM"), False, True)
-        same_citizen()
         if not last:
             act(A("MK", 64, 96), A("MK", 0, 32), Fn.Copy, scale=-1.0)
-            mm(A("E1", 0, 64), A("BO"), A("AM"), False, False)
+        same_citizen(1)
+        same_citizen(0)
+        act(A("VG"), IND(V, cf), Fn.Copy)
+        if not last:
             for j in (0, 1):
                 mm(A("E1", 32 * j, 32 * j + 32), SEL(3), FH, False, False)
-                mm(A("E1", 64 + 32 * j, 96 + 32 * j), SEL(4), FH, False, j == 1)
-            together(5)
+                mm(A("E1", 64 + 32 * j, 96 + 32 * j), SEL(4), FH, False, False)
+            mm(A("E1", 0, 64), A("BO"), A("AM"), False, True)
         scan(A("LF", 32, 64), A("KH"), A("D1", 65, 128, 2), 0.0, Op.add, Op.max)
         same_asset(0)
-        ts1(lb, A("LF", 47, 64, 16), float(OFF), Op.add)
         same_asset(1)
-        act(A("VG"), IND(V, cf), Fn.Copy)
+        ts1(lb, A("LF", 47, 64, 16), float(OFF), Op.add)
         act(A("YA"), IND(Y, ab), Fn.Copy)
         act(A("YB"), IND(Y, ba), Fn.Copy)
         for j, (l_, r_) in enumerate((("IDB", "VG"), ("NIB", "YA"), ("IDB", "YB"))):
             mm(A("PP", 0, 64), A(l_), A(r_), j == 0, j == 2)
         together(3)
         act(A("U"), A("PP", 0, 64), Fn.Copy)
-        scan(A("CF", 0, 192), A("KC", 0, 192), A("EQ", 0, 192), 0.0, Op.add, Op.max)
         if not last:
             tt(A("DA"), A("E1", 0, 64), MKS, Op.mult)
         for hs in (1, 0):
-            a_, b_ = 192 + 64 * hs, 256 + 128 * hs
-            scan(A("CF", a_, b_), A("KC", a_, b_), A("EQ", a_, b_), A("CF", b_ - 193, b_ - 192), Op.add, Op.max)
+            a_, b_ = 64 * hs, 64 + 128 * hs
+            scan(A("CF", a_, b_), A("KC", a_, b_), A("EQ", a_, b_), A("ACC", 4 + hs, 5 + hs), Op.add, Op.max)
         if not last:
             tt(A("NA"), IND(WA, cf), A("DA"), Op.add)
         for hs in (1, 0):
             for ty in (0, 1):
-                x, y = 2 * ty + hs, 255 + 128 * hs
+                x, y = 2 * ty + hs, 63 + 128 * hs
                 z = 47 + 16 * hs if ty else x + 6
                 ts2(A("LO", x, x + 7, 6), A("LF", x, z + 1, z - x), A("CF", y, y + 1), col(7 + x), Op.add, Op.min)
         for t in (0, 1):
-            mm(A("PF", 256 + 128 * t, 384 + 128 * t, 1, 8), fld(hx, t, 0), A("IDB"))
+            mm(A("PF", 256 + 128 * t, 384 + 128 * t, 1, 8), EQL(ft, t, 16, 1), A("IDB"))
         together(2)
         act(A("HO", 256 * st, 256 * st + 256, 1, 8), A("PF", 256, 512, 1, 8), Fn.Identity, bias=float(MID))
         if not last:
-            tt(A("DO"), A("E1", 64, 128), MKS, Op.mult)
             cp(IND(WA, A("LO", 0, 4)), A("NA"))
+            tt(A("DO"), A("E1", 64, 128), MKS, Op.mult)
         else:
-            store("s", T.ho[:, :], A("HO", 0, 768, 1, 8), "sh")
+            store("y", T.ho[:, :], A("HO", 0, 768, 1, 8), "sh")
             write_v()
             store("y", T.vo[:, :], A("V", 0, C), "so")
     for i in schedule(ops):

from concourse.mybir import AluOpType as Op, ActivationFunctionType as Fn

C, D, S, HOP = 2560, 256, 3, 2
WD = 2640
NONE = 2624
MID = 1280
OFF = 5376
MAG = 1.5 * 2.0 ** 35
BIG = 1.0e9
W1, W2 = 65536, 131072
J2V = (96, 212)
REP_G = (160, 128, 128)
HI_S = 2
NB = 3

f32, bf, i32, u16, h16 = "float32", "bfloat16", "int32", "uint16", "float16"
SB = {
    "WA": (WD, i32), "WO": (WD, i32), "Y": (WD, bf), "V": (WD, bf), "HD": (16, i32), "HDF": (16, f32), "Z": (256, bf),
    "ZR0": (2560, bf), "ZR1": (2560, bf), "ZR2": (2560, bf), "M1": (4096, bf), "M2": (4096, bf), "GS": (512 * NB, bf),
    "ZT0": (128, bf), "ZT1": (128, bf), "ZT2": (128, bf), "SP0": (512, bf), "SP1": (512, bf), "KR": (512, bf), "VR": (16 * (J2V[1] - J2V[0]), bf),
    "HL0": (16, u16), "HL1": (16, u16), "HL2": (16, u16), "FT0": (520, h16), "FT1": (520, h16), "FT2": (520, h16),
    "HS0": (16, u16), "HS1": (16, u16), "HO": (768, f32),
    "CA": (256, u16), "CO": (256, u16), "PL1": (256, h16), "PL2": (256, h16), "EE": (512, f32), "E2": (512, f32),
    "HI2": (32, f32), "HK": (16, f32), "KI": (16, i32), "XH": (256, h16), "AL": (16, u16), "LS": (256, f32),
    "VCS": (256, bf), "VCT": (256, bf), "FB": (512, bf), "JK": (256, bf), "ACC": (6, f32), "PRE": (2, f32),
    "DL": (4, u16), "FL": (264, f32), "FC": (64, f32), "KB": (64, bf), "TR": (64, f32), "LU": (16, u16), "LF": (64, f32), "LO": (16, u16),
    "MK": (96, f32), "AM": (64, f32), "DA": (64, f32), "NA": (64, i32), "DO": (64, f32), "NO": (64, i32),
    "EQ": (192, bf), "CF": (192, f32), "YA": (64, bf), "YB": (64, bf), "VG": (64, bf), "U": (64, bf),
    "IO": (256, bf), "IO8": (64, bf), "IOC": (192, bf), "PI": (8, i32), "CC": (48, f32), "CI": (64, i32), "CL": (144, u16),
    "ONB": (520, bf), "IDB": (128, bf), "NIB": (128, bf), "GB": (16, bf), "GI": (16, bf), "NGI": (16, bf), "GJ": (8, bf),
    "RM": (256, bf), "RN": (1024, bf), "K16": (256, bf), "KL": (64, f32), "TRI": (128, bf), "NTR": (256, bf), "EXP": (512, bf),
    "CK": (256, bf), "CK2": (144, bf), "CND": (32, bf),
    "BO": (128, f32), "SEL": (640, f32), "SELK": (128, bf), "CAB": (320, bf), "KH": (32, f32), "KC": (192, bf), "CM": (96, bf),
}
PS = ["D0", "D1", "D2", "E0", "E1", "LL", "PP", "PF"]
SCRATCH = {k: ("sbuf", [128, w], d) for k, (w, d) in SB.items()}
SCRATCH.update({k: ("psum", [128, 512], f32) for k in PS})
AO = [0, 1536, 2560]
NAO = len(AO) - 1
SEMAPHORES = ["qg", "qv", "qs", "qp", "lh", "lz", "ly", "lv", "so", "sh", "z1", "z2", "t1", "t2", "hl10", "hl11", "hl20", "hl21", "hc10", "hc11", "hc20", "hc21", "sent", "la0", "la1"]
COSTS = [dict(pe=0.44, el=0.85, ga=1.33, sc=3.2, by=0.003, lat=1600, far=2500, first=4000, wake=150),
         dict(pe=0.6, el=1.2, ga=2.2, sc=5.0, by=0.004, lat=2000, far=3000, first=5000, wake=120),
         dict(pe=0.5, el=0.95, ga=1.5, sc=3.6, by=0.0025, lat=1400, far=2500, first=4000, wake=100),
         dict(pe=0.45, el=0.88, ga=1.0, sc=2.3, by=0.003, lat=1500, far=3000, first=3000, wake=140)]
ROUNDS, SEED, DRIFT, FREE, EARLY = 200000, 1, 0.002, 30, 0.2
PLAN = {}


def A(name, lo=0, hi=None, step=1, rows=128, r0=0):
    if hi is None:
        hi = SB[name][0] if name in SB else 512
    return ("ap", name, lo, hi, step, rows, r0)


def IND(win, off):
    return ("ind", win, off)


def col(j):
    return A("CC", j, j + 1)


def meet(a, b, same):
    if a[1] in PS and not same:
        return True
    if a[3] <= b[2] or b[3] <= a[2]:
        return False
    return not (a[4] == b[4] and (a[2] - b[2]) % a[4] != 0)


def width(x):
    return 16 * (x[2][3] - x[2][2]) if x[0] == "ind" else (x[3] - x[2] + x[4] - 1) // x[4]


def size(x):
    return 4 if x[1] in PS or SB[x[1]][1] in (f32, i32) else 2


def schedule(ops):
    if "order" in PLAN:
        return PLAN["order"]
    m = len(ops)
    before, seen, anc, soft = [], {}, [], set()
    for i, (q, wr, rd, cost, lat, emit) in enumerate(ops):
        d = set()
        for aps, w_ in ((wr, True), (rd, False)):
            for x in aps:
                for y, yw, yq, j in seen.get(x[1], []):
                    if q == yq == "p" and (x[6] + x[5] <= y[6] or y[6] + y[5] <= x[6]):
                        continue
                    if (x[1] in PS and (yq != q or q == "p")) or ((w_ or yw) and meet(x, y, yq == q)):
                        d.add(j)
        for aps, w_ in ((wr, True), (rd, False)):
            for x in aps:
                seen.setdefault(x[1], []).append((x, w_, q, i))
        mask, keep = 0, []
        for j in sorted(d, reverse=True):
            if not mask >> j & 1:
                keep.append(j)
                mask |= anc[j] | 1 << j
        if lat or q == "g":
            for j in [j for j in range(i) if ops[j][0] == q and (ops[j][4] or q == "g")][-1:]:
                if j not in keep:
                    keep.append(j)
                    soft.add((j, i))
                    mask |= anc[j] | 1 << j
        anc.append(mask)
        before.append(keep)
    qs = ["gvspy".index(o[0]) for o in ops]
    sets = []
    for c in COSTS:
        busy = [o[3][1] + o[3][2] * c[o[3][0]] for o in ops]
        lat = [o[4] and c["far" if o[0] == "g" else "lat"] + o[4] * c["by"] for o in ops]
        edge = [[(j, 0 if qs[i] == qs[j] == 3 or (j, i) in soft else lat[j] + c["wake"]) for j in before[i]] for i in range(m)]
        sets.append((busy, lat, edge))

    def finish(seq, k, trace=False):
        busy, lat, edge = sets[k]
        free, end, who, why = [0.0] * 5, [0.0] * m, [-1] * 5, [-1] * m
        for i in seq:
            q = qs[i]
            t, y = free[q], who[q]
            for j, e in edge[i]:
                if end[j] + e > t:
                    t, y = end[j] + e, j
            end[i] = free[q] = t + busy[i]
            who[q], why[i] = i, y
        i = m - 1
        if not trace:
            return end[i] + lat[i]
        path = []
        while i >= 0:
            path.append(i)
            i = why[i]
        return path

    seed = [SEED]

    def rnd(k):
        seed[0] = (seed[0] * 1103515245 + 12345) % 2147483648
        return (seed[0] >> 8) % k

    def first_order(k):
        busy, lat, edge = sets[k]
        ahead = [list(e) for e in edge]
        last = {}
        for i in range(m):
            if qs[i] != 3 and qs[i] in last:
                ahead[i].append((last[qs[i]], 0))
            last[qs[i]] = i
        way, after = [busy[i] + lat[i] for i in range(m)], [[] for _ in range(m)]
        for i in reversed(range(m)):
            for j, e in ahead[i]:
                way[j] = max(way[j], busy[j] + e + way[i])
                after[j].append(i)
        free, end, left, out = [0.0] * 5, [0.0] * m, [len(x) for x in ahead], []
        ready = {i: 0.0 for i in range(m) if not left[i]}
        while ready:
            i = min(ready, key=lambda i: max(ready[i], free[qs[i]]) + busy[i] * (qs[i] == 3))
            if qs[i] == 3:
                t0 = max(ready[i], free[3]) + busy[i]
                i = max((x for x in ready if qs[x] == 3 and ready[x] < t0), key=lambda x: way[x])
            end[i] = free[qs[i]] = max(ready.pop(i), free[qs[i]]) + busy[i]
            out.append(i)
            for j in after[i]:
                left[j] -= 1
                if not left[j]:
                    ready[j] = max(end[x] + e for x, e in ahead[j])
        return out

    seq = first_order(0)
    norm = [finish(seq, k) for k in range(len(sets))]
    ends = [[0.0] * m for _ in sets]

    def score(s_, lo):
        head, out, total = {}, [], 0.0
        for i in reversed(s_[:lo]):
            head.setdefault(qs[i], i)
            if len(head) == 5:
                break
        for k, (busy, lat, edge) in enumerate(sets):
            end = ends[k][:]
            free = [end[head[q]] if q in head else 0.0 for q in range(5)]
            for i in s_[lo:]:
                q = qs[i]
                t = free[q]
                for j, e in edge[i]:
                    e += end[j]
                    if e > t:
                        t = e
                end[i] = free[q] = t + busy[i]
            out.append(end)
            total += (end[m - 1] + lat[m - 1] + EARLY * sum(end) / m) / norm[k]
        return total, out

    cur, ends[:] = score(seq, 0)
    paths = [finish(seq, k, True) for k in range(len(sets))]
    for it in range(ROUNDS):
        path = paths[rnd(len(paths))]
        z = rnd(len(path) - 1)
        i, j = path[z], path[z + 1]
        if rnd(100) < FREE:
            a_ = rnd(m - 1)
            near = [x for x in seq[a_ + 1:a_ + 40] if qs[x] == qs[seq[a_]]][:4]
            if not near:
                continue
            j, i = seq[a_], near[rnd(len(near))]
        if qs[i] == 4 or qs[j] == 4 or anc[i] >> j & 1:
            continue
        pi_, pj = seq.index(i), seq.index(j)
        if pi_ < pj:
            continue
        if rnd(2):
            lo = max(0, pj - (rnd(12) if rnd(2) else 0))
            part = seq[lo:pi_]
            new = seq[:lo] + [x for x in part if anc[i] >> x & 1] + [i] + [x for x in part if not anc[i] >> x & 1] + seq[pi_ + 1:]
        else:
            lo, hi = pj, min(m, pi_ + 1 + (rnd(12) if rnd(2) else 0))
            part = seq[pj + 1:hi]
            new = seq[:pj] + [x for x in part if not anc[x] >> j & 1] + [j] + [x for x in part if anc[x] >> j & 1] + seq[hi:]
        sc_, out = score(new, lo)
        if sc_ <= cur + DRIFT * (1 - it / ROUNDS):
            if sc_ != cur:
                k = rnd(len(sets))
                paths[k] = finish(new, k, True)
            seq, cur = new, sc_
            ends[:] = out
    PLAN["order"], PLAN["est"] = seq, [finish(seq, k) for k in range(len(sets))] + norm
    return seq


def rank_program(g, core, T, topo):
    rank = T.rank_of(core)
    if rank is None:
        return
    n = len(T.cores)
    Q = {"g": g, "v": g.vector, "s": g.scalar, "p": g.tensor, "y": g.sync}
    count = {}
    known = {q: {} for q in Q}
    acc = {}
    ops = []

    def mk(x):
        if isinstance(x, tuple) and x[0] == "ap":
            r = slice(x[6], x[6] + x[5])
            return T[x[1]][r, x[2]:x[3]:x[4]] if x[4] > 1 else T[x[1]][r, x[2]:x[3]]
        if isinstance(x, tuple) and x[0] == "ind":
            return mk(x[1]).indirect(mk(x[2]))
        return x

    def need(q, tok):
        sem, val, clock = tok
        if known[q].get(sem, 0) < val:
            Q[q].wait_ge(T.sem[sem], val)
            known[q][sem] = val
            for k, v in clock.items():
                known[q][k] = max(known[q].get(k, 0), v)

    def order(q, wr, rd):
        toks = {}
        for aps, w in ((wr, True), (rd, False)):
            for a in aps:
                for b, bw, bq, tok in acc.get(a[1], []):
                    if q == "p" and bq == "p":
                        continue
                    if (w or bw or (a[1] in PS and bq != q)) and meet(a, b, bq == q):
                        if tok[1] > toks.get(tok[0], (0, 0))[1]:
                            toks[tok[0]] = tok
        for tok in sorted(toks.values(), key=lambda t: -len(t[2])):
            need(q, tok)

    def note(q, wr, rd, tok):
        for aps, w in ((wr, True), (rd, False)):
            for a in aps:
                acc.setdefault(a[1], []).append((a, w, q, tok))

    def token(q, sem, inc):
        count[sem] = count.get(sem, 0) + inc
        return (sem, count[sem], dict(known[q]))

    def parts(xs):
        out = []
        for x in xs:
            if isinstance(x, tuple):
                out += [x] if x[0] == "ap" else [x[1], x[2]]
        return out

    def op(q, rate, call, *a, **kw):
        o = a[0]
        wr = [o] if o[0] == "ap" else [o[1]]
        ins = [x for x in a[1:] if isinstance(x, tuple)]
        rd = ([] if o[0] == "ap" else [o[2]]) + parts(a[1:]) + parts([v for k, v in kw.items() if k != "accum_out"])
        if "accum_out" in kw:
            wr.append(kw["accum_out"])
        if q == "p":
            cost = ("pe", 0, max(min(64, width(a[1])), width(a[2])) * (4 if size(a[1]) == 4 else 1))
        elif o[0] == "ind":
            cost = ("sc", 60, width(o))
        elif any(x[0] == "ind" for x in ins):
            cost = ("ga", 60 if q == "v" else 75, width(o))
        else:
            if rate == 0.5 and any(size(x) == 4 for x in [o] + ins if width(x) > 1):
                rate = 1
            if rate == 2 and any(x[1] in PS for x in ins):
                rate = 1
            cost = ("el", {"v": 0, "s": 30, "g": 180}[q], max(64 * (q != "g"), rate * width(o)))

        def emit():
            order(q, wr, rd)
            call(*[mk(x) for x in a], **{k: mk(v) for k, v in kw.items()}).then_inc(T.sem["q" + q], 1)
            note(q, wr, rd, token(q, "q" + q, 1))
        ops.append((q, wr, rd, cost, 0, emit))

    def together(k):
        run = [ops.pop() for _ in range(k)][::-1]
        cost = (run[0][3][0], sum(o[3][1] for o in run), sum(o[3][2] for o in run))
        ops.append((run[0][0], [x for o in run for x in o[1]], [x for o in run for x in o[2]], cost, 0, lambda: [o[5]() for o in run]))

    ve, sc, pe = g.vector, g.scalar, g.tensor
    cp = lambda o, i: op("v", 0.5, ve.tensor_copy, o, i)
    tt = lambda o, a, b, x: op("v", 2, ve.tensor_tensor, o, a, b, x)
    ts1 = lambda o, a, s1, x: op("v", 0.5, ve.tensor_scalar, o, a, s1, None, x)
    ts2 = lambda o, a, s1, s2, x, y: op("v", 0.5, ve.tensor_scalar, o, a, s1, s2, x, y)
    ms = lambda o, c: op("v", 0.5, ve.memset, o, c)
    scan = lambda o, a, b, i, x, y: op("v", 0.5, ve.tensor_tensor_scan, o, a, b, i, x, y)
    act = lambda o, i, f, **kw: op("s", 1, sc.activation, o, i, f, **kw)
    mm = lambda o, l, r, st=True, sp=True: op("p", 1, pe.matmul, o, l, r, st, sp)
    iota = lambda o, p, b, c: op("g", 2, g.iota, o, p, b, c, **({} if SB[o[1]][1] == i32 else {"allow_small_or_imprecise_dtypes": True}))
    asel = lambda o, i, p, x, f, b, c: op("g", 2, g.affine_select, o, i, p, x, f, b, c)

    def load(q, o, src, sem, after=()):
        def emit():
            order(q, [o], list(after))
            Q[q].dma_start(mk(o), src).then_inc(T.sem[sem], 16)
            note(q, [o], [], token(q, sem, 16))
        ops.append((q, [o], [], ("by", 100, width(o) * size(o) * 128), 1, emit))

    def store(q, dst, i, sem):
        def emit():
            order(q, [], [i])
            Q[q].dma_start(dst, mk(i)).then_inc(T.sem[sem], 16)
            note(q, [], [i], token(q, sem, 16))
        ops.append((q, [], [i], ("el", 100, 0), width(i) * size(i) * i[5], emit))

    def send(hops, o, i, sem, after=()):
        dst = T.cores[(rank + hops * HOP) % n]
        src = T.cores[(rank - hops * HOP) % n]
        rid, pid, _ = topo.addr(dst)

        def emit():
            order("g", [], [i] + list(after))
            g.remote_dma(out_ap=mk(o), in_ap=mk(i), remote_sem=T.sem[sem], local_sem=T.sem.sent, pid=pid, routing_id=rid,
                         dma_engine_mask=topo.mask(core, dst))
            token("g", "sent", len(topo.engines(core, dst)))
            count[sem] = len(topo.engines(src, core))
            note("x", [o], [], (sem, count[sem], {}))
        ops.append(("g", [o], [i] + list(after), ("first", 700, sem == "t1"), width(i) * size(i) * 128, emit))

    WA, WO, Y, V = A("WA"), A("WO"), A("Y"), A("V")
    BC0, PAR = (lambda a, b: A("CL", a, b)), A("CL", 128, 129)
    tl = lambda name, t: A(name, 128 * t, 128 * t + 128)
    LT = lambda b_, t, s_=1, j=0: A(b_, 128 + 128 * t + j, 256 + 128 * t, s_)
    EQL = lambda b_, t, s_=1, j=0: A(b_, 384 * t + j, 384 * t + 128, s_)
    fld = lambda name, t, j: LT(name, t, 16, j)
    ONE = A("ONB", 0, 128)
    SEL = lambda j: A("SEL", 128 * j, 128 * j + 128)

    load("y", A("Z"), T.zc[:, :], "lz")
    load("y", A("HD"), T.hd[:, :], "lh")
    for j in range(NAO):
        load("y", A("WO", AO[j], AO[j + 1]), T.ao[:, AO[j]:AO[j + 1]], "la%d" % j)
    load("y", A("Y", 0, C), T.yd[:, :], "ly")
    load("y", A("V", 0, C), T.ve[:, :], "lv", [A("WO", AO[NAO - 2], AO[NAO - 1])])

    iota(A("PI", 0, 1), [[0, 1]], 0, 1)
    ms(A("ONB"), 1.0)
    asel(A("IDB"), ONE, [[-1, 128]], Op.is_equal, 0.0, 0, 1)
    iota(A("CI"), [[1, 64]], 0, 0)
    iota(A("IO8"), [[0, 8], [1, 8]], 0, 0)
    iota(A("IOC"), [[1, 192]], 0, 0)
    iota(A("IO"), [[0, 16], [1, 16]], 0, 0)
    ms(A("KR"), 1.0)
    ms(A("SP0"), 0.0)
    ms(A("SP1"), 0.0)
    ms(A("KR", 0, 512, 16), 0.0)
    ts1(A("PI", 1, 2), A("PI", 0, 1), 15, Op.bitwise_and)
    ts2(A("PI", 2, 3), A("PI", 0, 1), 4, 1, Op.arith_shift_right, Op.bitwise_and)
    ts1(A("PI", 3, 4), A("PI", 0, 1), 1, Op.bitwise_and)
    ts1(A("PI", 4, 5), A("PI", 0, 1), 4, Op.arith_shift_right)
    ts1(A("PI", 5, 6), A("PI", 0, 1), 31, Op.bitwise_and)
    ts1(col(36), A("PI", 0, 1), float(J2V[0]), Op.is_lt)
    ts1(col(37), A("PI", 0, 1), float(J2V[1] - 128), Op.is_ge)
    cp(A("CC", 0, 5), A("PI", 1, 6))
    cp(A("CL", 0, 64), A("CI"))
    ms(A("WA", C, WD), NONE)
    ms(A("WO", C, WD), 0)
    ms(A("Y", C, WD), 0.0)
    ms(A("V", C, WD), 0.0)
    ts1(A("FT0"), A("ONB"), 0.0, Op.mult)
    ts1(A("GB"), A("IO8", 0, 16), col(3), Op.is_equal)
    act(A("NIB"), A("IDB"), Fn.Copy, scale=-1.0)
    act(A("K16"), A("KR", 0, 256), Fn.Identity, scale=BIG, bias=-BIG)
    act(A("NTR", 128, 256), ONE, Fn.Copy, scale=-1.0)
    act(A("CC", 11, 13), A("CC", 36, 38), Fn.Identity, scale=-5.75 * W2, bias=10.75 * W2)
    act(A("CC", 13, 15), A("CC", 36, 38), Fn.Copy, scale=-16.0 * W2)
    mm(A("PP", 0, 128, 1, 64, 0), A("Z", 128, 192), A("IDB"))
    mm(A("PP", 0, 128, 1, 64, 64), A("Z", 64, 128), A("IDB"))
    act(A("ZT0"), A("PP", 0, 128), Fn.Copy)
    send(1, A("ZT1"), A("ZT0"), "t1")
    act(A("ZR0", 1536, 2560), IND(A("Z", 192, 256), BC0(0, 64)), Fn.Copy)

    def repeat_costs(j):
        sp = "SP%d" % (j % 2)
        cp(A(sp, 0, 512, 16), A("Z", 32 * j, 32 * j + 32))
        scan(A("ZR0", 512 * j, 512 * j + 512), A("KR"), A(sp), 0.0, Op.mult, Op.add)

    repeat_costs(0)
    cp(A("HL0"), A("HD"))
    ts1(A("HDF"), A("HD"), -float(MID), Op.add)
    repeat_costs(1)
    unpack = lambda j: ts1(A("WA", AO[j], AO[j + 1]), A("WO", AO[j], AO[j + 1]), 4095, Op.bitwise_and)
    ts1(A("SP1", 0, 512, 16), A("IOC", 0, 32), col(4), Op.is_equal)
    repeat_costs(2)
    scan(A("EXP"), A("KR"), A("SP1"), 0.0, Op.mult, Op.add)
    unpack(0)
    ts1(A("RM"), A("IO"), col(0), Op.is_equal)
    ts2(A("KL"), A("IO8"), col(3), -BIG, Op.is_equal, Op.mult)
    for x in (0, 384):
        ts1(A("FT1", x, x + 136 - 8 * (x == 0)), A("ONB", 0, 136 - 8 * (x == 0)), 0.0, Op.mult)
    tt(A("XH"), IND(A("HDF"), BC0(0, 16)), A("RM"), Op.mult)
    for t in (0, 1):
        mm(A("PF", 256 + 8 * t, 264 + 8 * t), tl("XH", t), A("GB", 0, 8))
    for j in range(8):
        ts1(tl("RN", j), A("RM", 0, 128), A("GB", j, j + 1), Op.mult)
    act(A("GI"), A("GB"), Fn.Copy, scale=float(W1))
    act(A("NGI"), A("GB"), Fn.Copy, scale=-float(W1))
    act(A("GJ"), A("GB", 0, 8), Fn.Copy, scale=float(W2))
    act(A("CK"), A("IO"), Fn.Identity, scale=-32.0, bias=480.0)
    act(A("CK2"), A("IO", 0, 144), Fn.Identity, scale=-32.0, bias=480.0)
    act(A("CK2", 128, 136), A("ONB", 0, 8), Fn.Copy, scale=0.0)
    act(A("CK2", 136, 144), A("ONB", 0, 8), Fn.Copy, scale=480.0)
    act(A("KL"), A("KL"), Fn.Identity, bias=4096.0)
    act(A("KH"), A("RM", 0, 32), Fn.Identity, scale=-BIG, bias=3072.0)
    for t in (0, 1):
        act(A("CND", 16 * t, 16 * t + 8), A("ONB", 0, 8), Fn.Copy, scale=col(11 + t))
        act(A("CND", 16 * t + 8, 16 * t + 16), A("ONB", 0, 8), Fn.Copy, scale=col(13 + t))
    for j, (x_, a_, b_) in {19: (3, -4096, 7 * 4096 - MID), 5: (0, -1, -0.5), 6: (0, -1, -16.5), 23: (0, 1, C), 15: (0, -1 / 16, 15 / 16),
                            16: (0, 4, 0), 17: (0, 4, 128), 22: (0, 3072, -OFF - 15 * 3072),
                            24: (0, -2, 0.5), 25: (0, -2, -31.5)}.items():
        act(col(j), col(x_), Fn.Identity, scale=float(a_), bias=float(b_))
    act(A("CC", 7, 11), A("IOC", 0, 64, 16), Fn.Identity, bias=col(23))
    act(A("CAB", 129, 192, 2), A("ONB", 0, 32), Fn.Copy, scale=col(22))
    act(A("CC", 20, 22), A("ONB", 0, 2), Fn.Copy, scale=-0.5)
    if NAO > 2:
        unpack(1)
    cp(A("FT0", 128, 384, 16), A("PF", 256, 272))
    ts2(col(18), col(0), 6.0, col(2), Op.is_ge, Op.add)
    ts2(A("FL", 256, 264), A("RM", 3, 131, 16), -float(NONE - MID), float(NONE - MID), Op.mult, Op.add)
    ts2(col(34), col(0), 2.0, col(18), Op.is_ge, Op.add)
    ts2(A("KC", 0, 64), A("IOC", 0, 64), col(16), float(OFF), Op.is_equal, Op.mult)
    ts2(col(35), col(2), 31.0, col(34), Op.mult, Op.add)
    ts2(A("KC", 64, 192), A("IOC", 64, 192), col(17), float(OFF), Op.is_equal, Op.mult)
    ts2(PAR, col(1), 16.0, col(35), Op.mult, Op.add)
    for hs in (0, 1):
        act(A("CM", 32 * hs, 32 + 64 * hs), A("IOC", 0, 32 + 32 * hs), Fn.Sign, bias=col(24 + hs))
    act(A("CM"), A("CM"), Fn.Copy, scale=float(OFF - MID))
    cp(A("SP1", 0, 128, 16), A("GB", 0, 8))
    unpack(NAO - 1)
    scan(A("BO"), A("KR", 0, 128), A("SP1", 0, 128), 0.0, Op.mult, Op.add)
    for x, y, s_, v in ((64, 192, 2, MID - OFF), (65, 128, 2, -OFF), (192, 256, 1, -MID / 128), (256, 320, 1, 0)):
        act(A("CAB", x, y, s_), A("ONB", 0, (y - x + s_ - 1) // s_), Fn.Copy, scale=float(v))

    def late_constants():
        pick = lambda o, i, j, x=Op.is_equal, f=0.0: asel(o, i, [[-16, 8], [0, 16]], x, f, -j, 1)
        asel(A("TRI"), ONE, [[1, 128]], Op.is_ge, 0.0, 0, -1)
        asel(A("NTR", 0, 128), A("NTR", 128, 256), [[1, 128]], Op.is_ge, 0.0, 0, -1)
        iota(SEL(4), [[0, 128]], 4096, 0)
        pick(A("SELK"), ONE, 3)
        pick(SEL(4), SEL(4), 1)
        asel(A("SEL", 0, 384), A("ONB", 0, 384), [[-1, 3], [-16, 8], [0, 16]], Op.is_equal, 0.0, 0, 1)
        pick(SEL(4), SEL(4), 0, Op.not_equal, -4096.0)
        pick(SEL(3), A("NTR", 128, 256), 2)

    cf, ff, ab, ba, lb = A("LU", 0, 4), A("LU", 2, 6), A("LU", 6, 10), A("LU", 8, 12), A("LU", 8, 10)
    MKS = A("MK", 32, 96)
    write_v = lambda: cp(IND(V, A("LO", 0, 4)), A("U"))
    go = lambda line, k=1: [next(line, None) for _ in range(k)]
    bank = [0]

    def s_job(first, table, lst, d0, d1, sign, out, fn, **kw):
        j, w_ = bank[0] % NB, 16 * (d1 - d0)
        bank[0] += 1
        gs, b_ = A("GS", 512 * j, 512 * j + w_), A("D%d" % j, 0, w_)
        act(gs, IND(table, A(lst, d0, d1)), Fn.Copy)
        yield
        mm(b_, *first, True, False)
        mm(b_, A(sign), gs, False, True)
        yield
        act(A(out, 16 * d0, 16 * d1), b_, fn, **kw)

    def head_1(t):
        mm(A("E%d" % t, 0, 256), ONE, A("CK"), True, False)
        mm(A("E%d" % t, 128 * t, 128 * t + 128), tl("PL1", t), A("IDB"), False, False)
        together(2)

    def head_2(t, ft):
        e = "E%d" % t
        mm(A(e, 0, 144), ONE, A("CK2"), True, False)
        mm(A(e, 128, 144), A("IDB"), A("CND", 16 * t, 16 * t + 16), False, False)
        for x in (128, 136):
            mm(A(e, x, x + 8), A("IDB"), fld(ft, t, 0), False, False)
        together(4)
        mm(A(e, 0, 128), tl("PL2", t), A("IDB"), False, False)

    def reduce(a, b, m, gi):
        t, end = a // 128, 256 if m == "M1" else 128
        for x in range(a, b, 32):
            for k in range(16):
                mm(A("E%d" % t, k, end, 16, 32, x - 128 * t), A(m, 16 * x + k, 16 * x + 512, 16), A(gi), False, k == 15)
                if k % 8 == 7:
                    together(8)

    def to_list(src, base, out):
        for x in range(8):
            mm(A("LL", base + 8 * x, base + 8 * x + 8), A("RN", 128 * x, 128 * x + 128), src)
        together(8)
        yield
        scan(A("LS", base, base + 64), A("KL"), A("LL", base, base + 64), 0.0, Op.add, Op.max)
        yield
        ts1(out, A("LS", base + 7, base + 64, 8), col(19), Op.subtract)

    def owners(t, ft):
        scan(A("EE", 256 * t, 256 * t + 256), A("K16"), A("E%d" % t, 0, 256), 0.0, Op.add, Op.max)
        yield
        tt(fld(ft, t, 2), A("EE", 384 * t + 15, 384 * t + 128, 16), A("EE", 128 * t + 143, 128 * t + 256, 16), Op.subtract)
        al = A("AL", 8 * t, 8 * t + 8)
        yield from to_list(fld(ft, t, 2), 64 * t, al)
        yield
        for a, b in ((0, 2), (2, 8)) if t == 0 else ((8, 16),):
            ts2(A("CO", 16 * a, 16 * b), IND(WO, A("AL", a, b)), 1.0 / 4096, -0.3125, Op.mult, Op.add)
        yield
        ts1(tl("PL2", t), tl("CO", t), -float(MID), Op.add)


    def verdict(t, st):
        ft, e, hi = "FT%d" % st, "E%d" % t, A("HI2", 16 * t, 16 * t + 16)
        best, both = LT("E2", t, 16, 15), A("E2", 256 * t + 15, 256 * t + 256, 16)
        scan(LT("E2", t), A("K16", 0, 128), A(e, 0, 128), 0.0, Op.add, Op.max)
        yield
        ts1(LT("SP1", t, 16), best, col(11 + t), Op.is_lt)
        tt(EQL("SP1", t, 16), best, A(e, 136, 144), Op.is_equal)
        tt(EQL("E2", t, 16, 15), best, A(e, 128, 136), Op.max)
        yield
        scan(A("FB", 256 * t, 256 * t + 256), A("KR", 0, 256), A("SP1", 256 * t, 256 * t + 256), 0.0, Op.mult, Op.add)
        if t < HI_S:
            ts2(hi, both, MAG, MAG, Op.add, Op.subtract)
        else:
            act(hi, both, Fn.Identity, bias=MAG)
            act(hi, hi, Fn.Identity, bias=-MAG)
        yield
        tt(A(ft, 256 * t + 1, 256 * t + 256, 16), both, hi, Op.subtract)
        mm(tl("PF", t), LT(ft, t), A("IDB"))
        yield
        if st < S - 1:
            hs_ = A("HS%d" % st, 8 * t, 8 * t + 8)
            yield from to_list(EQL(ft, t, 16, 1), 128 + 64 * t, hs_)
            send(1, A("HL%d" % (st + 1), 8 * t, 8 * t + 8), hs_, "hl%d%d" % (st + 1, t))
            for x in range(2 * t):
                send(1, LT("FT%d" % (st + 1), x), A(ft, 384 * x + 1, 384 * x + 129), "hc%d%d" % (st + 1, x))

    def repeat_g(x):
        y = J2V[1]
        for j in range(16):
            asel(A("VR", 16 * (x - J2V[0]) + j, 16 * (y - J2V[0]), 16), A("VCS", x, y), [[0, y - x]], Op.is_ge, 0.0, 0, 0)
        together(16)

    def repeat_v(x):
        act(A("SP0", 0, 512, 16), A("VCS", x, x + 32), Fn.Copy)
        yield
        scan(A("VR", 16 * (x - J2V[0]), 16 * (x + 32 - J2V[0])), A("KR"), A("SP0"), 0.0, Op.mult, Op.add)

    def least(zr, a, b):
        x = 16 * (a - 96 * (a >= 192))
        tt(A("M1", 16 * a, 16 * b), IND(Y, A("CA", a, b)), A(zr, x, x + 16 * (b - a)), Op.min)

    def compare(a, b):
        tt(A("M2", 16 * a, 16 * b), IND(V, A("CO", a, b)), A("VR", 16 * (a - J2V[0]), 16 * (b - J2V[0])), Op.is_gt)

    def prefix(t):
        o = tl("PP", t)
        mm(o, LT("FB", t), A("TRI", 0, 128), t == 0, False)
        mm(o, EQL("FB", t), A("NTR", 0, 128), False, True)
        together(2)
        yield
        for hs in (0, 1):
            act(A("JK", 128 * hs, 128 * hs + 128), o, Fn.Sign, bias=col(5 + hs), accum_out=A("ACC", 2 * t + hs, 2 * t + hs + 1))

    def same_citizen(hs):
        j, w_ = 64 * hs, 32 + 32 * hs
        for own in (0, 1):
            x = 2 * own + hs
            ts2(A("JK", j + own * w_, j + own * w_ + w_), A("D0", 32 * hs, 32 * hs + w_), A("LF", x, x + 1), float(OFF), Op.is_equal, Op.mult)
        act(A("JK", j, j + 2 * w_), A("JK", j, j + 2 * w_), Fn.Copy, accum_out=A("ACC", 4 + hs, 5 + hs))

    def same_asset(own):
        for hs in (1, 0):
            j, x = 64 * hs, 47 + 16 * hs if own else 6 + hs
            ts2(A("EQ", j + own, j + 64 + 64 * hs, 2), A("D1", 0, 32 + 32 * hs), A("LF", x, x + 1), float(OFF), Op.is_equal, Op.mult)

    for st in range(S):
        hl, ft, zr, later, last = "HL%d" % st, "FT%d" % st, "ZR%d" % st, st > 0, st == S - 1
        ya, yb, yc = [s_job((A("ZT%d" % st, 0, 128, 1, 32, x % 128), A("EXP", 0, 512, 1, 32, x % 128)), Y, "CA", x, x + 32, "NIB", "M1", Fn.Relu)
                      for x in (96, 128, 160)]
        held = lambda x, y: (A("VCT", x // 128 * 128, x // 128 * 128 + 128, 1, 32, x % 128 // 32 * 32),
                             A("EXP", 16 * (x % 32), 16 * (x % 32 + y - x), 1, 32, x % 128 // 32 * 32))
        va, vb, vc, vd, vf = [s_job(held(x, y), V, "CO", x, y, "IDB", "M2", Fn.Sign, bias=-0.5)
                              for x, y in ((0, 32), (32, 64), (64, 96), (224, 256), (J2V[1], 224))]
        own0, own1, ver0, ver1, pre0, pre1 = owners(0, ft), owners(1, ft), verdict(0, st), verdict(1, st), prefix(0), prefix(1)
        cp(tl("CA", 0), IND(WA, A(hl, 0, 8)))
        go(ya, 2)
        if later:
            write_v()
        cp(tl("CA", 1), IND(WA, A(hl, 8, 16)))
        least(zr, 0, 32)
        if not later:
            send(1, A("ZR1"), A("ZR0"), "z1", after=[V])
        act(tl("VCS", 1), IND(V, A(hl, 8, 16)), Fn.Copy)
        repeat_g(REP_G[st])
        if not later:
            late_constants()
        go(yb, 2)
        for t in (0, 1):
            ts1(tl("PL1", t), tl("CA", t), -float(MID), Op.add)
        head_1(0)
        least(zr, 32, 64)
        go(ya)
        reduce(96, 128, "M1", "NGI")
        reduce(0, 64, "M1", "GI")
        act(tl("VCS", 0), IND(V, A(hl, 0, 8)), Fn.Copy)
        least(zr, 64, 96)
        reduce(64, 96, "M1", "GI")
        go(yc, 2)
        for t in (0, 1):
            mm(tl("PF", t), tl("VCS", t), A("NIB"))
        together(2)
        head_1(1)
        least(zr, 192, 208)
        go(yb)
        go(own0)
        if later:
            tt(A("NO"), IND(WO, ab), A("DO"), Op.add)
        act(A("VCT"), A("PF", 0, 256), Fn.Copy)
        go(own0)
        if later:
            cp(IND(WO, A("LO", 6, 10)), A("NO"))
        go(yc)
        rep = repeat_v(J2V[0])
        go(rep)
        go(own0, 3)
        reduce(128, 192, "M1", "NGI")
        go(va)
        least(zr, 208, 224)
        go(own0)
        reduce(192, 224, "M1", "GI")
        go(va)
        least(zr, 224, 256)
        go(vb)
        reduce(224, 256, "M1", "GI")
        go(vb)
        head_2(0, ft)
        go(rep)
        for x in range(128, REP_G[st], 32):
            go(repeat_v(x), 2)
        go(va)
        go(own1, 2)
        go(vc, 2)
        compare(96, 112)
        go(own1, 2)
        go(vb)
        reduce(0, 64, "M2", "GJ")
        go(own1)
        compare(112, 128)
        reduce(96, 128, "M2", "GJ")
        go(vc)
        act(A("HK"), A("EE", 143, 384, 16), Fn.Copy, scale=1.0 / W1)
        go(own1)
        reduce(64, 96, "M2", "GJ")
        go(vd, 2)
        head_2(1, ft)
        compare(128, 160)
        ts1(A("KI"), A("HK"), -0.47, Op.add)
        go(vf, 2)
        go(ver0)
        tt(A(ft, 131, 384, 16), A("HK"), A("KI"), Op.subtract)
        go(ver0)
        go(vd)
        compare(160, 192)
        reduce(224, 256, "M2", "GJ")
        go(ver0)
        go(pre0)
        reduce(128, 192, "M2", "GJ")
        go(vf)
        go(ver0)
        compare(192, J2V[1])
        reduce(192, 224, "M2", "GJ")
        go(pre0)
        act(A("FL", 0, 128), tl("PF", 0), Fn.Copy)
        act(A("PRE"), A("ACC", 0, 2), Fn.Identity, scale=-0.5, bias=128.0)
        go(ver0)
        mm(tl("PP", 1), LT("FB", 0), ONE, True, False)
        mm(tl("PP", 1), EQL("FB", 0), A("NTR", 128, 256), False, False)
        together(2)
        go(ver1)
        go(ver0)
        go(ver1)
        go(ver0)
        go(ver1)
        go(pre1)
        go(ver1)
        go(pre1)
        act(A("FL", 128, 256), tl("PF", 1), Fn.Copy)
        go(ver1)
        mm(A("D0", 0, 96), A("IDB"), A("CM"), True, False)
        mm(A("D1", 0, 128), A("IDB"), A("CAB", 64, 192), True, False)
        if not last:
            mm(A("E1", 0, 128), ONE, A("CAB", 192, 320), True, False)
        go(ver1)
        for hs in (0, 1):
            ts2(A("DL", 2 * hs, 2 * hs + 2), A("CC", 20, 22), A("ACC", 2 + hs, 3 + hs), A("PRE", hs, hs + 1), Op.mult, Op.add)
        go(ver1)
        cp(A("FC"), IND(A("FL"), A("DL")))
        act(A("KB"), IND(A("FL"), A("DL")), Fn.Copy)
        if st == 0:
            send(2, A("ZT2"), A("ZT0"), "t2")
            send(2, A("ZR2"), A("ZR0"), "z2")
        FH = A("FC", 16, 48)
        mm(A("D0", 0, 96, 2), SEL(0), A("FC", 0, 48), False, False)
        for j in (0, 1):
            mm(A("E0", 32 * j, 32 * j + 32), A("SELK"), A("KB", 16, 48))
        together(2)
        op("v", 1, ve.transpose, A("TR"), A("FC"))
        mm(A("D0", 1, 96, 2), SEL(1), A("FC", 0, 48), False, True)
        mm(A("D1", 0, 64, 2), SEL(2), FH, False, False)
        ts1(A("LU"), IND(A("TR"), PAR), float(MID), Op.add)
        act(A("LF", 0, 16), IND(A("TR"), PAR), Fn.Identity, bias=float(MID - OFF))
        ts1(A("MK", 0, 64), A("E0", 0, 64), col(15), Op.is_equal)
        tt(A("AM"), IND(WA, ff), A("MK", 0, 64), Op.mult)
        mm(A("D1", 1, 128, 2), A("BO"), A("AM"), False, True)
        if not last:
            act(A("MK", 64, 96), A("MK", 0, 32), Fn.Copy, scale=-1.0)
        same_citizen(1)
        same_citizen(0)
        act(A("VG"), IND(V, cf), Fn.Copy)
        if not last:
            for j in (0, 1):
                mm(A("E1", 32 * j, 32 * j + 32), SEL(3), FH, False, False)
                mm(A("E1", 64 + 32 * j, 96 + 32 * j), SEL(4), FH, False, False)
            mm(A("E1", 0, 64), A("BO"), A("AM"), False, True)
        scan(A("LF", 32, 64), A("KH"), A("D1", 65, 128, 2), 0.0, Op.add, Op.max)
        same_asset(0)
        same_asset(1)
        ts1(lb, A("LF", 47, 64, 16), float(OFF), Op.add)
        act(A("YA"), IND(Y, ab), Fn.Copy)
        act(A("YB"), IND(Y, ba), Fn.Copy)
        for j, (l_, r_) in enumerate((("IDB", "VG"), ("NIB", "YA"), ("IDB", "YB"))):
            mm(A("PP", 0, 64), A(l_), A(r_), j == 0, j == 2)
        together(3)
        act(A("U"), A("PP", 0, 64), Fn.Copy)
        if not last:
            tt(A("DA"), A("E1", 0, 64), MKS, Op.mult)
        for hs in (1, 0):
            a_, b_ = 64 * hs, 64 + 128 * hs
            scan(A("CF", a_, b_), A("KC", a_, b_), A("EQ", a_, b_), A("ACC", 4 + hs, 5 + hs), Op.add, Op.max)
        if not last:
            tt(A("NA"), IND(WA, cf), A("DA"), Op.add)
        for hs in (1, 0):
            for ty in (0, 1):
                x, y = 2 * ty + hs, 63 + 128 * hs
                z = 47 + 16 * hs if ty else x + 6
                ts2(A("LO", x, x + 7, 6), A("LF", x, z + 1, z - x), A("CF", y, y + 1), col(7 + x), Op.add, Op.min)
        for t in (0, 1):
            mm(A("PF", 256 + 128 * t, 384 + 128 * t, 1, 8), EQL(ft, t, 16, 1), A("IDB"))
        together(2)
        act(A("HO", 256 * st, 256 * st + 256, 1, 8), A("PF", 256, 512, 1, 8), Fn.Identity, bias=float(MID))
        if not last:
            cp(IND(WA, A("LO", 0, 4)), A("NA"))
            tt(A("DO"), A("E1", 64, 128), MKS, Op.mult)
        else:
            store("y", T.ho[:, :], A("HO", 0, 768, 1, 8), "sh")
            write_v()
            store("y", T.vo[:, :], A("V", 0, C), "so")
    for i in schedule(ops):
        ops[i][5]()
    for sem, val in count.items():
        if known["g"].get(sem, 0) < val or sem == "qg":
            g.wait_ge(T.sem[sem], val)
